import numpy as np, ml_dtypes
CORES = [24,25,26,27,28,29,30,31]
N = 8
BF = ml_dtypes.bfloat16
V, VB, S, L, LB, B, RO = 4096, 12, 1536, 240, 80, 3, 3
def picks(lm, s, j):
    g = np.arange(8)[:, None, None]; k = np.arange(16)[None, :, None]
    a = lm[g, k, s[:, None, :]] >> VB
    return lm[g, (j[:, None, :] + k) & 15, a] & (V - 1)
def sample(f, lm, x, p, q, s, t):
    g = np.arange(8)[:, None, None, None]; i = np.arange(16)[None, :, None, None]; k = np.arange(16)[None, :, None]
    j = (np.sum(x, axis=1) + t) & 15
    m = picks(lm, s, j)
    void = np.any(m[:, :, None, :] == q[:, None, :, :], axis=2)
    n = np.where((p >= 0) & (((j[:, None, :] + k) & 1) == 1), p, np.where(void, -1, m))
    fz = f[g, i, np.maximum(n, 0)[:, None, :, :]]
    dist = np.where(n < 0, 1 << 20, np.sum(np.abs(fz - x[:, :, None, :]), axis=1))
    return j, n, dist, np.argmin(dist, axis=1)
def names(rng, pop, share, n):
    i = rng.integers(0, 64, (N, 8, 16, n)); g = np.arange(8).reshape(1, 8, 1, 1)
    return np.where(rng.random(i.shape) < share, pop[g, i], rng.integers(0, V, i.shape))
def parts(rng, share=0.5, fp=0.5, fq=0.6):
    pop = rng.integers(0, V, (8, 64)); d = {}
    d["f"] = rng.integers(0, 256, (N, 8, 16, V)); d["lm"] = rng.integers(0, S, (N, 8, 16, S)) * V + names(rng, pop, share, S)
    d["sn"] = rng.integers(0, S, (N, 8, V)); d["th"] = rng.integers(500, 1200, (N, 8, L)); d["x"] = rng.integers(0, 256, (N, 8, 16, L))
    d["p"] = np.where(rng.random((N, 8, 16, L)) < fp, names(rng, pop, share, L), -1)
    d["q"] = np.where(rng.random((N, 8, 16, L)) < fq, names(rng, pop, share, L), -1)
    d["s"] = rng.integers(0, S, (N, 8, L)); d["v"] = rng.integers(0, V, (N, 8, L))
    return d
def pack(d):
    o = {"feat": d["f"].reshape(N, 128, V).astype(np.float32).astype(BF), "lm": d["lm"].reshape(N, 128, S).astype(np.int32), "sn": d["sn"].astype(np.int32), "th": d["th"].astype(np.int32),
         "lx": d["x"].reshape(N, 128, L).astype(np.float32).astype(BF), "lp": d["p"].reshape(N, 128, L).astype(np.int32), "lq": d["q"].reshape(N, 128, L).astype(np.int32),
         "ls": d["s"].astype(np.int32), "lv": d["v"].astype(np.int32)}
    return {k: np.ascontiguousarray(a) for k, a in o.items()}
def setup_inputs(rng):
    return pack(parts(rng))
def setup_inputs_spread(rng):
    d = parts(rng, share=rng.choice(np.array([0.0, 0.3, 0.7, 0.95]), (N, 8, 1, 1)), fp=rng.random((N, 8, 1, L)), fq=rng.random((N, 8, 1, L)))
    d["f"] = np.minimum((np.exp2(8 * rng.random((N, 8, 1, V))) * rng.random((N, 8, 16, V))).astype(np.int64), 255)
    d["x"] = np.minimum((np.exp2(8 * rng.random((N, 8, 1, L))) * rng.random((N, 8, 16, L))).astype(np.int64), 255)
    d["th"] = np.minimum(np.exp2(12 * rng.random((N, 8, L))).astype(np.int64), 4095)
    d["lm"] = np.minimum((S * rng.random((N, 8, 16, S)) ** 4).astype(np.int64), S - 1) * V + (d["lm"] & (V - 1))
    d["sn"] = np.minimum((S * rng.random((N, 8, V)) ** 3).astype(np.int64), S - 1)
    d["s"] = np.minimum((S * rng.random((N, 8, L)) ** 2).astype(np.int64), S - 1)
    return pack(d)
def twoends(rng, lo, hi, *shape):
    share = np.array([1.0, 0.7, 1.0, 0.7, 0.9, 0.7, 0.8, 1.0]).reshape((1, 8) + (1,) * (len(shape) - 2))
    return np.where(rng.random(shape) < share, np.where(rng.random(shape) < 0.5, lo, hi), rng.integers(lo, hi + 1, shape))
def byrecord(rng, lo, hi, n):
    c = rng.integers(0, 4, (N, 8, 1, n))
    return np.where(c == 0, lo, np.where(c == 1, hi, twoends(rng, lo, hi, N, 8, 16, n)))
def setup_inputs_ends(rng):
    d = {"f": byrecord(rng, 0, 255, V), "x": byrecord(rng, 0, 255, L), "p": byrecord(rng, -1, V - 1, L), "q": byrecord(rng, -1, V - 1, L), "lm": twoends(rng, 0, S * V - 1, N, 8, 16, S),
         "sn": twoends(rng, 0, S - 1, N, 8, V), "th": twoends(rng, 0, 4095, N, 8, L), "s": twoends(rng, 0, S - 1, N, 8, L), "v": twoends(rng, 0, V - 1, N, 8, L)}
    r = N - 1
    d["f"][r, 7, :, 0] = 255; d["f"][r, 7, :, V - 1] = 255; d["x"][r, 7, :, 0::2] = 255; d["x"][r, 7, :, 1::2] = 0
    d["th"][r, 7, 1::4] = 4095; d["th"][r, 7, L - 1] = 4095; d["sn"][r, 7, 0] = 0; d["sn"][r, 7, V - 1] = S - 1
    d["s"][r, 7, L - 1] = 0; d["p"][r, 7, :, L - 1] = -1; d["q"][r, 7, :, L - 1] = -1
    d["lm"][r, 7, 0, 0] = S * V - 1; d["lm"][r, 7, 0, S - 1] = S * V - 1; d["lm"][r, 7, 15, 0] = 0
    d["sn"][0, 6:] = S - 1; d["s"][0, 6:] = 0; d["th"][0, 6:] = 4095; d["q"][0, 6:] = -1; d["s"][0, 6, L - 1] = S - 1
    return pack(d)
def setup_inputs_corners(rng):
    d = parts(rng)
    u = rng.random((N, 8, 16, S)); w = rng.random((N, 8, 16, S)); c = np.arange(S)
    link = np.where(u < 0.2, c, np.where(u < 0.3, 0, np.where(u < 0.4, S - 1, d["lm"] >> VB)))
    d["lm"] = link * V + np.where(w < 0.05, 0, np.where(w < 0.1, V - 1, d["lm"] & (V - 1)))
    u = rng.random((N, 8, L)); d["s"] = np.where(u < 0.05, 0, np.where(u < 0.1, S - 1, d["s"]))
    u = rng.random((N, 8, L)); d["v"] = np.where(u < 0.05, 0, np.where(u < 0.1, V - 1, d["v"]))
    k = np.arange(16)[None, :, None]
    for r in range(N):
        m = picks(d["lm"][r], d["s"][r], np.sum(d["x"][r], axis=1) & 15)
        kind = rng.integers(0, 7, (8, 1, L)); kind[:, 0, :7] = np.arange(7); kind[:, 0, L - 7:] = np.arange(7)[::-1]
        o = rng.integers(0, 16, (8, 1, L)); keep = np.take_along_axis(m, o, 1); full = rng.integers(0, V, (8, 16, L))
        p, q = d["p"][r], d["q"][r]
        p = np.where((kind == 0) | (kind == 1) | (kind == 3), -1, np.where(kind == 2, full, np.where(kind == 4, np.where(k == o, full, -1), np.where(kind == 5, m[:, ::-1], p))))
        q = np.where((kind == 0) | (kind == 2), m, np.where(kind == 1, np.where(m == keep, -1, m), np.where(kind == 3, -1, np.where((kind == 4) | (kind == 5), full[::-1], q))))
        d["p"][r] = p; d["q"][r] = q
        j, n, dist, best = sample(d["f"][r], d["lm"][r], d["x"][r], p, q, d["s"][r], 0)
        nb = np.take_along_axis(n, best[:, None, :], 1)[:, 0]; db = np.take_along_axis(dist, best[:, None, :], 1)[:, 0]
        e = rng.integers(0, 6, (8, L))
        d["th"][r] = np.minimum(np.where(e == 0, db, np.where(e == 1, db + 1, np.where(e == 2, 0, np.where(e == 3, 4095, d["th"][r])))), 4095)
        gi, li = np.nonzero((nb >= 0) & (rng.random((8, L)) < 0.1))
        d["sn"][r][gi, nb[gi, li]] = d["s"][r][gi, li]
    d["lm"][:, 5] = (d["lm"][:, 5] >> VB) * V + 7; d["v"][:, 5] = 7; d["p"][:, 5] = -1; d["th"][:, 5] = 4095
    d["q"][:, 5] = 7; d["q"][:, 5, :, :31] = -1; d["sn"][:, 5, 7] = 10 + np.arange(N); d["s"][:, 5, :31] = 100
    return pack(d)
def setup_inputs_crowd(rng):
    d = parts(rng)
    d["f"][:, 1::2] = np.tile(rng.integers(0, 256, (N, 8, 16, 16)), V >> 4)[:, 1::2]
    d["sn"][:, 1::2] = np.take_along_axis(rng.integers(0, S, (N, 8, 2)), rng.integers(0, 2, (N, 8, V)), 2)[:, 1::2]
    c = np.stack([rng.permutation(S)[:N] for g in range(8)], axis=1); c[:, 6] = c[0, 6]
    a = (100 + np.arange(N) % 3)[:, None, None]
    for g in (0, 2, 4, 6):
        d["sn"][:, g] = c[:, g, None]; d["s"][:, g] = (c[:, g, None] + 1 + rng.integers(0, S - 1, (N, L))) % S
        d["q"][:, g] = -1; d["th"][:, g] = 4095
        if g < 4: d["f"][:, g] = a; d["x"][:, g] = a; d["th"][:, g] = 1
        if g == 2 or g == 4:
            pos = rng.integers(0, L, N); pos[N - 1] = L - 1; d["s"][np.arange(N), g, pos] = c[:, g]
    return pack(d)
def setup_inputs_turns(rng):
    d = parts(rng)
    base = rng.integers(0, 100, (8, 16)); base[:, 0] ^= 1 - (np.sum(base, axis=1) & 1)
    lev = np.stack([6 * rng.permutation(N) for g in range(8)], axis=1) + rng.integers(0, 14, 8) + 100 * (np.arange(N) & 1)[:, None]
    d["f"][:] = (base + lev[:, :, None])[..., None]; d["x"][:] = (base + lev[:, :, None])[..., None]
    c = rng.choice(np.array([0, 1, 31, L - 1, L]), (N, 8)); c[0] = L; c[N - 1] = L - 1
    for r in range(N):
        for g in range(8):
            z = rng.permutation(V)[:L]; u = rng.permutation(S)[:L]; go = rng.permutation(L) < c[r, g]
            d["sn"][r, g, z] = u; d["p"][r, g, 0] = z
            d["s"][r, g] = np.where(go, (u + 1 + rng.integers(0, S - 1, L)) % S, u)
    h = 1 + np.arange(L) // LB; rr = np.arange(N)[:, None]; here = lev[:, :, None]
    one = lev[(rr - h) % N].transpose(0, 2, 1); two = lev[(rr - 2 * h) % N].transpose(0, 2, 1)
    d1 = 16 * np.abs(here - one); d2 = 16 * np.abs(here - ((one + two) >> 1)); e = rng.integers(0, 2, (N, 8, L))
    d["th"] = d1 - (c[:, :, None] & 31) + e
    calm = np.where((d2 > 0) & (d2 + 32 <= d1), d2 + e, 1)
    for g in (1, 6): d["th"][:, g] = calm[:, g]
    return pack(d)
def check_inputs(d):
    bad = []
    for k, lo, hi in (("feat", 0, 255), ("lm", 0, S * V - 1), ("sn", 0, S - 1), ("th", 0, 4095), ("lx", 0, 255), ("lp", -1, V - 1), ("lq", -1, V - 1), ("ls", 0, S - 1), ("lv", 0, V - 1)):
        a = np.asarray(d[k]).astype(np.float64)
        if not np.all((a >= lo) & (a <= hi) & (np.floor(a) == a)): bad.append("range of " + k)
    return bad
def reference(feat, lm, sn, th, lx, lp, lq, ls, lv):
    f = feat.astype(np.float32).astype(np.int64).reshape(N, 8, 16, V); rec = lm.astype(np.int64).reshape(N, 8, 16, S)
    sup = sn.astype(np.int64); thr = th.astype(np.int64)
    x = lx.astype(np.float32).astype(np.int64).reshape(N, 8, 16, L); p = lp.astype(np.int64).reshape(N, 8, 16, L); q = lq.astype(np.int64).reshape(N, 8, 16, L)
    s = ls.astype(np.int64); v = lv.astype(np.int64); moved = np.zeros((N, 8), np.int64)
    g2 = np.arange(8)[:, None]; g3 = np.arange(8)[:, None, None]; i3 = np.arange(16)[None, :, None]
    for t in range(RO):
        for r in range(N):
            j, n, dist, best = sample(f[r], rec[r], x[r], p[r], q[r], s[r], t)
            nb = np.take_along_axis(n, best[:, None, :], 1)[:, 0]; db = np.take_along_axis(dist, best[:, None, :], 1)[:, 0]
            live = nb >= 0; z = np.maximum(nb, 0); s2 = sup[r][g2, z]
            go = live & (db < thr[r] + (moved[r][:, None] & 31)) & (s2 != s[r])
            m2 = picks(rec[r], s2, j)
            eq = n[:, :, None, :] == m2[:, None, :, :]
            p[r] = np.where(go[:, None, :], np.where(np.any(eq, axis=2), -1, n), p[r])
            q[r] = np.where(go[:, None, :], np.where(np.any(eq, axis=1), -1, m2), q[r])
            for g in range(8):
                w = np.flatnonzero(go[g]); u, first = np.unique(s2[g, w], return_index=True); w = w[first]
                rec[r, g, j[g, w], u] = s[r, g, w] * V + v[r, g, w]
            x[r] = np.where(live[:, None, :], (x[r] + f[r][g3, i3, z[:, None, :]]) >> 1, x[r])
            s[r] = np.where(go, s2, s[r]); moved[r] = np.sum(go, axis=1)
        if t < RO - 1:
            for b in range(B):
                lo, hi = b * LB, (b + 1) * LB
                for a in (x, p, q, s, v): a[..., lo:hi] = np.roll(a[..., lo:hi], 1 + b, axis=0)
    return {"ylm": rec.reshape(N, 128, S).astype(np.float32), "yx": x.reshape(N, 128, L).astype(np.float32), "yp": p.reshape(N, 128, L).astype(np.float32),
            "yq": q.reshape(N, 128, L).astype(np.float32), "ys": s.astype(np.float32)}

@@ -1,0 +1,861 @@
+import math
+import numpy as np
+from concourse.bass import DstId, RemoteDMATransfer
+from concourse.mybir import AluOpType as A, AxisListType as AX, ActivationFunctionType as F
+
+V, S, L, NH, LB, RO = 4096, 1536, 240, 15, 80, 3
+CH = [(0, 6), (6, 10), (10, 15)]
+MS = [(0, 128), (128, 240)]
+E3, E7 = "AAV", "AAA"
+E4 = "AAVAAAAA"
+SEED, ROUNDS, SLACK, STAGGER = 6, 3500, 130.0, -2000.0
+KB = "V"
+PIECE = 32
+XB = 4112
+WIN = XB + RO * L
+CEN = 2047.0
+MAGIC = 12582912.0
+BIGV = 262144.0
+UP = 0.48
+SIGC, SIGB = 128.0, -math.log(31.0)
+
+SCRATCH = {}
+BUF = {}
+POOL = {}
+DUP = ("ju", "eb", "pen", "mask", "n16", "vf", "nogo", "pk", "h", "kmin", "s2u", "bc", "bm", "au")
+
+
+def _sb(name, cols, dt, parts=128):
+    names = [name + "~0", name + "~1"] if name in DUP else [name]
+    pool = "small_" + dt if cols <= 16 else name
+    for nm in names:
+        BUF[nm] = ("sbuf", [parts, cols], dt)
+        at = SCRATCH[pool][1][1] if pool in SCRATCH else 0
+        SCRATCH[pool] = ("sbuf", [parts, at + max(cols, 16)], dt)
+        POOL[nm] = (pool, at)
+
+
+for _n, _c, _d in [
+    ("fw", WIN, "bfloat16"), ("snb", WIN, "int32"), ("lmi", S, "int32"), ("memi", S, "int32"),
+    ("comb", S + L, "float32"), ("mem", S + L, "float32"), ("pqi", 2 * L, "int32"),
+    ("ones", 256, "bfloat16"), ("c128", 256, "bfloat16"), ("c2048", L, "bfloat16"), ("c05", L, "bfloat16"),
+    ("mI", 128, "bfloat16"), ("mN", 128, "bfloat16"), ("mBIG", 128, "bfloat16"), ("mPB", 128, "bfloat16"),
+    ("mO1", 128, "bfloat16"), ("mO", 128, "bfloat16"), ("mZ", 144, "bfloat16"), ("mZ2", 144, "bfloat16"), ("mY", 208, "bfloat16"),
+    ("mYP", 208, "bfloat16"), ("mY8", 208, "bfloat16"), ("mD0", 256, "bfloat16"), ("mD", 2048, "bfloat16"), ("mR", 17 * 64, "bfloat16"),
+    ("mJ", 128, "bfloat16"), ("mH", 1024, "bfloat16"), ("hm", 16, "float32"), ("sc", 16, "float32"), ("par", 16, "float32"), ("ob", L, "bfloat16"),
+    ("um0", 2 * L, "float16"), ("um1", 2 * L, "float16"), ("um2", 2 * L, "float16"), ("mB", 2048, "bfloat16"), ("mB4", 2048, "bfloat16"), ("mT", 2048, "bfloat16"),
+    ("io1", 16, "int32"), ("ei", 16, "int32"), ("oi", 16, "int32"), ("etab", 16, "bfloat16"), ("otab", 16, "bfloat16"),
+    ("ef", 16, "float32"), ("rm", 16, "float32"), ("mO4", 128, "bfloat16"), ("hi", 16, "int32"), ("hoff", 16, "uint16"), ("rmb", 128, "bfloat16"), ("kx", L, "bfloat16"), ("ne", 16, "float32"),
+    ("h16", 16, "float32"), ("lw", 16, "float32"), ("dum", 16, "float32"), ("dums", 16, "float32"), ("lc", 48, "float32"),
+    ("kc", L, "bfloat16"), ("thw", 16, "float32"), ("thx", 16, "float32"), ("thr", 16, "float32"),
+    ("ji", 16, "int32"), ("ji2", 16, "int32"), ("ju", 16, "uint16"), ("su", 16, "uint16"),
+    ("eb", L, "bfloat16"), ("pen", L, "bfloat16"), ("mask", 16 * L, "bfloat16"), ("au", L, "uint16"), ("a2u", L, "uint16"),
+    ("pu", L, "float16"), ("rr", 2 * L, "bfloat16"), ("n16", 2 * L, "float16"), ("nu", L, "uint16"),
+    ("vf", L, "bfloat16"), ("kmin", 16, "int32"), ("ki2", 16, "int32"), ("kb", 16, "bfloat16"),
+    ("seln", L, "float16"), ("xo", 16, "float32"), ("xu", 16, "uint16"), ("s2b", L, "float16"),
+    ("s2u", 16, "uint16"), ("fs", L, "bfloat16"), ("xy", L, "float32"), ("xn", 2 * L, "bfloat16"),
+    ("s2w", 16, "float32"), ("c1", 16, "float32"), ("df", 16, "float32"), ("d2", 16, "float32"), ("gw", 16, "bfloat16"),
+    ("sn1", 16, "float16"), ("sn2", 16, "float16"), ("sn3", 16, "float16"),
+    ("k0", 16, "float32"), ("k1", 16, "float32"), ("k32", 16, "float32"), ("k16", 16, "float16"), ("kbb", L, "float16"),
+    ("eq", NH * L, "bfloat16"), ("lb", L, "bfloat16"), ("of", 16, "float32"), ("ou", 16, "uint16"),
+    ("nogo", L, "bfloat16"), ("cnt", 4, "float32"), ("a1", 4, "float32"), ("a2", 4, "float32"), ("a3", 4, "float32"), ("a4", 4, "float32"),
+    ("oc", L, "float32"), ("om", L, "float32"), ("bc", L, "float32"), ("bm", L, "float32"),
+    ("r2", 4 * L, "bfloat16"), ("pk", 2 * L, "float16"),
+    ("pm0", 2 * L, "float16"), ("pm1", 2 * L, "float16"), ("pm2", 2 * L, "float16"),
+    ("po0", 2 * L, "float16"), ("po1", 2 * L, "float16"), ("pf", 2 * L, "float32"), ("pf2", 2 * L, "float32"),
+    ("s0", 16, "float16"), ("s1", 16, "float16"), ("s2", 16, "float16"),
+    ("v0", L, "float16"), ("v1", L, "float16"), ("v2", L, "float16"),
+    ("xf", L, "float32"), ("sf", L, "float32"),
+    ("g", 16 * L, "float16"), ("h", 16 * L, "float16"), ("sg", 16 * L, "bfloat16"), ("f", 16 * L, "bfloat16"),
+    ("ab", 16 * L, "bfloat16"), ("sh", 16 * L, "bfloat16"),
+]:
+    _sb(_n, _c, _d)
+_sb("rwi", L, "int32", 24)
+_sb("rw", L, "float16", 24)
+_sb("z24", 2 * 144 + 128, "bfloat16", 24)
+for _i in range(8):
+    SCRATCH["bank%d" % _i] = ("psum", [128, 512], "float32")
+
+NDMA = 20
+SEMAPHORES = (["eV", "eA", "eP", "eG", "sent", "snl"] + ["d%d" % _i for _i in range(NDMA)]
+              + ["%s%d_%d" % (_a, _t, _b) for _a in ("ax", "ap") for _t in (1, 2) for _b in range(3)]
+              + ["as1", "as2", "av1", "av2"])
+SIZE = {"float32": 4, "int32": 4, "bfloat16": 2, "float16": 2, "uint16": 2}
+CYC, PEC, HOP, GAT, SCT = 1.04, 0.52, 120.0, 1.56, 3.8
+PAR, TAG = [0], ["init"]
+BIAS = {}
+
+
+def R(name, lo=0, hi=None, step=1, p0=0, p1=None, pstep=1):
+    if name in DUP:
+        name = "%s~%d" % (name, PAR[0])
+    shp = [128, 512] if name[:2] == "ps" else BUF[name][1]
+    return (name, lo, shp[1] if hi is None else hi, step, p0, shp[0] if p1 is None else p1, pstep)
+
+
+def cnt(r):
+    return (r[2] - r[1] + r[3] - 1) // r[3]
+
+
+def two(*rs):
+    return all(r[0][:2] != "ps" and SIZE[BUF[r[0]][2]] == 2 for r in rs)
+
+
+def plan():
+    ops = []
+    PAR[0], TAG[0] = 0, "init"
+
+    def add(eng, kind, args, reads, writes, cost, lat=0.0, after=None):
+        ops.append({"eng": eng, "kind": kind, "args": args, "r": reads, "w": writes, "cost": cost, "lat": lat, "after": after, "id": len(ops),
+                    "tag": TAG[0]})
+        return ops[-1]
+
+    def aps(*xs):
+        return [x for x in xs if isinstance(x, tuple)]
+
+    def vc(n):
+        return max(64.0, n) * CYC
+
+    def copy(out, in_):
+        add("V", "copy", (out, in_), [in_], [out], vc(cnt(out) * (0.5 if two(out, in_) else 1)))
+
+    def ts(out, in0, s1, op0, s2=None, op1=None):
+        add("V", "ts", (out, in0, s1, s2, op0, op1), aps(in0, s1, s2), [out], vc(cnt(out) * (0.5 if two(out, in0) else 1)))
+
+    def tt(out, in0, in1, op):
+        ps = in0[0][:2] == "ps" or in1[0][:2] == "ps"
+        add("V", "tt", (out, in0, in1, op), [in0, in1], [out], vc(cnt(out) * (1 if ps else 2)))
+
+    def gat(kind, out, win, off, *rest):
+        add("V", kind, (out, win, off) + rest, aps(win, off, *rest), [out], 50 + GAT * CYC * cnt(out))
+
+    def mset(out, val):
+        add("V", "mset", (out, val), [], [out], vc(cnt(out) * (0.5 if two(out) else 1)))
+
+    def act(out, in_, f, bias=0.0, scale=1.0, acc=None):
+        add("A", "act", (out, in_, f, bias, scale, acc), aps(in_, bias, scale), aps(out, acc), vc(cnt(out)) + 30)
+
+    def agat(out, win, off):
+        add("A", "agat", (out, win, off), [win, off], [out], 65 + GAT * CYC * cnt(out))
+
+    def mm(lst):
+        add("P", "mm", lst, [m[1] for m in lst] + [m[2] for m in lst], [m[0] for m in lst], sum(max(64, cnt(m[2])) for m in lst) * PEC)
+
+    def grp(lst, first=True, last=True):
+        return [(o, l, r, first and i == 0, last and i == len(lst) - 1) for i, (o, l, r) in enumerate(lst)]
+
+    nd, nt = [0], [0]
+
+    def tile():
+        nt[0] += 1
+        return "ps%d" % nt[0]
+
+    def dma(q, out, in_, nbytes, sem=None):
+        if sem is None:
+            sem = "d%d" % nd[0]
+            nd[0] += 1
+        rd = [in_] if in_[0] in BUF else []
+        wr = [out] if out[0] in BUF else []
+        return add(q, "dma", (out, in_, sem), rd, wr, 100.0, 1800.0 + nbytes / 200.0)
+
+    def send(items, sem):
+        s = add("G", "send", (items, sem), [i[0] for i in items], [], 700.0)
+        add("X", "land", (len(items), sem), [], [i[1] for i in items], 0.0, 2500.0, s)
+
+    Zr = lambda u, m="mZ": R(m, 15 - u, 143 - u)
+    Bm = lambda m, u: R(m, 128 * u, 128 * u + 128)
+    I, NI, BIG, PB, O = R("mI"), R("mN"), R("mBIG"), R("mPB"), R("mO")
+    w = lambda n, a=0, b=NH: R(n, a, b)
+
+    dma("S", R("fw", XB, XB + L), ("lx",), 61440)
+    for i, n in enumerate(("ls", "lv", "th")):
+        dma("A", R("rwi", p0=8 * i, p1=8 * i + 8), (n,), 90000, "d19")
+    dma("S", R("lmi", 0, 768), ("lm", 0, 768), 480000)
+    dma("S", R("lmi", 768, S), ("lm", 768, S), 880000)
+    for h in range(2):
+        dma("S", R("pqi", L * h, L * h + L, p0=64 * h, p1=64 * h + 64), ("lp", 0, L, 64 * h), 1120000, "d18")
+        dma("S", R("pqi", L * h, L * h + L, p0=64 - 64 * h, p1=128 - 64 * h), ("lq", 0, L, 64 * h), 1120000, "d18")
+    dma("S", R("fw", 0, V), ("feat",), 2170000)
+    for i in range(16):
+        dma("S", R("snb", 0, V, p0=i, pstep=16), ("sn",), 2170000 + 131072 * (i + 1), "snl")
+
+    def pool(kind, out, in_, *args):
+        add("G", kind, (out, in_) + args, aps(in_), [out], 170 + 2 * CYC * cnt(out))
+    mset(R("ones"), 1.0)
+    pool("iota", R("io1"), None, [[-1, 16]], 128, 1)
+    pool("sel", R("mO1"), R("ones", 0, 128), [[-16, 8], [0, 16]], A.is_ge, 0, 1)
+    pool("sel", O, R("mO1"), [[16, 8], [0, 16]], A.is_ge, 15, -1)
+    for i in range(2):
+        pool("sel", R("z24", 144 * i, 144 * i + 143), R("ones", 0, 143, p1=24), [[-1, 143]], A.is_equal, 15 - 256 * i, 16)
+    pool("sel", I, R("ones", 0, 128), [[-1, 128]], A.is_equal, 0, 1)
+    pool("iota", R("h16"), None, [[16, 16]], 0, 0)
+    pool("sel", R("z24", 288, 416), R("ones", 0, 128, p1=24), [[-1, 8], [0, 16]], A.is_equal, -8, 1)
+    for a, b in CH:
+        pool("iota", R("kc", 16 * a, 16 * b), None, [[1, 16], [0, b - a]], 0, 0)
+    pool("iota", R("snb", V, WIN), None, [[0, WIN - V]], 0, 0)
+    mset(R("mZ"), 0.0)
+    copy(R("mZ", 15, 143, 16), R("mO", 0, 128, 16))
+    mset(R("fw", V, XB), 1024.0)
+    ts(R("ei"), R("io1"), 15, A.bitwise_and)
+    ts(R("oi"), R("io1"), 1, A.bitwise_and)
+    copy(R("etab"), R("ei"))
+    copy(R("ef"), R("ei"))
+    ts(R("otab"), R("oi"), 4096.0, A.mult, -2048.0, A.add)
+    ts(R("rm"), R("ei"), 0.0, A.is_equal)
+    icol = R("ef", 0, 1)
+    act(NI, I, F.Identity, 0.0, -1.0)
+    act(R("c128"), R("ones"), F.Identity, 0.0, 128.0)
+    act(R("c2048"), R("ones", 0, L), F.Identity, 0.0, 2048.0)
+    act(BIG, I, F.Identity, 0.0, -BIGV)
+    act(PB, I, F.Identity, 0.0, BIGV)
+    half = lambda m, h, lo, hi, step=1: R(m, lo, hi, step, 64 * h, 64 * h + 64)
+    own = lambda m, h, step=1: half(m, h, 64 * h, 64 * h + 64, step)
+    mset(R("mZ2"), 0.0)
+    mset(R("mY"), 0.0)
+    mset(R("sc"), 1.0)
+    for h in range(2):
+        copy(half("mZ2", h, 79 - 64 * h, 143 - 64 * h, 16), own("mO", h, 16))
+        copy(half("mY", h, 78 + h, 142 + h, 16), own("mO", h, 16))
+        tt(half("sc", h, 8 * h, 8 * h + 8), half("rm", h, 0, 16, 2), half("rm", h, 1, 16, 2), A.add)
+    ts(R("par", 0, 1), R("oi", 0, 1), 0.0, A.is_equal)
+    copy(R("par", 1, 2), R("oi", 0, 1))
+    for h in range(2):
+        for kk in range(2):
+            act(half("mD0", h, 128 * h + 64 * kk, 128 * h + 64 * kk + 64), own("mO", h), F.Identity, 0.0, half("par", h, kk, kk + 1))
+            act(half("mD0", 1 - h, 128 * h + 64 * kk, 128 * h + 64 * kk + 64), own("mN", 1 - h), F.Identity)
+        for kp in range(8):
+            act(Bm("mD", 8 * h + kp), R("mD0", 128 * h, 128 * h + 128), F.Identity, 0.0, R("sc", 8 * h + kp, 8 * h + kp + 1))
+    if "A" in E3:
+        act(R("mYP"), R("mY"), F.Identity, 0.0, BIGV)
+    if "V" in E3:
+        act(R("mY8"), R("mY"), F.Identity, 0.0, 8192.0)
+    for h in range(2):
+        act(half("mR", h, 0, 64), own("mBIG", h), F.Identity)
+    for kp in range(8):
+        act(R("mR", 128 * kp + 64, 128 * kp + 128), R("mY", 78 - 2 * kp, 142 - 2 * kp), F.Identity, 0.0, -BIGV)
+        act(R("mR", 128 * kp + 128, 128 * kp + 192), R("mR", 0, 64), F.Identity)
+    for h in range(2):
+        act(R("mJ", 64 * h, 64 * h + 64), R("mR", 0, 64), F.Identity)
+    mset(R("hm", 0, 2), 0.0)
+    for h in range(2):
+        mset(half("hm", h, h, h + 1), 1.0)
+    for h in range(2):
+        act(Bm("mH", h), I, F.Identity, 0.0, R("hm", h, h + 1))
+        act(Bm("mH", 2 + h), BIG, F.Identity, 0.0, R("hm", h, h + 1))
+        act(Bm("mH", 4 + h), R("mJ"), F.Identity, 0.0, R("hm", h, h + 1))
+        act(Bm("mH", 6 + h), Bm("mH", 4 + h), F.Identity, 0.0, -4096.0 / BIGV)
+    act(R("c05"), R("ones", 0, L), F.Identity, 0.0, 0.5)
+    act(R("lw"), R("h16"), F.Identity, icol)
+    act(R("dum"), R("lw"), F.Identity, float(S))
+    for t in range(RO):
+        act(R("lc", 16 * t, 16 * t + 16), R("lw"), F.Identity, XB + L * t - CEN)
+    if KB == "V":
+        for a, b in CH:
+            pool("iota", R("hi", a, b), None, [[1, b - a]], a - (a & 8), 0)
+        copy(w("hoff"), w("hi"))
+        mset(R("ki2"), 0)
+        act(R("rmb", 0, 16), R("rm"), F.Identity)
+        for i in (16, 32, 64):
+            act(R("rmb", i, 2 * i), R("rmb", 0, i), F.Identity)
+    act(R("mO4"), O, F.Identity, 0.0, 4096.0)
+    for u in range(16):
+        pool("sel", Bm("mB", u), O, [[-16, 8], [0, 16]], A.is_equal, -u, 1)
+    for u in range(16):
+        pool("sel", Bm("mB4", u), R("mO4"), [[-16, 8], [0, 16]], A.is_equal, -u, 1)
+    for u in range(1, 16):
+        pool("sel", Bm("mT", u), O, [[16, 8], [0, 16]], A.is_gt, u, -1)
+
+    ts(R("rw"), R("rwi"), -CEN, A.add)
+    p = tile()
+    mm(grp([(R(p, 0, NH), R("z24", 15 - u, 143 - u), R("rw", u, L, 16)) for u in range(16)]))
+    ts(w("s0"), R(p, 0, NH), CEN, A.add)
+    p = tile()
+    mm(grp([(R(p, 0, NH), R("z24", 159 - u, 287 - u), R("rw", u, L, 16)) for u in range(16)]))
+    act(w("thr"), R(p, 0, NH), F.Identity, 16 * CEN, 16.0)
+    act(w("thx"), R(p, 0, NH), F.Identity, 16 * (CEN + L), 16.0)
+    p = tile()
+    mm(grp([(R(p, 0, L), R("z24", 288, 416), R("rw"))]))
+    copy(R("v0"), R(p, 0, L))
+    for t in (1, 2):
+        send([(R("v0", LB * b, LB * b + LB), R("v%d" % t, LB * b, LB * b + LB), t * (1 + b)) for b in range(3)], "av%d" % t)
+    for a, b in ((0, 768), (768, S)):
+        ts(R("memi", a, b), R("lmi", a, b), V - 1, A.bitwise_and)
+        ts(R("mem", a, b), R("memi", a, b), -CEN, A.add)
+    ts(R("pm0"), R("pqi"), -CEN, A.add)
+    copy(R("um0"), R("pm0"))
+    for a, b in ((0, 512), (512, 1024), (1024, S)):
+        copy(R("comb", a, b), R("lmi", a, b))
+
+    def ksplit(n):
+        nb = -(-16 // (512 // n))
+        return [(16 * i // nb, 16 * (i + 1) // nb) for i in range(nb)]
+
+    def links(out, tab, off):
+        gat("gts", out, tab, off, -2047.5, 1.0 / 4096, A.add, A.mult)
+
+    def diffs(a, n, src, lhs, sub, dst, f, bias, scale):
+        for k0, k1 in ksplit(n):
+            bk = tile()
+            lst = []
+            for k in range(k0, k1):
+                o = R(bk, (k - k0) * n, (k - k0 + 1) * n)
+                lst += grp([(o, lhs, R(src, 16 * a + k, 16 * (a + n), 16))] + ([(o, NI, sub)] if f else []))
+            mm(lst)
+            if f:
+                act(R(dst, 16 * a + k0 * n, 16 * a + k1 * n), R(bk, 0, (k1 - k0) * n), f, bias, scale)
+            else:
+                for k in range(k0, k1):
+                    tt(R(dst, 16 * a + k * n, 16 * a + (k + 1) * n), R(bk, (k - k0) * n, (k - k0 + 1) * n), sub, A.is_equal)
+
+    def pairs(a, n, u, dst, eng):
+        for j0, j1 in ksplit(n):
+            bk = tile()
+            mm([(R(bk, (j - j0) * n, (j - j0 + 1) * n), Bm("mD", j), R(u, L * (j // 8) + a, L * (j // 8) + a + n), True, True) for j in range(j0, j1)])
+            o, i_ = R(dst, 16 * a + j0 * n, 16 * a + j1 * n), R(bk, 0, (j1 - j0) * n)
+            if eng == "A":
+                act(o, i_, F.Sigmoid, SIGB, SIGC)
+            else:
+                ts(o, i_, 0.0, A.is_equal)
+
+    def visit(t):
+        PAR[0] = t % 2
+        last = t == RO - 1
+        X = lambda a, b: R("fw", XB + L * t + a, XB + L * t + b)
+        pm, sw, vw = "pm%d" % t, "s%d" % t, "v%d" % t
+        tab = R("lmi") if t == 0 else R("comb", 0, S)
+
+        def front():
+            p = tile()
+            mm(grp([(R(p, 0, NH), Zr(u), R("fw", XB + L * t + u, XB + L * (t + 1), 16)) for u in range(16)]))
+            ts(w("ji"), R(p, 0, NH), float(t), A.add)
+            ts(w("ji2"), w("ji"), 15, A.bitwise_and)
+            copy(w("ju"), w("ji2"))
+            agat(R("eb"), R("etab"), w("ju"))
+            copy(w("su"), w(sw))
+            links(R("au"), tab, w("su"))
+            for a, b in MS:
+                for k in range(16):
+                    ts(R("mask", 16 * a + k, 16 * b, 16), R("eb", a, b), float(k), A.is_equal)
+            agat(R("ob"), R("otab"), w("ju"))
+            act(R("pen"), R("eb"), F.Identity, -4096.0, 8388608.0)
+
+        def pick(c, buf, off):
+            for a in range(16 * CH[c][0], 16 * CH[c][1], PIECE):
+                b = min(a + PIECE, 16 * CH[c][1])
+                gat("gtt", R(buf, 16 * a, 16 * b), R("mem", 0, S), R(off, a, b), R("mask", 16 * a, 16 * b), A.mult)
+
+        def sample(c):
+            h0, h1 = CH[c]
+            a, b = 16 * h0, 16 * h1
+            n = b - a
+            sg = lambda k: R("sg", 16 * a + k * n, 16 * a + (k + 1) * n)
+            um = "um%d" % t
+            p = tile()
+            mm(grp([(R(p, 0, n), Bm("mH", h), R(pm, L * h + a, L * h + b)) for h in range(2)]))
+            tt(R("pu", a, b), R(p, 0, n), R("ob", a, b), A.min)
+            p = tile()
+            mm(grp([(R(p, 0, n), Zr(k), R("g", 16 * a + k, 16 * b, 16)) for k in range(16)]))
+            for h in range(2):
+                copy(half(um, h, L * h + a, L * h + b), half(p, h, 0, n))
+            pairs(a, n, um, "sg", E3[c])
+            p = tile()
+            Mp = R(p, 0, n)
+            rest = [(Mp, BIG, R("c2048", 0, n)), (Mp, BIG, R("pu", a, b))] \
+                + [(Mp, Bm("mH", h), R(um, L * h + a, L * h + b)) for h in range(2)]
+            Y = lambda m, j: R(m, 78 - 64 * (j // 8) - 2 * (j % 8), 206 - 64 * (j // 8) - 2 * (j % 8))
+            if E3[c] == "A":
+                Sp = R(tile(), 0, n)
+                mm(grp([(Sp, PB, R("c128", 0, n))] + [(Sp, Y("mYP", j), sg(j)) for j in range(16)]))
+                act(R("rr", a, b), Sp, F.Identity, 0.0, 1.0 / BIGV / 32)
+                act(R("rr", L + a, L + b), Sp, F.Identity, UP / 32, 1.0 / BIGV / 32)
+                mm(grp(rest + [(Mp, BIG, R("rr", a, b)), (Mp, PB, R("rr", L + a, L + b))]))
+            else:
+                mm(grp(rest + [(Mp, Y("mY8", j), sg(j)) for j in range(16)]))
+                ts(Mp, Mp, 8192.0, A.min)
+            tt(R("n16", a, b), Mp, R("pu", a, b), A.max)
+            copy(R("n16", L + a, L + b), R("n16", a, b))
+            ts(R("nu", a, b), R("n16", a, b), V - CEN, A.min, CEN, A.add)
+            act(R("vf", a, b), Mp, F.Relu, -4096.0)
+
+        def dist(c):
+            a, b = 16 * CH[c][0], 16 * CH[c][1]
+            for a1 in range(a, b, PIECE):
+                b1 = min(a1 + PIECE, b)
+                if E4[a1 // PIECE] == "A":
+                    agat(R("f", 16 * a1, 16 * b1), R("fw", 0, XB), R("nu", a1, b1))
+                else:
+                    gat("gcp", R("f", 16 * a1, 16 * b1), R("fw", 0, XB), R("nu", a1, b1))
+            diffs(a, b - a, "f", I, X(a, b), "ab", F.Abs, 0.0, 16.0)
+
+        def mid(c):
+            h0, h1 = CH[c]
+            a, b, nh = 16 * h0, 16 * h1, h1 - h0
+            n = b - a
+            p = tile()
+            mm(grp([(R(p, 0, n), I, R("kc", a, b))] + [(R(p, 0, n), Zr(u), R("ab", 16 * a + u, 16 * b, 16)) for u in range(16)]))
+            for h in range(nh):
+                o, i_ = R("kmin", h0 + h, h0 + h + 1), R(p, h, n, nh)
+                add("V", "red", (o, i_), [i_], [o], vc(16))
+            ts(w("ki2", h0, h1), w("kmin", h0, h1), 15, A.bitwise_and)
+            p = tile()
+            if KB == "P":
+                copy(w("kb", h0, h1), w("ki2", h0, h1))
+                mm([(R(p, u, n, 16), Bm("mB", u), w("kb", h0, h1), True, True) for u in range(16)])
+            else:
+                gat("gtt", R("kx", a, b), R("ki2", h0 & 8, h1), w("hoff", h0, h1), R("rmb", 0, n), A.mult)
+                mm([(R(p, 0, n), O, R("kx", a, b), True, True)])
+            ts(R(p, 0, n), R(p, 0, n), icol, A.is_equal)
+            tt(R("seln", a, b), R(p, 0, n), R("n16", a, b), A.mult)
+            Np = R(tile(), 0, nh)
+            mm(grp([(Np, Zr(u), R("seln", a + u, b, 16)) for u in range(16)]))
+            tt(w("xo", h0, h1), Np, R("lc", 16 * t + h0, 16 * t + h1), A.min)
+            ts(w("xu", h0, h1), w("xo", h0, h1), CEN, A.add)
+            gat("gcp", R("s2b", a, b), R("snb"), w("xu", h0, h1))
+            Sp = R(tile(), 0, nh)
+            mm(grp([(Sp, Zr(u), R("s2b", a + u, b, 16)) for u in range(16)]))
+            ts(w("s2u", h0, h1), Sp, 1.0 / 16, A.mult)
+            act(w("s2w", h0, h1), Sp, F.Identity, 0.0, 1.0 / 16)
+            links(R("a2u", a, b), tab, w("s2u", h0, h1))
+            agat(R("fs", a, b), R("fw", 0, XB + L * (t + 1)), w("xu", h0, h1))
+            Xp = R(tile(), 0, n)
+            mm(grp([(Xp, I, R("fs", a, b)), (Xp, I, X(a, b)), (Xp, NI, R("c05", 0, n))]))
+            act(R("xy", a, b), Xp, F.Identity, MAGIC, 0.5)
+            act(R("xf", a, b) if last else R("xn", L * t + a, L * t + b), R("xy", a, b), F.Identity, -MAGIC)
+            gat("gtt", R("oc", a, b), tab, w("s2u", h0, h1), R("pen", a, b), A.min)
+            if not last:
+                gat("gtt", R("om", a, b), R("mem", 0, S), w("s2u", h0, h1), R("pen", a, b), A.min)
+
+        def xsend(b):
+            send([(R("xn", L * t + LB * b, L * t + LB * (b + 1)), R("fw", XB + L * (t + 1) + LB * b, XB + L * (t + 1) + LB * (b + 1)), 1 + b)],
+                 "ax%d_%d" % (t + 1, b))
+
+        def late():
+            snew = "sn%d" % (t + 1)
+            tt(w("c1"), w("kmin"), w("thr"), A.is_lt)
+            tt(w("df"), w("s2w"), w(sw), A.subtract)
+            tt(w("d2"), w("df"), w("c1"), A.mult)
+            ts(w("ne"), w("d2"), 0.0, A.is_equal, 4096.0, A.mult)
+            tt(w("k1"), w("ne"), w("s2w"), A.add)
+            tt(w("k16"), w("k1"), w("dum"), A.min)
+            tt(w("k32"), w("k1"), w("dum"), A.min)
+            tt(w(snew), w("d2"), w(sw), A.add)
+            if not last:
+                send([(R(snew, 5 * b, 5 * b + 5), R("s%d" % (t + 1), 5 * b, 5 * b + 5), 1 + b) for b in range(3)], "as%d" % (t + 1))
+            act(w("gw"), w("ne"), F.Identity, -4096.0)
+            p = tile()
+            mm([(R(p, u, L, 16), Bm("mB", u), w("k16"), True, True) for u in range(16)])
+            copy(R("kbb"), R(p, 0, L))
+            p = tile()
+            Gp = R(p, 0, L)
+            mm(grp([(Gp, I, R("c2048"))] + [(R(p, u, L, 16), Bm("mB", u), w("gw")) for u in range(16)]))
+            act(R("nogo"), Gp, F.Relu, 0.0, 1.0 / 2048, None if last else R("cnt", 0, 1))
+            p = tile()
+            mm([m for h in range(2) for m in grp([(R(p, L * h, L * h + L), NI, R("c2048")),
+                                                  (R(p, L * h, L * h + L), Bm("mH", 6 + h), R("nogo"))])])
+            tt(R("pk"), R(p, 0, 2 * L), R(pm), A.min)
+            for h in range(NH):
+                ts(R("eq", L * h + 16 * h, L * (h + 1)), R("kbb", 16 * h, L), R("k32", h, h + 1), A.is_equal)
+            p = tile()
+            Lp = R(p, 0, L)
+            mm(grp([(Lp, I, R("ones", 0, L))] + [(R(p, 16 * h + 16, L), O, R("eq", L * h + 16 * h + 16, L * (h + 1))) for h in range(8)], last=False))
+            mm(grp([(R(p, 16 * h + 16, L), O, R("eq", L * h + 16 * h + 16, L * (h + 1))) for h in range(8, NH - 1)]
+                   + [(R(p, u, L, 16), Bm("mT", u), R("eq", u, L * NH, L + 16)) for u in range(1, 16)], first=False))
+            act(R("lb"), Lp, F.Identity, -256.0, 256.0)
+            Op = R(tile(), 0, NH)
+            mm(grp([(Op, I, w("k16"))] + [(Op, Zr(u), R("lb", u, L, 16)) for u in range(16)]))
+            tt(w("of"), Op, w("dum"), A.min)
+            copy(w("ou"), w("of"))
+            if not last:
+                c0 = lambda n: R(n, 0, 1)
+                act(c0("a1"), c0("cnt"), F.Identity, (L - 15.5) / 32, -1.0 / 32)
+                act(c0("a2"), c0("a1"), F.Identity, MAGIC)
+                act(c0("a3"), c0("a2"), F.Identity, 512 * MAGIC, -512.0)
+                act(c0("a4"), c0("cnt"), F.Identity, c0("a3"), -16.0)
+                act(w("thr"), w("thx"), F.Identity, c0("a4"))
+            else:
+                p = tile()
+                mm([(R(p, u, L, 16), Bm("mB", u), w(snew), True, True) for u in range(16)])
+                act(R("sf"), R(p, 0, L), F.Identity)
+                dma("S", ("ys",), R("sf", pstep=16), 8000)
+
+        def values():
+            if not last:
+                Vp = R(tile(), 0, L)
+                mm(grp([(Vp, NI, R("pen")), (Vp, I, R(vw))]))
+                act(R("bm"), Vp, F.Identity, -4096.0)
+            p = tile()
+            Vp = R(p, 0, L)
+            mm(grp([(Vp, NI, R("pen")), (Vp, I, R(vw))] + [(R(p, u, L, 16), Bm("mB4", u), w(sw)) for u in range(16)]))
+            act(R("bc"), Vp, F.Identity, CEN - 4096.0)
+
+        def write():
+            for tb, o, bb in (("comb", "oc", "bc"), ("mem", "om", "bm"))[:1 if last else 2]:
+                add("V", "sct", (R(tb), w("ou"), R(o), R(bb), A.max), [w("ou"), R(o), R(bb)], [R(tb)], 50 + SCT * CYC * L)
+
+        def recode(c):
+            a, b = 16 * CH[c][0], 16 * CH[c][1]
+            n = b - a
+            sh = lambda k: R("sh", 16 * a + k * n, 16 * a + (k + 1) * n)
+            p = tile()
+            Pp, Mp, PM = R(p, 0, n), R(p, n, 2 * n), R(p, 0, 2 * n)
+            x = tile()
+            mm(grp([(R(x, 0, n), Zr(k, "mZ2"), R("h", 16 * a + k, 16 * b, 16)) for k in range(16)]))
+            for h in range(2):
+                copy(half("n16", 1 - h, L * h + a, L * h + b), half(x, 1 - h, 0, n))
+            pairs(a, n, "n16", "sh", E7[c])
+            z = tile() if E7[c] == "A" else p
+            SS = R(z, 0, 2 * n)
+            sums = [(R(z, 0, n), R("mR", 128 * k + 64, 128 * k + 192), sh(k)) for k in range(8)] \
+                + [(R(z, n, 2 * n), R("mR", 128 * k, 128 * k + 128), sh(8 + k)) for k in range(8)]
+            rest = [(Pp, I, R("n16", a, b)), (Mp, I, R("n16", L + a, L + b))] \
+                + [(R(p, n * h, n * h + n), Bm("mH", 2 + h), R("vf", a, b)) for h in range(2)] \
+                + [(R(p, n * h, n * h + n), Bm("mH", 4 + h), R("nogo", a, b)) for h in range(2)]
+            if E7[c] == "A":
+                mm(grp([(SS, BIG, R("c128", 0, 2 * n))] + sums))
+                act(R("r2", 2 * a, 2 * b), SS, F.Identity, 0.0, -1.0 / BIGV)
+                act(R("r2", 2 * L + 2 * a, 2 * L + 2 * b), SS, F.Identity, UP, -1.0 / BIGV)
+                mm(grp([(PM, PB, R("r2", 2 * a, 2 * b)), (PM, BIG, R("r2", 2 * L + 2 * a, 2 * L + 2 * b))] + rest))
+            else:
+                mm(grp([(PM, BIG, R("c128", 0, 2 * n)), (PM, PB, R("c128", 0, 2 * n))] + sums + rest))
+            po = "pf" if last else "po%d" % t
+            tt(R(po, a, b), Pp, R("pk", a, b), A.max)
+            tt(R(po, L + a, L + b), Mp, R("pk", L + a, L + b), A.max)
+            if last:
+                act(R("pf2", a, b), R("pf", a, b), F.Identity, CEN)
+                act(R("pf2", L + a, L + b), R("pf", L + a, L + b), F.Identity, CEN)
+
+        def psend(b):
+            send([(R("po%d" % t, q + LB * b, q + LB * (b + 1)), R("%s%d" % (to, t + 1), q + LB * b, q + LB * (b + 1)), 1 + b)
+                  for to in ("um", "pm") for q in (0, L)],
+                 "ap%d_%d" % (t + 1, b))
+
+        nc = len(CH)
+        def stage(tag, fn, *args):
+            TAG[0] = tag + ("L" if last else "")
+            fn(*args)
+
+        stage("front", front)
+        stage("val", values)
+        for c in range(nc):
+            stage("p%d" % c, pick, c, "g", "au")
+            stage("s%d" % c, sample, c)
+            stage("d%d" % c, dist, c)
+            stage("m%d" % c, mid, c)
+            stage("q%d" % c, pick, c, "h", "a2u")
+        if not last:
+            for b in range(3):
+                xsend(b)
+        else:
+            dma("S", ("yx",), R("xf"), 122880)
+        stage("late", late)
+        stage("write", write)
+        if last:
+            dma("S", ("ylm", 0, 768), R("comb", 0, 768), 400000)
+            dma("S", ("ylm", 768, S), R("comb", 768, S), 800000)
+        for c in range(nc):
+            stage("r%d" % c, recode, c)
+        if not last:
+            for b in range(3):
+                psend(b)
+        else:
+            for h in range(2):
+                dma("S", ("yp", 0, L, 64 * h), half("pf2", h, L * h, L * h + L), 122880)
+                dma("A", ("yq", 0, L, 64 * h), half("pf2", 1 - h, L * h, L * h + L), 240000)
+
+    for t in range(RO):
+        visit(t)
+    return ops
+
+
+def clash(x, y):
+    if x[2] <= y[1] or y[2] <= x[1]:
+        return False
+    if x[3] == y[3] and x[3] > 1 and (x[1] - y[1]) % x[3]:
+        return False
+    if x[5] <= y[4] or y[5] <= x[4]:
+        return False
+    return not (x[6] == y[6] and x[6] > 1 and (x[4] - y[4]) % x[6])
+
+
+def depend(ops):
+    hist = {}
+    for o in ops:
+        dep = set()
+        if o["after"] is not None:
+            dep.add(o["after"]["id"])
+        for isw, lst in ((False, o["r"]), (True, o["w"])):
+            for x in set(lst):
+                psum = x[0][:2] == "ps"
+                for (y, yw, oid, eng) in hist.get(x[0], ()):
+                    if oid != o["id"] and oid not in dep and ((psum and eng != o["eng"]) or ((isw or yw) and clash(x, y))):
+                        dep.add(oid)
+        o["dep0"] = dep
+        o["new"] = [n for n in set(x[0] for x in o["w"]) if n[:2] == "ps" and n not in hist]
+        for isw, lst in ((False, o["r"]), (True, o["w"])):
+            for x in set(lst):
+                hist.setdefault(x[0], []).append((x, isw, o["id"], o["eng"]))
+    return {n: set(e[2] for e in h) for n, h in hist.items() if n[:2] == "ps"}
+
+
+def schedule(ops, users, prio, slack):
+    if "succ" not in ops[0]:
+        for o in ops:
+            o["succ"] = []
+            o["tiles"] = sorted(set(x[0] for x in o["r"] + o["w"] if x[0][:2] == "ps"))
+        for o in ops:
+            for d in o["dep0"]:
+                ops[d]["succ"].append(o)
+        for o in reversed(ops):
+            o["tail"] = o["cost"] + o["lat"] + max([s["tail"] + HOP for s in o["succ"]] + [0.0])
+    if prio is None:
+        prio = {o["id"]: o["tail"] + BIAS.get(o["tag"], 0.0) for o in ops}
+    ready = {e: [] for e in "VAPGSX"}
+    for o in ops:
+        o["dep"], o["rt"], o["left"] = o["dep0"], 0.0, len(o["dep0"])
+        if not o["left"]:
+            ready[o["eng"]].append(o)
+    free = {e: 0.0 for e in "VAPGSX"}
+    tenant, banks, order = [None] * 8, {}, []
+    alive = {n: len(us) for n, us in users.items()}
+    ends = {n: 0.0 for n in users}
+    open_ = [(0.0, b) for b in range(8)]
+    while len(order) < len(ops):
+        t0, eng = None, None
+        for e, lst in ready.items():
+            if lst:
+                if e == "P":
+                    ts_ = [(o["rt"] if not o["new"] else max(o["rt"], open_[0][0])) for o in lst if open_ or not o["new"]]
+                    if not ts_:
+                        continue
+                    t = max(free[e], min(ts_))
+                else:
+                    t = max(free[e], min([o["rt"] for o in lst]))
+                if t0 is None or t < t0:
+                    t0, eng = t, e
+        if eng is None:
+            return None
+        lim = t0 + slack
+        cand = [o for o in ready[eng] if o["rt"] <= lim and (not o["new"] or (open_ and open_[0][0] <= lim))]
+        o = min(cand, key=lambda c: c["id"]) if eng in "SG" else max(cand, key=lambda c: prio[c["id"]])
+        st = max(free[eng], o["rt"])
+        if o["new"]:
+            st = max(st, open_[0][0])
+            pick = [x for x in open_ if x[0] <= st][-1]
+            open_.remove(pick)
+            if tenant[pick[1]]:
+                o["dep"] = o["dep0"] | users[tenant[pick[1]]]
+            tenant[pick[1]] = o["new"][0]
+            banks[o["new"][0]] = pick[1]
+        ready[eng].remove(o)
+        o["t0"] = st
+        free[eng] = st + o["cost"]
+        o["t1"] = t1 = st + o["cost"] + o["lat"]
+        order.append(o)
+        t1 += HOP
+        for n in o["tiles"]:
+            alive[n] -= 1
+            ends[n] = max(ends[n], t1)
+            if not alive[n]:
+                open_.append((ends[n], banks[n]))
+                open_.sort()
+        for s in o["succ"]:
+            if s["rt"] < t1:
+                s["rt"] = t1
+            s["left"] -= 1
+            if not s["left"]:
+                ready[s["eng"]].append(s)
+    return order, banks
+
+
+def latest(ops, order):
+    succ = {o["id"]: [] for o in ops}
+    for o in ops:
+        for d in o["dep0"]:
+            succ[d].append(o["id"])
+    back, busy = {}, {e: [] for e in "VAPGSX"}
+    for o in sorted(order, key=lambda o: (-o["t1"], -o["id"])):
+        at = max([back[s] + HOP for s in succ[o["id"]]] + [0.0]) + o["lat"]
+        lst, i = busy[o["eng"]], 0
+        while i < len(lst) and lst[i][0] < at + o["cost"]:
+            at = max(at, lst[i][1])
+            i += 1
+        while i and lst[i - 1][0] >= at + o["cost"]:
+            i -= 1
+        lst.insert(i, (at, at + o["cost"]))
+        back[o["id"]] = at + o["cost"]
+    return back
+
+
+def improve(ops, users, rounds, seed):
+    rnd = np.random.RandomState(seed)
+    tags = sorted(set(o["tag"] for o in ops))
+
+    def look(res):
+        before, on = {}, {}
+        for x in res[0]:
+            before[x["id"]] = on.get(x["eng"])
+            on[x["eng"]] = x
+        o, pairs = max(ops, key=lambda o: o["t1"]), []
+        end = o["t1"]
+        while o is not None:
+            c = [ops[d] for d in o["dep"] if abs(ops[d]["t1"] + HOP - o["t0"]) < 1]
+            if not c and before[o["id"]] is not None and o["rt"] < o["t0"] - 1 and o["eng"] in "VAP":
+                pairs.append((o["id"], before[o["id"]]["id"]))
+            o = c[0] if c else before[o["id"]]
+        return end, pairs, res[0]
+
+    for t in tags:
+        BIAS[t] = STAGGER * int(t[1]) if t[1].isdigit() and t[0] != "r" else 0.0
+    schedule(ops, users, None, SLACK)
+    prio = {o["id"]: o["tail"] + BIAS.get(o["tag"], 0.0) for o in ops}
+    now = look(schedule(ops, users, prio, SLACK))
+    best = (now[0], prio)
+    for r in range(rounds):
+        new, move = dict(prio), rnd.rand()
+        if move < 0.6 and now[1]:
+            for _ in range(int(rnd.randint(1, 4))):
+                a, b = now[1][int(rnd.randint(len(now[1])))]
+                d = abs(new[b] - new[a]) + float(rnd.choice([50.0, 500.0, 2000.0]))
+                if rnd.rand() < 0.5:
+                    new[a] += d
+                else:
+                    new[b] -= d
+        elif move < 0.97:
+            t, d = tags[int(rnd.randint(len(tags)))], float(rnd.choice([-1.0, 1.0]) * rnd.choice([300.0, 1000.0, 3000.0]))
+            eng = str(rnd.choice(["VAP", "V", "A", "P"]))
+            for o in ops:
+                if o["eng"] in eng and (o["tag"] == t or (d > 0 and o["tag"][:-1] == t)):
+                    new[o["id"]] += d
+        else:
+            schedule(ops, users, prio, SLACK)
+            new = latest(ops, now[2])
+        res = schedule(ops, users, new, SLACK)
+        if res is None:
+            continue
+        got = look(res)
+        if got[0] <= now[0] + 400.0 * (1.0 - r / rounds) * rnd.rand():
+            prio, now = new, got
+        if got[0] < best[0]:
+            best = (got[0], new)
+    return schedule(ops, users, best[1], SLACK)
+
+
+PLAN = []
+
+
+def rank_program(g, core, T, topo):
+    rank = T.rank_of(core)
+    if rank is None:
+        return
+    if not PLAN:
+        ops = plan()
+        PLAN.append((ops,) + improve(ops, depend(ops), ROUNDS, SEED))
+    ops, order, banks = PLAN[0]
+    n = len(T.cores)
+    Q = {"V": g.vector, "A": g.scalar, "P": g.tensor, "G": g, "S": g.sync}
+
+    def ap(r):
+        if not isinstance(r, tuple):
+            return r
+        if r[0] in banks:
+            name, at = "bank%d" % banks[r[0]], 0
+        elif r[0] in BUF:
+            name, at = POOL[r[0]]
+        elif len(r) == 4:
+            return T[r[0]][r[3]:r[3] + 64, r[1]:r[2]]
+        else:
+            return T[r[0]][:] if len(r) == 1 else T[r[0]][:, r[1]:r[2]]
+        last = r[1] + (cnt(r) - 1) * r[3] + 1
+        return T[name][r[4]:r[5]:r[6], at + r[1]:at + last:r[3]]
+
+    def ind(win, off):
+        return ap(win).indirect(ap(off))
+
+    def engines(dst, parts):
+        es = topo.engines(core, dst)
+        k = 1
+        while 2 * k * parts <= len(es):
+            k *= 2
+        return [sum(1 << e for e in es[i * k:(i + 1) * k]) for i in range(parts)], k
+
+    total, shared = {}, {}
+    for o in ops:
+        if o["kind"] == "dma":
+            shared[o["args"][2]] = shared.get(o["args"][2], 0) + 16
+    known = {e: {} for e in Q}
+    done = {}
+    for o in order:
+        e, k, a = o["eng"], o["kind"], o["args"]
+        if k == "land":
+            per = engines(T.cores[(rank + 1) % n], a[0])[1]
+            total[a[1]] = per * a[0]
+            done[o["id"]] = (a[1], per * a[0], {})
+            continue
+        q, kn = Q[e], known[e]
+        need = {}
+        for d in o["dep"]:
+            s, v, _ = done[d]
+            if kn.get(s, 0) < v:
+                need[d] = (s, v)
+        for d in sorted(need, key=lambda d: -ops[d]["t1"]):
+            s, v, clock = done[d]
+            if kn.get(s, 0) < v:
+                v = max(vv for (ss, vv) in need.values() if ss == s)
+                q.wait_ge(T.sem[s], v)
+                kn[s] = v
+            for s2, v2 in clock.items():
+                if kn.get(s2, 0) < v2:
+                    kn[s2] = v2
+        sem, inc = "e" + e, 1
+        if k == "copy":
+            i = q.tensor_copy(ap(a[0]), ap(a[1]))
+        elif k == "ts":
+            i = q.tensor_scalar(ap(a[0]), ap(a[1]), ap(a[2]), ap(a[3]), a[4]) if a[5] is None else \
+                q.tensor_scalar(ap(a[0]), ap(a[1]), ap(a[2]), ap(a[3]), a[4], a[5])
+        elif k == "tt":
+            i = q.tensor_tensor(ap(a[0]), ap(a[1]), ap(a[2]), a[3])
+        elif k == "mset":
+            i = q.memset(ap(a[0]), a[1])
+        elif k == "red":
+            i = q.tensor_reduce(ap(a[0]), ap(a[1]), AX.X, A.min)
+        elif k == "gcp":
+            i = q.tensor_copy(ap(a[0]), ind(a[1], a[2]))
+        elif k == "gts":
+            i = q.tensor_scalar(ap(a[0]), ind(a[1], a[2]), a[3], a[4], a[5], a[6])
+        elif k == "gtt":
+            i = q.tensor_tensor(ap(a[0]), ind(a[1], a[2]), ap(a[3]), a[4])
+        elif k == "sct":
+            i = q.tensor_tensor(ind(a[0], a[1]), ap(a[2]), ap(a[3]), a[4])
+        elif k == "act":
+            i = q.activation(ap(a[0]), ap(a[1]), a[2], bias=ap(a[3]), scale=ap(a[4]), accum_out=ap(a[5]))
+        elif k == "agat":
+            i = q.activation(ap(a[0]), ind(a[1], a[2]), F.Identity)
+        elif k == "mm":
+            for m in a:
+                i = q.matmul(ap(m[0]), ap(m[1]), ap(m[2]), m[3], m[4])
+        elif k == "iota":
+            if BUF[a[0][0]][2] == "int32":
+                i = q.iota(ap(a[0]), a[2], a[3], a[4])
+            else:
+                i = q.iota(ap(a[0]), a[2], a[3], a[4], allow_small_or_imprecise_dtypes=True)
+        elif k == "sel":
+            i = q.affine_select(ap(a[0]), ap(a[1]), a[2], a[3], 0.0, a[4], a[5])
+        elif k == "dma":
+            i = q.dma_start(ap(a[0]), ap(a[1]))
+            sem, inc = a[2], 16
+        elif k == "send":
+            trs = []
+            for j, (src, dst, ahead) in enumerate(a[0]):
+                to = T.cores[(rank + ahead) % n]
+                masks, per = engines(to, len(a[0]))
+                rid, pid, _ = topo.addr(to)
+                trs.append(RemoteDMATransfer(dst_ids=[DstId(rid=rid, pnc=pid)], dma_engine_mask=masks[j], remote_sem=T.sem[a[1]],
+                                             src=ap(src), dst=ap(dst)))
+                total["sent"] = total.get("sent", 0) + per
+            q.remote_dma_fused(trs, local_sem=T.sem.sent)
+            continue
+        i.then_inc(T.sem[sem], inc)
+        total[sem] = total.get(sem, 0) + inc
+        done[o["id"]] = (sem, shared[sem] if k == "dma" else total[sem], dict(kn))
+    for s, v in total.items():
+        g.wait_ge(T.sem[s], v)

@@ -8,8 +8,8 @@ CH = [(0, 6), (6, 10), (10, 15)]
 MS = [(0, 128), (128, 240)]
 E3, E7 = "AAV", "AAA"
 E4 = "AAVAAAAA"
-SEED, ROUNDS, SLACK, STAGGER = 6, 3500, 130.0, -2000.0
-KB = "V"
+SEED, ROUNDS, SLACK, STAGGER = 2, 4000, 120.0, -2000.0
+MIX = 0.7
 PIECE = 32
 XB = 4112
 WIN = XB + RO * L
@@ -22,7 +22,7 @@ SIGC, SIGB = 128.0, -math.log(31.0)
 SCRATCH = {}
 BUF = {}
 POOL = {}
-DUP = ("ju", "eb", "pen", "mask", "n16", "vf", "nogo", "pk", "h", "kmin", "s2u", "bc", "bm", "au")
+DUP = ("ju", "eb", "pen", "mask", "n16", "vf", "nogo", "pk", "h", "kmin", "s2u", "bc", "bm", "au", "ob")
 
 
 def _sb(name, cols, dt, parts=128):
@@ -36,16 +36,17 @@ def _sb(name, cols, dt, parts=128):
 
 
 for _n, _c, _d in [
-    ("fw", WIN, "bfloat16"), ("snb", WIN, "int32"), ("lmi", S, "int32"), ("memi", S, "int32"),
+    ("fw", WIN, "bfloat16"), ("snb", WIN, "float32"), ("sni", 256, "int32"), ("sn16", 256, "float16"), ("lmi", S, "int32"), ("memi", S, "int32"),
     ("comb", S + L, "float32"), ("mem", S + L, "float32"), ("pqi", 2 * L, "int32"),
     ("ones", 256, "bfloat16"), ("c128", 256, "bfloat16"), ("c2048", L, "bfloat16"), ("c05", L, "bfloat16"),
     ("mI", 128, "bfloat16"), ("mN", 128, "bfloat16"), ("mBIG", 128, "bfloat16"), ("mPB", 128, "bfloat16"),
     ("mO1", 128, "bfloat16"), ("mO", 128, "bfloat16"), ("mZ", 144, "bfloat16"), ("mZ2", 144, "bfloat16"), ("mY", 208, "bfloat16"),
-    ("mYP", 208, "bfloat16"), ("mY8", 208, "bfloat16"), ("mD0", 256, "bfloat16"), ("mD", 2048, "bfloat16"), ("mR", 17 * 64, "bfloat16"),
+    ("mYP", 208, "bfloat16"), ("mY8", 208, "bfloat16"), ("mYN", 208, "bfloat16"), ("mD0", 256, "bfloat16"), ("mD", 2048, "bfloat16"), ("mR", 17 * 64, "bfloat16"),
     ("mJ", 128, "bfloat16"), ("mH", 1024, "bfloat16"), ("hm", 16, "float32"), ("sc", 16, "float32"), ("par", 16, "float32"), ("ob", L, "bfloat16"),
     ("um0", 2 * L, "float16"), ("um1", 2 * L, "float16"), ("um2", 2 * L, "float16"), ("mB", 2048, "bfloat16"), ("mB4", 2048, "bfloat16"), ("mT", 2048, "bfloat16"),
     ("io1", 16, "int32"), ("ei", 16, "int32"), ("oi", 16, "int32"), ("etab", 16, "bfloat16"), ("otab", 16, "bfloat16"),
-    ("ef", 16, "float32"), ("rm", 16, "float32"), ("mO4", 128, "bfloat16"), ("hi", 16, "int32"), ("hoff", 16, "uint16"), ("rmb", 128, "bfloat16"), ("kx", L, "bfloat16"), ("ne", 16, "float32"),
+    ("ef", 16, "float32"), ("rm", 16, "float32"), ("mZ4", 144, "bfloat16"), ("ku", 16, "uint16"), ("gu", 16, "uint16"), ("t01", 16, "bfloat16"), ("go", L, "bfloat16"),
+    ("pk1", 2 * L, "float32"), ("ne", 16, "float32"),
     ("h16", 16, "float32"), ("lw", 16, "float32"), ("dum", 16, "float32"), ("dums", 16, "float32"), ("lc", 48, "float32"),
     ("kc", L, "bfloat16"), ("thw", 16, "float32"), ("thx", 16, "float32"), ("thr", 16, "float32"),
     ("ji", 16, "int32"), ("ji2", 16, "int32"), ("ju", 16, "uint16"), ("su", 16, "uint16"),
@@ -56,11 +57,11 @@ for _n, _c, _d in [
     ("s2u", 16, "uint16"), ("fs", L, "bfloat16"), ("xy", L, "float32"), ("xn", 2 * L, "bfloat16"),
     ("s2w", 16, "float32"), ("c1", 16, "float32"), ("df", 16, "float32"), ("d2", 16, "float32"), ("gw", 16, "bfloat16"),
     ("sn1", 16, "float16"), ("sn2", 16, "float16"), ("sn3", 16, "float16"),
-    ("k0", 16, "float32"), ("k1", 16, "float32"), ("k32", 16, "float32"), ("k16", 16, "float16"), ("kbb", L, "float16"),
+    ("k0", 16, "float32"), ("k1", 16, "float32"), ("k32", 16, "float32"), ("k16", 16, "float16"),
     ("eq", NH * L, "bfloat16"), ("lb", L, "bfloat16"), ("of", 16, "float32"), ("ou", 16, "uint16"),
     ("nogo", L, "bfloat16"), ("cnt", 4, "float32"), ("a1", 4, "float32"), ("a2", 4, "float32"), ("a3", 4, "float32"), ("a4", 4, "float32"),
     ("oc", L, "float32"), ("om", L, "float32"), ("bc", L, "float32"), ("bm", L, "float32"),
-    ("r2", 4 * L, "bfloat16"), ("pk", 2 * L, "float16"),
+    ("r2", 4 * L, "bfloat16"), ("pk", 2 * L, "float32"),
     ("pm0", 2 * L, "float16"), ("pm1", 2 * L, "float16"), ("pm2", 2 * L, "float16"),
     ("po0", 2 * L, "float16"), ("po1", 2 * L, "float16"), ("pf", 2 * L, "float32"), ("pf2", 2 * L, "float32"),
     ("s0", 16, "float16"), ("s1", 16, "float16"), ("s2", 16, "float16"),
@@ -81,7 +82,7 @@ SEMAPHORES = (["eV", "eA", "eP", "eG", "sent", "snl"] + ["d%d" % _i for _i in ra
               + ["%s%d_%d" % (_a, _t, _b) for _a in ("ax", "ap") for _t in (1, 2) for _b in range(3)]
               + ["as1", "as2", "av1", "av2"])
 SIZE = {"float32": 4, "int32": 4, "bfloat16": 2, "float16": 2, "uint16": 2}
-CYC, PEC, HOP, GAT, SCT = 1.04, 0.52, 120.0, 1.56, 3.8
+CYC, PEC, HOP, GAT, SCT = 0.93, 0.47, 170.0, 1.56, 3.8
 PAR, TAG = [0], ["init"]
 BIAS = {}
 
@@ -175,9 +176,9 @@ def plan():
     for h in range(2):
         dma("S", R("pqi", L * h, L * h + L, p0=64 * h, p1=64 * h + 64), ("lp", 0, L, 64 * h), 1120000, "d18")
         dma("S", R("pqi", L * h, L * h + L, p0=64 - 64 * h, p1=128 - 64 * h), ("lq", 0, L, 64 * h), 1120000, "d18")
-    dma("S", R("fw", 0, V), ("feat",), 2170000)
-    for i in range(16):
-        dma("S", R("snb", 0, V, p0=i, pstep=16), ("sn",), 2170000 + 131072 * (i + 1), "snl")
+    dma("S", R("sni"), ("sn",), 1250000, "snl")
+    dma("S", R("fw", 0, V), ("feat",), 2300000)
+
 
     def pool(kind, out, in_, *args):
         add("G", kind, (out, in_) + args, aps(in_), [out], 170 + 2 * CYC * cnt(out))
@@ -229,11 +230,13 @@ def plan():
         act(R("mYP"), R("mY"), F.Identity, 0.0, BIGV)
     if "V" in E3:
         act(R("mY8"), R("mY"), F.Identity, 0.0, 8192.0)
+    act(R("mYN"), R("mY"), F.Identity, 0.0, -BIGV)
+    late_pool = []
     for h in range(2):
         act(half("mR", h, 0, 64), own("mBIG", h), F.Identity)
     for kp in range(8):
-        act(R("mR", 128 * kp + 64, 128 * kp + 128), R("mY", 78 - 2 * kp, 142 - 2 * kp), F.Identity, 0.0, -BIGV)
-        act(R("mR", 128 * kp + 128, 128 * kp + 192), R("mR", 0, 64), F.Identity)
+        late_pool.append((R("mR", 128 * kp + 64, 128 * kp + 128), R("mYN", 78 - 2 * kp, 142 - 2 * kp)))
+        late_pool.append((R("mR", 128 * kp + 128, 128 * kp + 192), R("mR", 0, 64)))
     for h in range(2):
         act(R("mJ", 64 * h, 64 * h + 64), R("mR", 0, 64), F.Identity)
     mset(R("hm", 0, 2), 0.0)
@@ -243,27 +246,22 @@ def plan():
         act(Bm("mH", h), I, F.Identity, 0.0, R("hm", h, h + 1))
         act(Bm("mH", 2 + h), BIG, F.Identity, 0.0, R("hm", h, h + 1))
         act(Bm("mH", 4 + h), R("mJ"), F.Identity, 0.0, R("hm", h, h + 1))
-        act(Bm("mH", 6 + h), Bm("mH", 4 + h), F.Identity, 0.0, -4096.0 / BIGV)
     act(R("c05"), R("ones", 0, L), F.Identity, 0.0, 0.5)
     act(R("lw"), R("h16"), F.Identity, icol)
     act(R("dum"), R("lw"), F.Identity, float(S))
     for t in range(RO):
         act(R("lc", 16 * t, 16 * t + 16), R("lw"), F.Identity, XB + L * t - CEN)
-    if KB == "V":
-        for a, b in CH:
-            pool("iota", R("hi", a, b), None, [[1, b - a]], a - (a & 8), 0)
-        copy(w("hoff"), w("hi"))
-        mset(R("ki2"), 0)
-        act(R("rmb", 0, 16), R("rm"), F.Identity)
-        for i in (16, 32, 64):
-            act(R("rmb", i, 2 * i), R("rmb", 0, i), F.Identity)
-    act(R("mO4"), O, F.Identity, 0.0, 4096.0)
+    pool("iota", R("t01", 0, 2), None, [[1, 2]], 0, 0)
+    act(R("mZ4"), R("mZ"), F.Identity, 0.0, 4096.0)
     for u in range(16):
         pool("sel", Bm("mB", u), O, [[-16, 8], [0, 16]], A.is_equal, -u, 1)
-    for u in range(16):
-        pool("sel", Bm("mB4", u), R("mO4"), [[-16, 8], [0, 16]], A.is_equal, -u, 1)
+    for i in range(0, 2048, 512):
+        act(R("mB4", i, i + 512), R("mB", i, i + 512), F.Identity, 0.0, 4096.0)
     for u in range(1, 16):
-        pool("sel", Bm("mT", u), O, [[16, 8], [0, 16]], A.is_gt, u, -1)
+        pool("sel", Bm("mT", u), Zr(u, "mZ4"), [[16, 8], [0, 16]], A.is_gt, u, -1)
+    for o, i_ in late_pool:
+        pool("sel", o, i_, [[0, 64]], A.is_equal, 0, 0)
+    mset(R("lb", 0, 16), 0.0)
 
     ts(R("rw"), R("rwi"), -CEN, A.add)
     p = tile()
@@ -272,10 +270,15 @@ def plan():
     p = tile()
     mm(grp([(R(p, 0, NH), R("z24", 159 - u, 287 - u), R("rw", u, L, 16)) for u in range(16)]))
     act(w("thr"), R(p, 0, NH), F.Identity, 16 * CEN, 16.0)
-    act(w("thx"), R(p, 0, NH), F.Identity, 16 * (CEN + L), 16.0)
+    act(w("thx"), R(p, 0, NH), F.Identity, 16 * CEN, 16.0)
     p = tile()
     mm(grp([(R(p, 0, L), R("z24", 288, 416), R("rw"))]))
     copy(R("v0"), R(p, 0, L))
+    copy(R("sn16"), R("sni"))
+    for i in range(0, 16, 2):
+        p = tile()
+        mm([(R(p, 256 * j, 256 * j + 256), Bm("mB", i + j), R("sn16"), True, True) for j in range(2)])
+        act(R("snb", 256 * i, 256 * i + 512), R(p), F.Identity)
     for t in (1, 2):
         send([(R("v0", LB * b, LB * b + LB), R("v%d" % t, LB * b, LB * b + LB), t * (1 + b)) for b in range(3)], "av%d" % t)
     for a, b in ((0, 768), (768, S)):
@@ -325,18 +328,20 @@ def plan():
         tab = R("lmi") if t == 0 else R("comb", 0, S)
 
         def front():
-            p = tile()
-            mm(grp([(R(p, 0, NH), Zr(u), R("fw", XB + L * t + u, XB + L * (t + 1), 16)) for u in range(16)]))
-            ts(w("ji"), R(p, 0, NH), float(t), A.add)
-            ts(w("ji2"), w("ji"), 15, A.bitwise_and)
-            copy(w("ju"), w("ji2"))
-            agat(R("eb"), R("etab"), w("ju"))
             copy(w("su"), w(sw))
-            links(R("au"), tab, w("su"))
-            for a, b in MS:
+            for i, (a, b) in enumerate(MS):
+                TAG[0] = "f%d" % i + ("L" if last else "")
+                h0, h1 = a // 16, b // 16
+                p = R(tile(), 0, h1 - h0)
+                mm(grp([(p, Zr(u), R("fw", XB + L * t + a + u, XB + L * t + b, 16)) for u in range(16)]))
+                ts(w("ji", h0, h1), p, float(t), A.add)
+                ts(w("ji2", h0, h1), w("ji", h0, h1), 15, A.bitwise_and)
+                copy(w("ju", h0, h1), w("ji2", h0, h1))
+                agat(R("eb", a, b), R("etab"), w("ju", h0, h1))
+                links(R("au", a, b), tab, w("su", h0, h1))
                 for k in range(16):
                     ts(R("mask", 16 * a + k, 16 * b, 16), R("eb", a, b), float(k), A.is_equal)
-            agat(R("ob"), R("otab"), w("ju"))
+                agat(R("ob", a, b), R("otab"), w("ju", h0, h1))
             act(R("pen"), R("eb"), F.Identity, -4096.0, 8388608.0)
 
         def pick(c, buf, off):
@@ -397,15 +402,8 @@ def plan():
                 o, i_ = R("kmin", h0 + h, h0 + h + 1), R(p, h, n, nh)
                 add("V", "red", (o, i_), [i_], [o], vc(16))
             ts(w("ki2", h0, h1), w("kmin", h0, h1), 15, A.bitwise_and)
-            p = tile()
-            if KB == "P":
-                copy(w("kb", h0, h1), w("ki2", h0, h1))
-                mm([(R(p, u, n, 16), Bm("mB", u), w("kb", h0, h1), True, True) for u in range(16)])
-            else:
-                gat("gtt", R("kx", a, b), R("ki2", h0 & 8, h1), w("hoff", h0, h1), R("rmb", 0, n), A.mult)
-                mm([(R(p, 0, n), O, R("kx", a, b), True, True)])
-            ts(R(p, 0, n), R(p, 0, n), icol, A.is_equal)
-            tt(R("seln", a, b), R(p, 0, n), R("n16", a, b), A.mult)
+            copy(w("ku", h0, h1), w("ki2", h0, h1))
+            gat("gtt", R("seln", a, b), R("rm"), w("ku", h0, h1), R("n16", a, b), A.mult)
             Np = R(tile(), 0, nh)
             mm(grp([(Np, Zr(u), R("seln", a + u, b, 16)) for u in range(16)]))
             tt(w("xo", h0, h1), Np, R("lc", 16 * t + h0, 16 * t + h1), A.min)
@@ -414,7 +412,7 @@ def plan():
             Sp = R(tile(), 0, nh)
             mm(grp([(Sp, Zr(u), R("s2b", a + u, b, 16)) for u in range(16)]))
             ts(w("s2u", h0, h1), Sp, 1.0 / 16, A.mult)
-            act(w("s2w", h0, h1), Sp, F.Identity, 0.0, 1.0 / 16)
+            ts(w("s2w", h0, h1), Sp, 1.0 / 16, A.mult)
             links(R("a2u", a, b), tab, w("s2u", h0, h1))
             agat(R("fs", a, b), R("fw", 0, XB + L * (t + 1)), w("xu", h0, h1))
             Xp = R(tile(), 0, n)
@@ -436,41 +434,36 @@ def plan():
             tt(w("d2"), w("df"), w("c1"), A.mult)
             ts(w("ne"), w("d2"), 0.0, A.is_equal, 4096.0, A.mult)
             tt(w("k1"), w("ne"), w("s2w"), A.add)
-            tt(w("k16"), w("k1"), w("dum"), A.min)
-            tt(w("k32"), w("k1"), w("dum"), A.min)
+            tt(w("k16"), w("ne"), w("s2w"), A.add)
             tt(w(snew), w("d2"), w(sw), A.add)
             if not last:
                 send([(R(snew, 5 * b, 5 * b + 5), R("s%d" % (t + 1), 5 * b, 5 * b + 5), 1 + b) for b in range(3)], "as%d" % (t + 1))
-            act(w("gw"), w("ne"), F.Identity, -4096.0)
+            ts(w("gu"), w("d2"), 0.0, A.is_equal)
+            agat(R("nogo"), R("t01", 0, 2), w("gu"))
+            act(R("go"), R("nogo"), F.Identity, 1.0, -1.0, None if last else R("cnt", 0, 1))
             p = tile()
-            mm([(R(p, u, L, 16), Bm("mB", u), w("k16"), True, True) for u in range(16)])
-            copy(R("kbb"), R(p, 0, L))
-            p = tile()
-            Gp = R(p, 0, L)
-            mm(grp([(Gp, I, R("c2048"))] + [(R(p, u, L, 16), Bm("mB", u), w("gw")) for u in range(16)]))
-            act(R("nogo"), Gp, F.Relu, 0.0, 1.0 / 2048, None if last else R("cnt", 0, 1))
-            p = tile()
-            mm([m for h in range(2) for m in grp([(R(p, L * h, L * h + L), NI, R("c2048")),
-                                                  (R(p, L * h, L * h + L), Bm("mH", 6 + h), R("nogo"))])])
-            tt(R("pk"), R(p, 0, 2 * L), R(pm), A.min)
+            mm(grp([(R(p, 0, 2 * L), I, R(pm))] + [(R(p, L * h, L * h + L), Bm("mH", 4 + h), R("go")) for h in range(2)]))
+            act(R("pk1"), R(p, 0, 2 * L), F.Relu, 2048.0)
+            act(R("pk"), R("pk1"), F.Identity, -2048.0)
             for h in range(NH):
-                ts(R("eq", L * h + 16 * h, L * (h + 1)), R("kbb", 16 * h, L), R("k32", h, h + 1), A.is_equal)
+                ts(R("eq", L * h + 16 * h, L * (h + 1)), R("s2b", 16 * h, L), R("k1", h, h + 1), A.is_equal)
             p = tile()
-            Lp = R(p, 0, L)
-            mm(grp([(Lp, I, R("ones", 0, L))] + [(R(p, 16 * h + 16, L), O, R("eq", L * h + 16 * h + 16, L * (h + 1))) for h in range(8)], last=False))
-            mm(grp([(R(p, 16 * h + 16, L), O, R("eq", L * h + 16 * h + 16, L * (h + 1))) for h in range(8, NH - 1)]
-                   + [(R(p, u, L, 16), Bm("mT", u), R("eq", u, L * NH, L + 16)) for u in range(1, 16)], first=False))
-            act(R("lb"), Lp, F.Identity, -256.0, 256.0)
+            off = [(R(p, 16 * h + 16, L), O, R("eq", L * h + 16 * h + 16, L * (h + 1))) for h in range(NH - 1)]
+            mm(grp(off[:4], last=False))
+            mm(grp(off[4:9], first=False, last=False))
+            mm(grp(off[9:], first=False))
+            act(R("lb", 16, L), R(p, 16, L), F.Identity, 0.0, 256.0)
             Op = R(tile(), 0, NH)
-            mm(grp([(Op, I, w("k16"))] + [(Op, Zr(u), R("lb", u, L, 16)) for u in range(16)]))
+            mm(grp([(Op, I, w("k16"))] + [(Op, Bm("mT", u), R("eq", u, L * NH, L + 16)) for u in range(1, 16)], last=False))
+            mm(grp([(Op, Zr(u), R("lb", u, L, 16)) for u in range(16)], first=False))
             tt(w("of"), Op, w("dum"), A.min)
             copy(w("ou"), w("of"))
             if not last:
                 c0 = lambda n: R(n, 0, 1)
-                act(c0("a1"), c0("cnt"), F.Identity, (L - 15.5) / 32, -1.0 / 32)
+                act(c0("a1"), c0("cnt"), F.Identity, -15.5 / 32, 1.0 / 32)
                 act(c0("a2"), c0("a1"), F.Identity, MAGIC)
                 act(c0("a3"), c0("a2"), F.Identity, 512 * MAGIC, -512.0)
-                act(c0("a4"), c0("cnt"), F.Identity, c0("a3"), -16.0)
+                act(c0("a4"), c0("cnt"), F.Identity, c0("a3"), 16.0)
                 act(w("thr"), w("thx"), F.Identity, c0("a4"))
             else:
                 p = tile()
@@ -702,8 +695,21 @@ def improve(ops, users, rounds, seed):
             if not c and before[o["id"]] is not None and o["rt"] < o["t0"] - 1 and o["eng"] in "VAP":
                 pairs.append((o["id"], before[o["id"]]["id"]))
             o = c[0] if c else before[o["id"]]
-        return end, pairs, res[0]
+        free, fin = {e: 0.0 for e in "VAPGSX"}, {}
+        for x in res[0]:
+            st = max([free[x["eng"]]] + [fin[d] for d in x["dep"]])
+            free[x["eng"]] = st = st + slow[x["id"]]
+            fin[x["id"]] = st + x["lat"] + 80.0
+        return (end + MIX * max(fin.values())) / (1.0 + MIX), pairs, res[0]
 
+    slow = [o["cost"] * (1.0 if o["eng"] not in "VAP" else 1.55 if o["kind"] in ("gcp", "gts", "gtt", "agat", "sct") else 1.25) for o in ops]
+
+    same = {}
+    for o in ops:
+        wr = o["w"][0] if o["w"] else ("", 0)
+        name = "ps" if wr[0][:2] == "ps" else wr[0].split("~")[0].rstrip("0123")
+        same.setdefault((o["tag"].rstrip("L"), o["kind"], name, wr[1] % L if name == "xn" else wr[1], int(o["cost"])), []).append(o["id"])
+    twins = {i: lst for lst in same.values() for i in lst}
     for t in tags:
         BIAS[t] = STAGGER * int(t[1]) if t[1].isdigit() and t[0] != "r" else 0.0
     schedule(ops, users, None, SLACK)
@@ -716,10 +722,9 @@ def improve(ops, users, rounds, seed):
             for _ in range(int(rnd.randint(1, 4))):
                 a, b = now[1][int(rnd.randint(len(now[1])))]
                 d = abs(new[b] - new[a]) + float(rnd.choice([50.0, 500.0, 2000.0]))
-                if rnd.rand() < 0.5:
-                    new[a] += d
-                else:
-                    new[b] -= d
+                x, d = (a, d) if rnd.rand() < 0.5 else (b, -d)
+                for y in (twins[x] if rnd.rand() < 0.6 else [x]):
+                    new[y] += d
         elif move < 0.97:
             t, d = tags[int(rnd.randint(len(tags)))], float(rnd.choice([-1.0, 1.0]) * rnd.choice([300.0, 1000.0, 3000.0]))
             eng = str(rnd.choice(["VAP", "V", "A", "P"]))

@@ -3,67 +3,76 @@ import numpy as np
 from concourse.bass import DstId, RemoteDMATransfer
 from concourse.mybir import AluOpType as A, AxisListType as AX, ActivationFunctionType as F
 
-V, S, L, NH, LB, RO = 4096, 1536, 240, 15, 80, 3
-CH = [(0, 6), (6, 10), (10, 15)]
-MS = [(0, 128), (128, 240)]
-E3, E7 = "AAV", "AAA"
-E4 = "AAVAAAAA"
-SEED, ROUNDS, SLACK, STAGGER = 2, 4000, 120.0, -2000.0
-MIX = 0.7
-PIECE = 32
+V, S, L, NH, LB, HB, RO = 4096, 1536, 240, 15, 80, 5, 3
+ORDER = (2, 1, 0)
+MS = [(80, 240), (0, 80)]
+E3 = ("AAA", "AAA", "AAA")
+E7 = ("AAA", "AAA", "AAA")
+E4 = ("AA", "AA", "AA")
+EC = {"um": "A", "n2": "A", "dup": "G", "s2b": "V", "s2w": "A", "pm0": "A", "sn": "AAAAAAAA"}
+SEED, ROUNDS, HEAT, STAGGER, SHORT = 4, 24000, 400.0, -2000.0, 350.0
+MIX = 1.0
+SLOW = {"": 1.16, "dma": 1.0, "send": 1.0, "land": 1.0, "gcp": 1.49, "gts": 1.49, "gtt": 1.49, "agat": 1.49, "sct": 1.7}
+DEFER = {}
+RUNS = ((2,), (1,), (0,))
+HOLE = "A"
+NW = 160
+PIECE = 40
 XB = 4112
 WIN = XB + RO * L
+TW = S + 1 + L
 CEN = 2047.0
-MAGIC = 12582912.0
 BIGV = 262144.0
+P23 = 8388608.0
 UP = 0.48
 SIGC, SIGB = 128.0, -math.log(31.0)
 
 SCRATCH = {}
 BUF = {}
 POOL = {}
-DUP = ("ju", "eb", "pen", "mask", "n16", "vf", "nogo", "pk", "h", "kmin", "s2u", "bc", "bm", "au", "ob")
+DUP = ("pen", "q2", "mask", "n16", "vf", "nogo", "pk", "h", "kmin", "s2u", "bc", "bm", "au", "oc", "om", "ou")
 
 
 def _sb(name, cols, dt, parts=128):
     names = [name + "~0", name + "~1"] if name in DUP else [name]
-    pool = "small_" + dt if cols <= 16 else name
+    pool = "small_" + dt if cols <= 256 and parts == 128 else name
     for nm in names:
         BUF[nm] = ("sbuf", [parts, cols], dt)
         at = SCRATCH[pool][1][1] if pool in SCRATCH else 0
-        SCRATCH[pool] = ("sbuf", [parts, at + max(cols, 16)], dt)
+        SCRATCH[pool] = ("sbuf", [parts, at + -(-cols // 16) * 16], dt)
         POOL[nm] = (pool, at)
 
 
 for _n, _c, _d in [
-    ("fw", WIN, "bfloat16"), ("snb", WIN, "float32"), ("sni", 256, "int32"), ("sn16", 256, "float16"), ("lmi", S, "int32"), ("memi", S, "int32"),
-    ("comb", S + L, "float32"), ("mem", S + L, "float32"), ("pqi", 2 * L, "int32"),
-    ("ones", 256, "bfloat16"), ("c128", 256, "bfloat16"), ("c2048", L, "bfloat16"), ("c05", L, "bfloat16"),
+    ("fw", WIN, "bfloat16"), ("snb", WIN, "float32"), ("sni", 257, "int32"), ("sn16", 256, "float16"), ("lmi", S, "int32"), ("memi", S, "int32"),
+    ("comb", TW, "float32"), ("mem0", S, "float32"), ("mem1", TW, "float32"), ("mem2", TW, "float32"), ("pqi", 2 * L, "int32"),
+    ("ones", 160, "bfloat16"), ("rm4", 16, "float32"), ("c128", 160, "bfloat16"), ("c2048", LB, "bfloat16"), ("cK", LB, "bfloat16"),
+    ("c1281", 160, "float16"), ("c2047", 160, "float16"),
     ("mI", 128, "bfloat16"), ("mN", 128, "bfloat16"), ("mBIG", 128, "bfloat16"), ("mPB", 128, "bfloat16"),
     ("mO1", 128, "bfloat16"), ("mO", 128, "bfloat16"), ("mZ", 144, "bfloat16"), ("mZ2", 144, "bfloat16"), ("mY", 208, "bfloat16"),
     ("mYP", 208, "bfloat16"), ("mY8", 208, "bfloat16"), ("mYN", 208, "bfloat16"), ("mD0", 256, "bfloat16"), ("mD", 2048, "bfloat16"), ("mR", 17 * 64, "bfloat16"),
-    ("mJ", 128, "bfloat16"), ("mH", 1024, "bfloat16"), ("hm", 16, "float32"), ("sc", 16, "float32"), ("par", 16, "float32"), ("ob", L, "bfloat16"),
-    ("um0", 2 * L, "float16"), ("um1", 2 * L, "float16"), ("um2", 2 * L, "float16"), ("mB", 2048, "bfloat16"), ("mB4", 2048, "bfloat16"), ("mT", 2048, "bfloat16"),
-    ("io1", 16, "int32"), ("ei", 16, "int32"), ("oi", 16, "int32"), ("etab", 16, "bfloat16"), ("otab", 16, "bfloat16"),
-    ("ef", 16, "float32"), ("rm", 16, "float32"), ("mZ4", 144, "bfloat16"), ("ku", 16, "uint16"), ("gu", 16, "uint16"), ("t01", 16, "bfloat16"), ("go", L, "bfloat16"),
-    ("pk1", 2 * L, "float32"), ("ne", 16, "float32"),
-    ("h16", 16, "float32"), ("lw", 16, "float32"), ("dum", 16, "float32"), ("dums", 16, "float32"), ("lc", 48, "float32"),
-    ("kc", L, "bfloat16"), ("thw", 16, "float32"), ("thx", 16, "float32"), ("thr", 16, "float32"),
-    ("ji", 16, "int32"), ("ji2", 16, "int32"), ("ju", 16, "uint16"), ("su", 16, "uint16"),
-    ("eb", L, "bfloat16"), ("pen", L, "bfloat16"), ("mask", 16 * L, "bfloat16"), ("au", L, "uint16"), ("a2u", L, "uint16"),
+    ("mJ", 128, "bfloat16"), ("mH", 768, "bfloat16"), ("mB", 2048, "bfloat16"), ("mT1", 128, "bfloat16"), ("mT", 128, "bfloat16"),
+    ("hm", 16, "float32"), ("sc", 16, "float32"), ("par", 16, "float32"),
+    ("um0", 2 * L, "float16"), ("um1", 2 * L, "float16"), ("um2", 2 * L, "float16"),
+    ("io1", 16, "int32"), ("ei", 16, "int32"), ("oi", 16, "int32"), ("ef", 16, "float32"), ("rm", 16, "float32"),
+    ("iw", L, "int32"), ("iw2", L, "int32"), ("iw3", NW, "int32"), ("tb", L, "float32"), ("e0", NW, "bfloat16"), ("e15", NW, "bfloat16"), ("ds", NW, "bfloat16"),
+    ("cx", RO * NW, "bfloat16"), ("co", NW, "bfloat16"), ("nn", L, "float16"), ("ocr", L, "float32"), ("omr", L, "float32"),
+    ("mI32", 128, "float32"), ("mP", 128, "bfloat16"), ("bq", 16, "float32"), ("bp", 16, "float32"), ("cu", 16, "float32"),
+    ("ku", 24, "uint16"), ("gu", 24, "uint16"), ("su", 24, "uint16"), ("xu", 24, "uint16"), ("s2u", 24, "uint16"), ("ou", 24, "uint16"),
+    ("t01", 16, "bfloat16"), ("junk", L, "bfloat16"), ("pk1", 2 * L, "float32"),
+    ("kc", LB, "bfloat16"), ("thx", 16, "float32"), ("thr", 16, "float32"),
+    ("q16", L, "float16"), ("q2", L, "bfloat16"), ("pen", L, "bfloat16"), ("mask", 16 * L, "bfloat16"), ("au", L, "uint16"), ("a2u", L, "uint16"),
     ("pu", L, "float16"), ("rr", 2 * L, "bfloat16"), ("n16", 2 * L, "float16"), ("nu", L, "uint16"),
-    ("vf", L, "bfloat16"), ("kmin", 16, "int32"), ("ki2", 16, "int32"), ("kb", 16, "bfloat16"),
-    ("seln", L, "float16"), ("xo", 16, "float32"), ("xu", 16, "uint16"), ("s2b", L, "float16"),
-    ("s2u", 16, "uint16"), ("fs", L, "bfloat16"), ("xy", L, "float32"), ("xn", 2 * L, "bfloat16"),
-    ("s2w", 16, "float32"), ("c1", 16, "float32"), ("df", 16, "float32"), ("d2", 16, "float32"), ("gw", 16, "bfloat16"),
+    ("vf", L, "bfloat16"), ("kmin", 16, "int32"), ("ki2", 16, "int32"),
+    ("seln", L, "float16"), ("xo", L, "float32"), ("s2b", L, "float16"), ("s2x", L, "float16"), ("ox", L, "float32"),
+    ("fs", L, "bfloat16"), ("xy", L, "float16"), ("xn", 2 * L, "bfloat16"),
+    ("s2w", 16, "float32"), ("cs", L, "bfloat16"), ("c1", 16, "float32"), ("df", 16, "float32"), ("d2", 16, "float32"), ("go", 16, "float32"),
     ("sn1", 16, "float16"), ("sn2", 16, "float16"), ("sn3", 16, "float16"),
-    ("k0", 16, "float32"), ("k1", 16, "float32"), ("k32", 16, "float32"), ("k16", 16, "float16"),
-    ("eq", NH * L, "bfloat16"), ("lb", L, "bfloat16"), ("of", 16, "float32"), ("ou", 16, "uint16"),
-    ("nogo", L, "bfloat16"), ("cnt", 4, "float32"), ("a1", 4, "float32"), ("a2", 4, "float32"), ("a3", 4, "float32"), ("a4", 4, "float32"),
+    ("eq", NH * NW, "bfloat16"), ("nogo", L, "bfloat16"), ("cnt", 4, "float32"), ("a1", 4, "float16"), ("a4", 4, "float32"),
     ("oc", L, "float32"), ("om", L, "float32"), ("bc", L, "float32"), ("bm", L, "float32"),
-    ("r2", 4 * L, "bfloat16"), ("pk", 2 * L, "float32"),
+    ("r2", 2 * L, "bfloat16"), ("r3", 2 * L, "bfloat16"), ("pk", 2 * L, "float32"),
     ("pm0", 2 * L, "float16"), ("pm1", 2 * L, "float16"), ("pm2", 2 * L, "float16"),
-    ("po0", 2 * L, "float16"), ("po1", 2 * L, "float16"), ("pf", 2 * L, "float32"), ("pf2", 2 * L, "float32"),
+    ("po0", 2 * L, "float16"), ("po1", 2 * L, "float16"), ("pf", 2 * L, "float32"),
     ("s0", 16, "float16"), ("s1", 16, "float16"), ("s2", 16, "float16"),
     ("v0", L, "float16"), ("v1", L, "float16"), ("v2", L, "float16"),
     ("xf", L, "float32"), ("sf", L, "float32"),
@@ -77,19 +86,18 @@ _sb("z24", 2 * 144 + 128, "bfloat16", 24)
 for _i in range(8):
     SCRATCH["bank%d" % _i] = ("psum", [128, 512], "float32")
 
-NDMA = 20
-SEMAPHORES = (["eV", "eA", "eP", "eG", "sent", "snl"] + ["d%d" % _i for _i in range(NDMA)]
-              + ["%s%d_%d" % (_a, _t, _b) for _a in ("ax", "ap") for _t in (1, 2) for _b in range(3)]
-              + ["as1", "as2", "av1", "av2"])
+NDMA = 24
+SEMAPHORES = (["eV", "eA", "eP", "eG", "sent", "rw", "pq"] + ["d%d" % _i for _i in range(NDMA)]
+              + ["%s%d_%d" % (_a, _t, _b) for _a in ("ax", "as", "ap") for _t in (1, 2) for _b in range(3)] + ["av1", "av2"])
 SIZE = {"float32": 4, "int32": 4, "bfloat16": 2, "float16": 2, "uint16": 2}
-CYC, PEC, HOP, GAT, SCT = 0.93, 0.47, 170.0, 1.56, 3.8
+CYC, PEC, HOP, GAT, SCT = 1.04, 0.525, 150.0, 1.6, 3.8
 PAR, TAG = [0], ["init"]
-BIAS = {}
+ENG = "VAPGSX"
 
 
 def R(name, lo=0, hi=None, step=1, p0=0, p1=None, pstep=1):
     if name in DUP:
-        name = "%s~%d" % (name, PAR[0])
+        name = "%s~%d" % (name, PAR[0] % 2)
     shp = [128, 512] if name[:2] == "ps" else BUF[name][1]
     return (name, lo, shp[1] if hi is None else hi, step, p0, shp[0] if p1 is None else p1, pstep)
 
@@ -108,8 +116,13 @@ def plan():
 
     def add(eng, kind, args, reads, writes, cost, lat=0.0, after=None):
         ops.append({"eng": eng, "kind": kind, "args": args, "r": reads, "w": writes, "cost": cost, "lat": lat, "after": after, "id": len(ops),
-                    "tag": TAG[0]})
+                    "tag": TAG[0], "vis": PAR[0], "alt": []})
         return ops[-1]
+
+    def join(n):
+        sub = ops[-n:]
+        del ops[-n:]
+        add(sub[0]["eng"], "many", sub, [r for s in sub for r in s["r"]], [r for s in sub for r in s["w"]], sum(s["cost"] for s in sub))
 
     def aps(*xs):
         return [x for x in xs if isinstance(x, tuple)]
@@ -127,20 +140,56 @@ def plan():
         ps = in0[0][:2] == "ps" or in1[0][:2] == "ps"
         add("V", "tt", (out, in0, in1, op), [in0, in1], [out], vc(cnt(out) * (1 if ps else 2)))
 
+    def scan(out, d0, d1, init, op0, op1):
+        add("V", "scan", (out, d0, d1, init, op0, op1), [d0, d1], [out], vc(cnt(out) * (0.5 if two(out, d0, d1) else 1)))
+
     def gat(kind, out, win, off, *rest):
         add("V", kind, (out, win, off) + rest, aps(win, off, *rest), [out], 50 + GAT * CYC * cnt(out))
 
     def mset(out, val):
         add("V", "mset", (out, val), [], [out], vc(cnt(out) * (0.5 if two(out) else 1)))
 
-    def act(out, in_, f, bias=0.0, scale=1.0, acc=None):
+    def other():
+        o = ops.pop()
+        ops[-1]["alt"].append({k: o[k] for k in ("eng", "kind", "args", "cost")})
+
+    def act(out, in_, f=F.Identity, bias=0.0, scale=1.0, acc=None):
         add("A", "act", (out, in_, f, bias, scale, acc), aps(in_, bias, scale), aps(out, acc), vc(cnt(out)) + 30)
+        if f == F.Identity and acc is None:
+            ts(out, in_, scale, A.mult, bias, A.add)
+            other()
+        elif f == F.Relu and scale == 1.0:
+            ts(out, in_, bias, A.add, 0.0, A.max)
+            other()
 
     def agat(out, win, off):
         add("A", "agat", (out, win, off), [win, off], [out], 65 + GAT * CYC * cnt(out))
+        gat("gcp", out, win, off)
+        other()
+
+    def offs(out, in_, bias=0.0, scale=1.0):
+        ts(out, in_, scale, A.mult, bias, A.add)
+        add("A", "act", (out, in_, F.Identity, bias, scale, None), [], [], vc(cnt(out)) + 30)
+        other()
+
+    def pool(kind, out, in_, *args):
+        add("G", kind, (out, in_) + args, aps(in_), [out], 170 + 2 * CYC * cnt(out))
+
+    def keep(out, in_):
+        pool("sel", out, in_, [[0, cnt(out)]], A.is_equal, 0, 0, 0.0)
+
+    def move(eng, out, in_, bias=None):
+        if eng == "G":
+            keep(out, in_)
+            act(out, in_)
+            ops[-2]["alt"] += ops[-1]["alt"]
+            other()
+        else:
+            act(out, in_, F.Identity, 0.0 if bias is None else bias)
 
     def mm(lst):
-        add("P", "mm", lst, [m[1] for m in lst] + [m[2] for m in lst], [m[0] for m in lst], sum(max(64, cnt(m[2])) for m in lst) * PEC)
+        add("P", "mm", lst, [m[1] for m in lst] + [m[2] for m in lst], [m[0] for m in lst],
+            sum(max(64, cnt(m[2])) * (1 if two(m[2]) else 4) for m in lst) * PEC)
 
     def grp(lst, first=True, last=True):
         return [(o, l, r, first and i == 0, last and i == len(lst) - 1) for i, (o, l, r) in enumerate(lst)]
@@ -151,10 +200,15 @@ def plan():
         nt[0] += 1
         return "ps%d" % nt[0]
 
-    def dma(q, out, in_, nbytes, sem=None):
+    sofar = [0]
+
+    def dma(q, out, in_, nbytes, sem=None, load=False):
         if sem is None:
             sem = "d%d" % nd[0]
             nd[0] += 1
+        if load:
+            sofar[0] += nbytes
+            nbytes = sofar[0]
         rd = [in_] if in_[0] in BUF else []
         wr = [out] if out[0] in BUF else []
         return add(q, "dma", (out, in_, sem), rd, wr, 100.0, 1800.0 + nbytes / 200.0)
@@ -166,51 +220,79 @@ def plan():
     Zr = lambda u, m="mZ": R(m, 15 - u, 143 - u)
     Bm = lambda m, u: R(m, 128 * u, 128 * u + 128)
     I, NI, BIG, PB, O = R("mI"), R("mN"), R("mBIG"), R("mPB"), R("mO")
-    w = lambda n, a=0, b=NH: R(n, a, b)
+    run = lambda b: (b, b + 1) if isinstance(b, int) else (b[0], b[-1] + 1)
+    w = lambda n, b=(0, 1, 2): R(n, HB * run(b)[0], HB * run(b)[1])
+    wu = lambda n, b: R(n, 6 * run(b)[0], 6 * run(b)[0] + HB * (run(b)[1] - run(b)[0]))
+    ln = lambda n, b, step=1, at=0: R(n, LB * run(b)[0] + at, LB * run(b)[1], step)
+    end = lambda n, b: ln(n, b, 16, 15)
+    st2 = lambda n, b, h=None: R(n, 2 * LB * run(b)[0], 2 * LB * run(b)[1]) if h is None else R(n, LB * (2 * b + h), LB * (2 * b + h + 1))
+    half = lambda m, h, lo, hi, step=1: R(m, lo, hi, step, 64 * h, 64 * h + 64)
+    own = lambda m, h, step=1: half(m, h, 64 * h, 64 * h + 64, step)
+    col = lambda m, c: R(m, c, c + 1)
 
-    dma("S", R("fw", XB, XB + L), ("lx",), 61440)
+    dma("S", R("fw", XB, XB + L), ("lx",), 61440, load=True)
     for i, n in enumerate(("ls", "lv", "th")):
-        dma("A", R("rwi", p0=8 * i, p1=8 * i + 8), (n,), 90000, "d19")
-    dma("S", R("lmi", 0, 768), ("lm", 0, 768), 480000)
-    dma("S", R("lmi", 768, S), ("lm", 768, S), 880000)
+        dma("A", R("rwi", p0=8 * i, p1=8 * i + 8), (n,), 90000, "rw")
+    LM = [(0, 512), (512, 1024), (1024, S)]
+    dma("S", R("sni", 0, 256), ("sn",), 131072, load=True)
+    for a, b in LM:
+        dma("S", R("lmi", a, b), ("lm", a, b), 512 * (b - a), load=True)
     for h in range(2):
-        dma("S", R("pqi", L * h, L * h + L, p0=64 * h, p1=64 * h + 64), ("lp", 0, L, 64 * h), 1120000, "d18")
-        dma("S", R("pqi", L * h, L * h + L, p0=64 - 64 * h, p1=128 - 64 * h), ("lq", 0, L, 64 * h), 1120000, "d18")
-    dma("S", R("sni"), ("sn",), 1250000, "snl")
-    dma("S", R("fw", 0, V), ("feat",), 2300000)
+        dma("S", half("pqi", h, L * h, L * h + L), ("lp", 0, L, 64 * h), 61440, "pq", load=True)
+        dma("S", half("pqi", 1 - h, L * h, L * h + L), ("lq", 0, L, 64 * h), 61440, "pq", load=True)
+    for o in ops[-4:]:
+        o["lat"] = ops[-1]["lat"]
+    dma("S", R("fw", 0, V), ("feat",), 1048576, load=True)
 
-
-    def pool(kind, out, in_, *args):
-        add("G", kind, (out, in_) + args, aps(in_), [out], 170 + 2 * CYC * cnt(out))
     mset(R("ones"), 1.0)
     pool("iota", R("io1"), None, [[-1, 16]], 128, 1)
-    pool("sel", R("mO1"), R("ones", 0, 128), [[-16, 8], [0, 16]], A.is_ge, 0, 1)
-    pool("sel", O, R("mO1"), [[16, 8], [0, 16]], A.is_ge, 15, -1)
+    pool("sel", R("mO1"), R("ones", 0, 128), [[-16, 8], [0, 16]], A.is_ge, 0, 1, 0.0)
+    pool("sel", O, R("mO1"), [[16, 8], [0, 16]], A.is_ge, 15, -1, 0.0)
+    pool("sel", I, R("ones", 0, 128), [[-1, 128]], A.is_equal, 0, 1, 0.0)
     for i in range(2):
-        pool("sel", R("z24", 144 * i, 144 * i + 143), R("ones", 0, 143, p1=24), [[-1, 143]], A.is_equal, 15 - 256 * i, 16)
-    pool("sel", I, R("ones", 0, 128), [[-1, 128]], A.is_equal, 0, 1)
-    pool("iota", R("h16"), None, [[16, 16]], 0, 0)
-    pool("sel", R("z24", 288, 416), R("ones", 0, 128, p1=24), [[-1, 8], [0, 16]], A.is_equal, -8, 1)
-    for a, b in CH:
-        pool("iota", R("kc", 16 * a, 16 * b), None, [[1, 16], [0, b - a]], 0, 0)
+        pool("sel", R("z24", 144 * i, 144 * i + 143), R("ones", 0, 143, p1=24), [[-1, 143]], A.is_equal, 15 - 256 * i, 16, 0.0)
+    pool("sel", R("z24", 288, 416), R("ones", 0, 128, p1=24), [[-1, 8], [0, 16]], A.is_equal, -8, 1, 0.0)
+    pool("iota", R("kc"), None, [[1, 16], [0, HB]], 0, 0)
+    pool("iota", R("iw"), None, [[-16, NH], [-8193, 16]], 8192 * 128 + 255, 8192)
     pool("iota", R("snb", V, WIN), None, [[0, WIN - V]], 0, 0)
+    pool("iota", R("t01", 0, 2), None, [[-1, 2]], 1, 0)
+    pool("sel", R("mT1"), O, [[1, 128]], A.is_gt, 0, -1, 0.0)
+    pool("sel", R("mT"), R("mT1"), [[1, 128]], A.not_equal, 0, -1, -1.0)
     mset(R("mZ"), 0.0)
     copy(R("mZ", 15, 143, 16), R("mO", 0, 128, 16))
     mset(R("fw", V, XB), 1024.0)
+    mset(R("c1281"), -1281.0)
     ts(R("ei"), R("io1"), 15, A.bitwise_and)
     ts(R("oi"), R("io1"), 1, A.bitwise_and)
-    copy(R("etab"), R("ei"))
-    copy(R("ef"), R("ei"))
-    ts(R("otab"), R("oi"), 4096.0, A.mult, -2048.0, A.add)
     ts(R("rm"), R("ei"), 0.0, A.is_equal)
-    icol = R("ef", 0, 1)
+    ts(R("rm4"), R("ei"), 0.0, A.is_equal, 4096.0, A.mult)
+    for u in range(16):
+        act(Bm("mB", u), O, F.Identity, 0.0, col("rm4", u))
+    act(R("bq", 0, RO), R("ei", 0, RO), F.Identity, 20488.5)
+    act(R("bp", 0, RO), R("ei", 0, RO), F.Identity, -4096.0, P23)
+    ts(col("cu", 0), col("ei", 0), 15.0, A.not_equal, 2048.0, A.mult)
+    act(col("cu", 1), col("cu", 0), F.Identity, CEN, -1.0)
+    mset(R("cs"), P23)
+    mset(R("cs", 15, L, 16), 0.0)
+    ts(R("iw2"), R("iw"), 15 * 8192 + 255, A.bitwise_and)
+    act(R("tb"), R("iw2"), F.Identity, 256.0, -1.0)
+    nw = LB * max(len(b) for b in RUNS)
+    ts(R("iw3", 0, nw), R("iw2", 0, nw), 13, A.logical_shift_right)
+    ts(R("e0", 0, nw), R("iw3", 0, nw), 0.0, A.is_equal, 4096.0, A.mult)
+    ts(R("e15", 0, nw), R("iw3", 0, nw), 15.0, A.is_equal, -2048.0, A.mult)
+    tt(R("ds", 0, nw), R("e0", 0, nw), R("e15", 0, nw), A.add)
+    XC = [XB - 1 - CEN + L * t for t in range(RO)]
+    for t in range(RO):
+        act(R("cx", NW * t, NW * t + nw), R("e0", 0, nw), F.Identity, 4096.0, -(XC[t] + 4096.0) / 4096)
+    act(R("co", 0, nw), R("e0", 0, nw), F.Identity, 12288.0, (4096.0 - S - 12288.0) / 4096)
+    if HOLE != "V":
+        act(R("mI32"), I)
+        act(R("mP"), I, F.Identity, 0.0, -2 * P23)
     act(NI, I, F.Identity, 0.0, -1.0)
-    act(R("c128"), R("ones"), F.Identity, 0.0, 128.0)
-    act(R("c2048"), R("ones", 0, L), F.Identity, 0.0, 2048.0)
+    for n, c in (("c128", 128.0), ("c2048", 2048.0), ("cK", 255 * P23), ("c2047", CEN)):
+        mset(R(n), c)
     act(BIG, I, F.Identity, 0.0, -BIGV)
     act(PB, I, F.Identity, 0.0, BIGV)
-    half = lambda m, h, lo, hi, step=1: R(m, lo, hi, step, 64 * h, 64 * h + 64)
-    own = lambda m, h, step=1: half(m, h, 64 * h, 64 * h + 64, step)
     mset(R("mZ2"), 0.0)
     mset(R("mY"), 0.0)
     mset(R("sc"), 1.0)
@@ -218,258 +300,239 @@ def plan():
         copy(half("mZ2", h, 79 - 64 * h, 143 - 64 * h, 16), own("mO", h, 16))
         copy(half("mY", h, 78 + h, 142 + h, 16), own("mO", h, 16))
         tt(half("sc", h, 8 * h, 8 * h + 8), half("rm", h, 0, 16, 2), half("rm", h, 1, 16, 2), A.add)
-    ts(R("par", 0, 1), R("oi", 0, 1), 0.0, A.is_equal)
-    copy(R("par", 1, 2), R("oi", 0, 1))
+    ts(col("par", 0), col("oi", 0), 0.0, A.is_equal)
+    copy(col("par", 1), col("oi", 0))
     for h in range(2):
         for kk in range(2):
             act(half("mD0", h, 128 * h + 64 * kk, 128 * h + 64 * kk + 64), own("mO", h), F.Identity, 0.0, half("par", h, kk, kk + 1))
             act(half("mD0", 1 - h, 128 * h + 64 * kk, 128 * h + 64 * kk + 64), own("mN", 1 - h), F.Identity)
         for kp in range(8):
-            act(Bm("mD", 8 * h + kp), R("mD0", 128 * h, 128 * h + 128), F.Identity, 0.0, R("sc", 8 * h + kp, 8 * h + kp + 1))
-    if "A" in E3:
+            act(Bm("mD", 8 * h + kp), R("mD0", 128 * h, 128 * h + 128), F.Identity, 0.0, col("sc", 8 * h + kp))
+    if "AAA" in E3:
         act(R("mYP"), R("mY"), F.Identity, 0.0, BIGV)
-    if "V" in E3:
+    if "VVV" in E3:
         act(R("mY8"), R("mY"), F.Identity, 0.0, 8192.0)
     act(R("mYN"), R("mY"), F.Identity, 0.0, -BIGV)
-    late_pool = []
     for h in range(2):
         act(half("mR", h, 0, 64), own("mBIG", h), F.Identity)
-    for kp in range(8):
-        late_pool.append((R("mR", 128 * kp + 64, 128 * kp + 128), R("mYN", 78 - 2 * kp, 142 - 2 * kp)))
-        late_pool.append((R("mR", 128 * kp + 128, 128 * kp + 192), R("mR", 0, 64)))
     for h in range(2):
-        act(R("mJ", 64 * h, 64 * h + 64), R("mR", 0, 64), F.Identity)
+        act(R("mJ", 64 * h, 64 * h + 64), R("mR", 0, 64), F.Identity, 0.0, 8192.0 / BIGV)
     mset(R("hm", 0, 2), 0.0)
     for h in range(2):
         mset(half("hm", h, h, h + 1), 1.0)
     for h in range(2):
-        act(Bm("mH", h), I, F.Identity, 0.0, R("hm", h, h + 1))
-        act(Bm("mH", 2 + h), BIG, F.Identity, 0.0, R("hm", h, h + 1))
-        act(Bm("mH", 4 + h), R("mJ"), F.Identity, 0.0, R("hm", h, h + 1))
-    act(R("c05"), R("ones", 0, L), F.Identity, 0.0, 0.5)
-    act(R("lw"), R("h16"), F.Identity, icol)
-    act(R("dum"), R("lw"), F.Identity, float(S))
-    for t in range(RO):
-        act(R("lc", 16 * t, 16 * t + 16), R("lw"), F.Identity, XB + L * t - CEN)
-    pool("iota", R("t01", 0, 2), None, [[1, 2]], 0, 0)
-    act(R("mZ4"), R("mZ"), F.Identity, 0.0, 4096.0)
-    for u in range(16):
-        pool("sel", Bm("mB", u), O, [[-16, 8], [0, 16]], A.is_equal, -u, 1)
-    for i in range(0, 2048, 512):
-        act(R("mB4", i, i + 512), R("mB", i, i + 512), F.Identity, 0.0, 4096.0)
-    for u in range(1, 16):
-        pool("sel", Bm("mT", u), Zr(u, "mZ4"), [[16, 8], [0, 16]], A.is_gt, u, -1)
-    for o, i_ in late_pool:
-        pool("sel", o, i_, [[0, 64]], A.is_equal, 0, 0)
-    mset(R("lb", 0, 16), 0.0)
+        act(Bm("mH", h), I, F.Identity, 0.0, col("hm", h))
+        act(Bm("mH", 2 + h), BIG, F.Identity, 0.0, col("hm", h))
+        act(Bm("mH", 4 + h), R("mJ"), F.Identity, 0.0, col("hm", h))
+    for kp in range(8):
+        keep(R("mR", 128 * kp + 64, 128 * kp + 128), R("mYN", 78 - 2 * kp, 142 - 2 * kp))
+        keep(R("mR", 128 * kp + 128, 128 * kp + 192), R("mR", 0, 64))
 
-    ts(R("rw"), R("rwi"), -CEN, A.add)
+    act(R("rw"), R("rwi"), F.Identity, -CEN)
     p = tile()
     mm(grp([(R(p, 0, NH), R("z24", 15 - u, 143 - u), R("rw", u, L, 16)) for u in range(16)]))
-    ts(w("s0"), R(p, 0, NH), CEN, A.add)
+    act(w("s0"), R(p, 0, NH), F.Identity, col("cu", 1))
     p = tile()
     mm(grp([(R(p, 0, NH), R("z24", 159 - u, 287 - u), R("rw", u, L, 16)) for u in range(16)]))
     act(w("thr"), R(p, 0, NH), F.Identity, 16 * CEN, 16.0)
-    act(w("thx"), R(p, 0, NH), F.Identity, 16 * CEN, 16.0)
+    act(w("thx"), R(p, 0, NH), F.Identity, 16 * CEN + 512 * 1536.0, 16.0)
     p = tile()
     mm(grp([(R(p, 0, L), R("z24", 288, 416), R("rw"))]))
-    copy(R("v0"), R(p, 0, L))
-    copy(R("sn16"), R("sni"))
+    act(R("v0"), R(p, 0, L))
+    copy(R("sn16"), R("sni", 0, 256))
     for i in range(0, 16, 2):
         p = tile()
         mm([(R(p, 256 * j, 256 * j + 256), Bm("mB", i + j), R("sn16"), True, True) for j in range(2)])
-        act(R("snb", 256 * i, 256 * i + 512), R(p), F.Identity)
+        act(R("snb", 256 * i, 256 * i + 512), R(p), F.Identity, 0.0, 1.0 / 4096)
     for t in (1, 2):
-        send([(R("v0", LB * b, LB * b + LB), R("v%d" % t, LB * b, LB * b + LB), t * (1 + b)) for b in range(3)], "av%d" % t)
-    for a, b in ((0, 768), (768, S)):
+        send([(ln("v0", b), ln("v%d" % t, b), t * (1 + b)) for b in range(3)], "av%d" % t)
+    for a, b in LM:
         ts(R("memi", a, b), R("lmi", a, b), V - 1, A.bitwise_and)
-        ts(R("mem", a, b), R("memi", a, b), -CEN, A.add)
-    ts(R("pm0"), R("pqi"), -CEN, A.add)
-    copy(R("um0"), R("pm0"))
-    for a, b in ((0, 512), (512, 1024), (1024, S)):
-        copy(R("comb", a, b), R("lmi", a, b))
+        act(R("mem0", a, b), R("memi", a, b), F.Identity, -CEN)
+    for b in ORDER:
+        for h in range(2):
+            move(EC["pm0"], st2("pm0", b, h), R("pqi", L * h + LB * b, L * h + LB * b + LB), -CEN)
+        move("G", st2("um0", b), st2("pm0", b))
+    for a, b in LM:
+        keep(R("comb", a, b), R("lmi", a, b))
+        keep(R("mem1", a, b), R("mem0", a, b))
 
-    def ksplit(n):
-        nb = -(-16 // (512 // n))
-        return [(16 * i // nb, 16 * (i + 1) // nb) for i in range(nb)]
+    KS = [(0, 6), (6, 11), (11, 16)]
 
     def links(out, tab, off):
         gat("gts", out, tab, off, -2047.5, 1.0 / 4096, A.add, A.mult)
+        add("A", "agact", (out, tab, off, F.Identity, -2047.5 / 4096, 1.0 / 4096), [], [], 65 + GAT * CYC * cnt(out))
+        other()
 
-    def diffs(a, n, src, lhs, sub, dst, f, bias, scale):
-        for k0, k1 in ksplit(n):
+    def pairs(b, u, dst, engs):
+        for (j0, j1), eng in zip(KS, engs):
             bk = tile()
-            lst = []
-            for k in range(k0, k1):
-                o = R(bk, (k - k0) * n, (k - k0 + 1) * n)
-                lst += grp([(o, lhs, R(src, 16 * a + k, 16 * (a + n), 16))] + ([(o, NI, sub)] if f else []))
-            mm(lst)
-            if f:
-                act(R(dst, 16 * a + k0 * n, 16 * a + k1 * n), R(bk, 0, (k1 - k0) * n), f, bias, scale)
-            else:
-                for k in range(k0, k1):
-                    tt(R(dst, 16 * a + k * n, 16 * a + (k + 1) * n), R(bk, (k - k0) * n, (k - k0 + 1) * n), sub, A.is_equal)
-
-    def pairs(a, n, u, dst, eng):
-        for j0, j1 in ksplit(n):
-            bk = tile()
-            mm([(R(bk, (j - j0) * n, (j - j0 + 1) * n), Bm("mD", j), R(u, L * (j // 8) + a, L * (j // 8) + a + n), True, True) for j in range(j0, j1)])
-            o, i_ = R(dst, 16 * a + j0 * n, 16 * a + j1 * n), R(bk, 0, (j1 - j0) * n)
+            mm([(R(bk, (j - j0) * LB, (j - j0 + 1) * LB), Bm("mD", j), st2(u, b, j // 8), True, True) for j in range(j0, j1)])
+            o, i_ = R(dst, LB * (16 * b + j0), LB * (16 * b + j1)), R(bk, 0, (j1 - j0) * LB)
             if eng == "A":
                 act(o, i_, F.Sigmoid, SIGB, SIGC)
+                ts(o, i_, 0.0, A.is_equal, 1.0 / 32, A.mult)
+                other()
             else:
                 ts(o, i_, 0.0, A.is_equal)
 
-    def visit(t):
-        PAR[0] = t % 2
+    def visit(t, before):
+        PAR[0] = t
         last = t == RO - 1
         X = lambda a, b: R("fw", XB + L * t + a, XB + L * t + b)
-        pm, sw, vw = "pm%d" % t, "s%d" % t, "v%d" % t
+        pm, um, sw, vw, snew = "pm%d" % t, "um%d" % t, "s%d" % t, "v%d" % t, "sn%d" % (t + 1)
         tab = R("lmi") if t == 0 else R("comb", 0, S)
+        mem = R("mem%d" % t, 0, S)
 
-        def front():
-            copy(w("su"), w(sw))
-            for i, (a, b) in enumerate(MS):
-                TAG[0] = "f%d" % i + ("L" if last else "")
-                h0, h1 = a // 16, b // 16
-                p = R(tile(), 0, h1 - h0)
-                mm(grp([(p, Zr(u), R("fw", XB + L * t + a + u, XB + L * t + b, 16)) for u in range(16)]))
-                ts(w("ji", h0, h1), p, float(t), A.add)
-                ts(w("ji2", h0, h1), w("ji", h0, h1), 15, A.bitwise_and)
-                copy(w("ju", h0, h1), w("ji2", h0, h1))
-                agat(R("eb", a, b), R("etab"), w("ju", h0, h1))
-                links(R("au", a, b), tab, w("su", h0, h1))
-                for k in range(16):
-                    ts(R("mask", 16 * a + k, 16 * b, 16), R("eb", a, b), float(k), A.is_equal)
-                agat(R("ob", a, b), R("otab"), w("ju", h0, h1))
-            act(R("pen"), R("eb"), F.Identity, -4096.0, 8388608.0)
-
-        def pick(c, buf, off):
-            for a in range(16 * CH[c][0], 16 * CH[c][1], PIECE):
-                b = min(a + PIECE, 16 * CH[c][1])
-                gat("gtt", R(buf, 16 * a, 16 * b), R("mem", 0, S), R(off, a, b), R("mask", 16 * a, 16 * b), A.mult)
-
-        def sample(c):
-            h0, h1 = CH[c]
-            a, b = 16 * h0, 16 * h1
+        def front(a, b):
             n = b - a
-            sg = lambda k: R("sg", 16 * a + k * n, 16 * a + (k + 1) * n)
-            um = "um%d" % t
+            p = R(tile(), 0, n)
+            mm(grp([(p, O, X(a, b))]))
+            act(R("q16", a, b), p, F.Identity, col("bq", t), -1.0)
+            p = R(tile(), 0, n)
+            mm(grp([(p, O, R("c1281", 0, n)), (p, O, X(a, b)), (p, I, R("q16", a, b))]))
+            act(R("pen", a, b), p, F.Identity, col("bp", t), -P23)
+            for k in range(16):
+                ts(R("mask", 16 * a + k, 16 * b, 16), R("pen", a, b), k * P23 if k else -4096.0, A.is_equal)
+                if k % 4 == 3:
+                    join(4)
+            act(R("q2", a, b), R("pen", a, b), F.Identity, -127.8 * 2 * P23, -1.0)
+
+        def link(b):
+            offs(wu("su", b), w(sw, b), col("cu", 0))
+            links(ln("au", b), tab, wu("su", b))
+
+        def pick(b, buf, off):
+            for a in range(LB * b, LB * b + LB, PIECE):
+                c = min(a + PIECE, LB * b + LB)
+                gat("gtt", R(buf, 16 * a, 16 * c), mem, R(off, a, c), R("mask", 16 * a, 16 * c), A.mult)
+
+        def sample(b, engs):
+            a = LB * b
+            sg = lambda k: R("sg", 16 * a + k * LB, 16 * a + (k + 1) * LB)
+            p = R(tile(), 0, LB)
+            mm(grp([(p, I, ln("pen", b)), (p, I, ln("q2", b)), (p, I, R("cK"))] + [(p, Bm("mH", h), st2(pm, b, h)) for h in range(2)]))
+            ts(ln("pu", b), p, -2048.0, A.max)
             p = tile()
-            mm(grp([(R(p, 0, n), Bm("mH", h), R(pm, L * h + a, L * h + b)) for h in range(2)]))
-            tt(R("pu", a, b), R(p, 0, n), R("ob", a, b), A.min)
-            p = tile()
-            mm(grp([(R(p, 0, n), Zr(k), R("g", 16 * a + k, 16 * b, 16)) for k in range(16)]))
+            mm(grp([(R(p, 0, LB), Zr(k), R("g", 16 * a + k, 16 * (a + LB), 16)) for k in range(16)]))
             for h in range(2):
-                copy(half(um, h, L * h + a, L * h + b), half(p, h, 0, n))
-            pairs(a, n, um, "sg", E3[c])
-            p = tile()
-            Mp = R(p, 0, n)
-            rest = [(Mp, BIG, R("c2048", 0, n)), (Mp, BIG, R("pu", a, b))] \
-                + [(Mp, Bm("mH", h), R(um, L * h + a, L * h + b)) for h in range(2)]
+                move(EC["um"], half(um, h, LB * (2 * b + h), LB * (2 * b + h + 1)), half(p, h, 0, LB))
+            pairs(b, um, "sg", engs)
+            Mp = R(tile(), 0, LB)
+            rest = [(Mp, BIG, R("c2048")), (Mp, BIG, ln("pu", b))] + [(Mp, Bm("mH", h), st2(um, b, h)) for h in range(2)]
             Y = lambda m, j: R(m, 78 - 64 * (j // 8) - 2 * (j % 8), 206 - 64 * (j // 8) - 2 * (j % 8))
-            if E3[c] == "A":
-                Sp = R(tile(), 0, n)
-                mm(grp([(Sp, PB, R("c128", 0, n))] + [(Sp, Y("mYP", j), sg(j)) for j in range(16)]))
-                act(R("rr", a, b), Sp, F.Identity, 0.0, 1.0 / BIGV / 32)
-                act(R("rr", L + a, L + b), Sp, F.Identity, UP / 32, 1.0 / BIGV / 32)
-                mm(grp(rest + [(Mp, BIG, R("rr", a, b)), (Mp, PB, R("rr", L + a, L + b))]))
+            if "A" in engs:
+                Sp = R(tile(), 0, LB)
+                mm(grp([(Sp, PB, R("c128", 0, LB))] + [(Sp, Y("mYP", j), sg(j)) for j in range(16)]))
+                act(st2("rr", b, 0), Sp, F.Identity, 0.0, 1.0 / BIGV / 32)
+                act(st2("rr", b, 1), Sp, F.Identity, UP / 32, 1.0 / BIGV / 32)
+                mm(grp(rest + [(Mp, BIG, st2("rr", b, 0)), (Mp, PB, st2("rr", b, 1))]))
             else:
                 mm(grp(rest + [(Mp, Y("mY8", j), sg(j)) for j in range(16)]))
                 ts(Mp, Mp, 8192.0, A.min)
-            tt(R("n16", a, b), Mp, R("pu", a, b), A.max)
-            copy(R("n16", L + a, L + b), R("n16", a, b))
-            ts(R("nu", a, b), R("n16", a, b), V - CEN, A.min, CEN, A.add)
-            act(R("vf", a, b), Mp, F.Relu, -4096.0)
+            tt(ln("nn", b), Mp, ln("pu", b), A.max)
+            for h in range(2):
+                move("G", st2("n16", b, h), ln("nn", b))
+            ts(ln("nu", b), ln("nn", b), V - CEN, A.min, CEN, A.add)
+            act(ln("vf", b), Mp, F.Relu, -4096.0)
 
-        def dist(c):
-            a, b = 16 * CH[c][0], 16 * CH[c][1]
-            for a1 in range(a, b, PIECE):
-                b1 = min(a1 + PIECE, b)
-                if E4[a1 // PIECE] == "A":
-                    agat(R("f", 16 * a1, 16 * b1), R("fw", 0, XB), R("nu", a1, b1))
-                else:
-                    gat("gcp", R("f", 16 * a1, 16 * b1), R("fw", 0, XB), R("nu", a1, b1))
-            diffs(a, b - a, "f", I, X(a, b), "ab", F.Abs, 0.0, 16.0)
+        def dist(b, engs):
+            a = LB * b
+            n = LB // len(engs)
+            for i, e in enumerate(engs):
+                a1 = a + i * n
+                agat(R("f", 16 * a1, 16 * (a1 + n)), R("fw", 0, XB), R("nu", a1, a1 + n))
+            for k0, k1 in KS:
+                bk = tile()
+                lst = []
+                for k in range(k0, k1):
+                    o = R(bk, (k - k0) * LB, (k - k0 + 1) * LB)
+                    lst += grp([(o, NI, X(a, a + LB)), (o, I, R("f", 16 * a + k, 16 * (a + LB), 16))])
+                mm(lst)
+                act(R("ab", 16 * a + k0 * LB, 16 * a + k1 * LB), R(bk, 0, (k1 - k0) * LB), F.Abs, 0.0, 16.0)
 
-        def mid(c):
-            h0, h1 = CH[c]
-            a, b, nh = 16 * h0, 16 * h1, h1 - h0
-            n = b - a
+        def least(b):
+            a = LB * b
             p = tile()
-            mm(grp([(R(p, 0, n), I, R("kc", a, b))] + [(R(p, 0, n), Zr(u), R("ab", 16 * a + u, 16 * b, 16)) for u in range(16)]))
-            for h in range(nh):
-                o, i_ = R("kmin", h0 + h, h0 + h + 1), R(p, h, n, nh)
+            mm(grp([(R(p, 0, LB), I, R("kc"))] + [(R(p, 0, LB), Zr(u), R("ab", 16 * a + u, 16 * (a + LB), 16)) for u in range(16)]))
+            for h in range(HB):
+                o, i_ = col("kmin", HB * b + h), R(p, h, LB, HB)
                 add("V", "red", (o, i_), [i_], [o], vc(16))
-            ts(w("ki2", h0, h1), w("kmin", h0, h1), 15, A.bitwise_and)
-            copy(w("ku", h0, h1), w("ki2", h0, h1))
-            gat("gtt", R("seln", a, b), R("rm"), w("ku", h0, h1), R("n16", a, b), A.mult)
-            Np = R(tile(), 0, nh)
-            mm(grp([(Np, Zr(u), R("seln", a + u, b, 16)) for u in range(16)]))
-            tt(w("xo", h0, h1), Np, R("lc", 16 * t + h0, 16 * t + h1), A.min)
-            ts(w("xu", h0, h1), w("xo", h0, h1), CEN, A.add)
-            gat("gcp", R("s2b", a, b), R("snb"), w("xu", h0, h1))
-            Sp = R(tile(), 0, nh)
-            mm(grp([(Sp, Zr(u), R("s2b", a + u, b, 16)) for u in range(16)]))
-            ts(w("s2u", h0, h1), Sp, 1.0 / 16, A.mult)
-            ts(w("s2w", h0, h1), Sp, 1.0 / 16, A.mult)
-            links(R("a2u", a, b), tab, w("s2u", h0, h1))
-            agat(R("fs", a, b), R("fw", 0, XB + L * (t + 1)), w("xu", h0, h1))
-            Xp = R(tile(), 0, n)
-            mm(grp([(Xp, I, R("fs", a, b)), (Xp, I, X(a, b)), (Xp, NI, R("c05", 0, n))]))
-            act(R("xy", a, b), Xp, F.Identity, MAGIC, 0.5)
-            act(R("xf", a, b) if last else R("xn", L * t + a, L * t + b), R("xy", a, b), F.Identity, -MAGIC)
-            gat("gtt", R("oc", a, b), tab, w("s2u", h0, h1), R("pen", a, b), A.min)
-            if not last:
-                gat("gtt", R("om", a, b), R("mem", 0, S), w("s2u", h0, h1), R("pen", a, b), A.min)
+            join(HB)
 
-        def xsend(b):
-            send([(R("xn", L * t + LB * b, L * t + LB * (b + 1)), R("fw", XB + L * (t + 1) + LB * b, XB + L * (t + 1) + LB * (b + 1)), 1 + b)],
-                 "ax%d_%d" % (t + 1, b))
-
-        def late():
-            snew = "sn%d" % (t + 1)
-            tt(w("c1"), w("kmin"), w("thr"), A.is_lt)
-            tt(w("df"), w("s2w"), w(sw), A.subtract)
-            tt(w("d2"), w("df"), w("c1"), A.mult)
-            ts(w("ne"), w("d2"), 0.0, A.is_equal, 4096.0, A.mult)
-            tt(w("k1"), w("ne"), w("s2w"), A.add)
-            tt(w("k16"), w("ne"), w("s2w"), A.add)
-            tt(w(snew), w("d2"), w(sw), A.add)
+        def mid(b):
+            a, n = LB * b[0], LB * len(b)
+            ts(w("ki2", b), w("kmin", b), 15, A.bitwise_and)
+            offs(wu("ku", b), w("ki2", b))
+            tt(w("c1", b), w("kmin", b), w("thr", b), A.is_lt)
+            gat("gtt", ln("seln", b), R("rm"), wu("ku", b), ln("nn", b), A.mult)
+            p = R(tile(), 0, n)
+            mm(grp([(p, I, R("cx", NW * t, NW * t + n)), (p, O, ln("seln", b))]))
+            scan(ln("xo", b), ln("tb", b), p, -8192.0, A.max, A.min)
+            offs(wu("xu", b), end("xo", b), XC[t] + CEN)
+            agat(ln("s2b", b), R("snb"), wu("xu", b))
+            scan(ln("s2x", b), R("ds", 0, n), ln("s2b", b), 0.0, A.add, A.min)
+            offs(wu("s2u", b), end("s2x", b), col("cu", 0))
+            act(w("s2w", b), end("s2x", b), F.Identity, col("cu", 0))
+            agat(ln("fs", b), R("fw", 0, XB + L * (t + 1)), wu("xu", b))
+            p = R(tile(), 0, n)
+            mm(grp([(p, I, X(a, a + n)), (p, I, ln("fs", b))]))
+            act(ln("xy", b), p, F.Identity, 1535.75, 0.5)
+            act(ln("xf", b) if last else R("xn", L * t + a, L * t + a + n), ln("xy", b), F.Identity, -1536.0)
             if not last:
-                send([(R(snew, 5 * b, 5 * b + 5), R("s%d" % (t + 1), 5 * b, 5 * b + 5), 1 + b) for b in range(3)], "as%d" % (t + 1))
-            ts(w("gu"), w("d2"), 0.0, A.is_equal)
-            agat(R("nogo"), R("t01", 0, 2), w("gu"))
-            act(R("go"), R("nogo"), F.Identity, 1.0, -1.0, None if last else R("cnt", 0, 1))
-            p = tile()
-            mm(grp([(R(p, 0, 2 * L), I, R(pm))] + [(R(p, L * h, L * h + L), Bm("mH", 4 + h), R("go")) for h in range(2)]))
-            act(R("pk1"), R(p, 0, 2 * L), F.Relu, 2048.0)
-            act(R("pk"), R("pk1"), F.Identity, -2048.0)
-            for h in range(NH):
-                ts(R("eq", L * h + 16 * h, L * (h + 1)), R("s2b", 16 * h, L), R("k1", h, h + 1), A.is_equal)
-            p = tile()
-            off = [(R(p, 16 * h + 16, L), O, R("eq", L * h + 16 * h + 16, L * (h + 1))) for h in range(NH - 1)]
-            mm(grp(off[:4], last=False))
-            mm(grp(off[4:9], first=False, last=False))
-            mm(grp(off[9:], first=False))
-            act(R("lb", 16, L), R(p, 16, L), F.Identity, 0.0, 256.0)
-            Op = R(tile(), 0, NH)
-            mm(grp([(Op, I, w("k16"))] + [(Op, Bm("mT", u), R("eq", u, L * NH, L + 16)) for u in range(1, 16)], last=False))
-            mm(grp([(Op, Zr(u), R("lb", u, L, 16)) for u in range(16)], first=False))
-            tt(w("of"), Op, w("dum"), A.min)
-            copy(w("ou"), w("of"))
-            if not last:
-                c0 = lambda n: R(n, 0, 1)
-                act(c0("a1"), c0("cnt"), F.Identity, -15.5 / 32, 1.0 / 32)
-                act(c0("a2"), c0("a1"), F.Identity, MAGIC)
-                act(c0("a3"), c0("a2"), F.Identity, 512 * MAGIC, -512.0)
-                act(c0("a4"), c0("cnt"), F.Identity, c0("a3"), 16.0)
-                act(w("thr"), w("thx"), F.Identity, c0("a4"))
+                at = XB + L * (t + 1)
+                send([(R("xn", L * t + LB * c, L * t + LB * c + LB), R("fw", at + LB * c, at + LB * c + LB), 1 + c) for c in b], "ax%d_%d" % (t + 1, b[0]))
+            for o, tb in (("oc", tab), ("om", mem))[:1 if last else 2]:
+                if HOLE == "V":
+                    gat("gtt", ln(o, b), tb, wu("s2u", b), ln("pen", b), A.min)
+                else:
+                    agat(ln(o + "r", b), tb, wu("s2u", b))
+                    p = R(tile(), 0, n)
+                    mm(grp([(p, R("mI32"), ln(o + "r", b)), (p, R("mP"), R("mask", 16 * a, 16 * (a + n), 16))]))
+                    act(ln(o, b), p)
+            if HOLE == "V":
+                links(ln("a2u", b), tab, wu("s2u", b))
             else:
+                offs(ln("a2u", b), ln("ocr", b), -2047.5 / 4096, 1.0 / 4096)
+
+        def late(b):
+            a, n, nh = LB * b[0], LB * len(b), HB * len(b)
+            tt(w("df", b), end("s2x", b), w(sw, b), A.subtract)
+            tt(w("d2", b), w("df", b), w("c1", b), A.mult)
+            ts(w("go", b), w("d2", b), 0.0, A.not_equal, 4096.0, A.mult)
+            tt(w(snew, b), w("d2", b), w(sw, b), A.add)
+            if not last:
+                send([(w(snew, c), w("s%d" % (t + 1), c), 1 + c) for c in b], "as%d_%d" % (t + 1, b[0]))
+            offs(wu("gu", b), w("go", b), 0.0, 1.0 / 4096)
+            agat(ln("nogo", b), R("t01", 0, 2), wu("gu", b))
+            eq = lambda h, lo, hi: R("eq", NW * (HB * b[0] + h) + lo, NW * (HB * b[0] + h) + hi)
+            for h in range(nh):
+                ts(eq(h, 16 * h, n), R("s2b", a + 16 * h, a + n), col("s2w", HB * b[0] + h), A.is_equal, col("go", HB * b[0] + h), A.mult)
+                if h % HB == HB - 1:
+                    join(HB)
+            p = tile()
+            mm(grp([(R(p, 0, n), I, R("co", 0, n)), (R(p, 0, n), I, ln("s2b", b))], last=False))
+            mm(grp([(R(p, 16 * h + 16, n), O, eq(h, 16 * h + 16, n)) for h in range(nh - 1)]
+                   + [(R(p, 16 * h, 16 * h + 16), R("mT"), eq(h, 16 * h, 16 * h + 16)) for h in range(nh)], first=False))
+            scan(ln("ox", b), ln("tb", b), R(p, 0, n), -8192.0, A.max, A.min)
+            offs(wu("ou", b), end("ox", b), float(S))
+            p = tile()
+            mm(grp([(R(p, 0, 2 * n), NI, st2(pm, b))] + [(R(p, LB * (2 * (c - b[0]) + h), LB * (2 * (c - b[0]) + h + 1)), Bm("mH", 4 + h), ln("nogo", c))
+                                                         for c in b for h in range(2)]))
+            if last:
+                act(st2("pk1", b), R(p, 0, 2 * n), F.Relu, 2048.0 - 8192.0, -1.0)
+                act(st2("pk", b), st2("pk1", b), F.Identity, -1.0)
                 p = tile()
-                mm([(R(p, u, L, 16), Bm("mB", u), w(snew), True, True) for u in range(16)])
-                act(R("sf"), R(p, 0, L), F.Identity)
-                dma("S", ("ys",), R("sf", pstep=16), 8000)
+                mm(grp([(R(p, 0, n), I, ln("cs", b))] + [(R(p, u, n, 16), Bm("mB", u), w(snew, b)) for u in range(16)]))
+                act(ln("sf", b), R(p, 0, n), F.Identity, 0.0, 1.0 / 4096)
+            else:
+                act(st2("pk", b), R(p, 0, 2 * n), F.Identity, -8192.0, -1.0)
+
+        def count():
+            act(R("junk"), R("nogo"), F.Identity, 16.0, -16.0, col("cnt", 0))
+            act(col("a1", 0), col("cnt", 0), F.Identity, 1536.0 - 15.5 / 32, 1.0 / 512)
+            act(col("a4", 0), col("a1", 0), F.Identity, col("cnt", 0), -512.0)
+            act(w("thr"), w("thx"), F.Identity, col("a4", 0))
 
         def values():
             if not last:
@@ -478,85 +541,103 @@ def plan():
                 act(R("bm"), Vp, F.Identity, -4096.0)
             p = tile()
             Vp = R(p, 0, L)
-            mm(grp([(Vp, NI, R("pen")), (Vp, I, R(vw))] + [(R(p, u, L, 16), Bm("mB4", u), w(sw)) for u in range(16)]))
+            mm(grp([(Vp, I, R("cs"))] + [(R(p, u, L, 16), Bm("mB", u), w(sw)) for u in range(16)] + [(Vp, NI, R("pen")), (Vp, I, R(vw))]))
             act(R("bc"), Vp, F.Identity, CEN - 4096.0)
 
-        def write():
-            for tb, o, bb in (("comb", "oc", "bc"), ("mem", "om", "bm"))[:1 if last else 2]:
-                add("V", "sct", (R(tb), w("ou"), R(o), R(bb), A.max), [w("ou"), R(o), R(bb)], [R(tb)], 50 + SCT * CYC * L)
+        def write(b, tb, o, bb):
+            add("V", "sct", (R(tb), wu("ou", b), ln(o, b), ln(bb, b), A.max), [wu("ou", b), ln(o, b), ln(bb, b)], [R(tb)], 50 + SCT * CYC * LB * len(b))
 
-        def recode(c):
-            a, b = 16 * CH[c][0], 16 * CH[c][1]
-            n = b - a
-            sh = lambda k: R("sh", 16 * a + k * n, 16 * a + (k + 1) * n)
-            p = tile()
-            Pp, Mp, PM = R(p, 0, n), R(p, n, 2 * n), R(p, 0, 2 * n)
+        def recode(b, engs):
+            a = LB * b
+            sh = lambda k: R("sh", 16 * a + k * LB, 16 * a + (k + 1) * LB)
             x = tile()
-            mm(grp([(R(x, 0, n), Zr(k, "mZ2"), R("h", 16 * a + k, 16 * b, 16)) for k in range(16)]))
+            mm(grp([(R(x, 0, LB), Zr(k, "mZ2"), R("h", 16 * a + k, 16 * (a + LB), 16)) for k in range(16)]))
             for h in range(2):
-                copy(half("n16", 1 - h, L * h + a, L * h + b), half(x, 1 - h, 0, n))
-            pairs(a, n, "n16", "sh", E7[c])
-            z = tile() if E7[c] == "A" else p
-            SS = R(z, 0, 2 * n)
-            sums = [(R(z, 0, n), R("mR", 128 * k + 64, 128 * k + 192), sh(k)) for k in range(8)] \
-                + [(R(z, n, 2 * n), R("mR", 128 * k, 128 * k + 128), sh(8 + k)) for k in range(8)]
-            rest = [(Pp, I, R("n16", a, b)), (Mp, I, R("n16", L + a, L + b))] \
-                + [(R(p, n * h, n * h + n), Bm("mH", 2 + h), R("vf", a, b)) for h in range(2)] \
-                + [(R(p, n * h, n * h + n), Bm("mH", 4 + h), R("nogo", a, b)) for h in range(2)]
-            if E7[c] == "A":
-                mm(grp([(SS, BIG, R("c128", 0, 2 * n))] + sums))
-                act(R("r2", 2 * a, 2 * b), SS, F.Identity, 0.0, -1.0 / BIGV)
-                act(R("r2", 2 * L + 2 * a, 2 * L + 2 * b), SS, F.Identity, UP, -1.0 / BIGV)
-                mm(grp([(PM, PB, R("r2", 2 * a, 2 * b)), (PM, BIG, R("r2", 2 * L + 2 * a, 2 * L + 2 * b))] + rest))
+                move(EC["n2"], half("n16", 1 - h, LB * (2 * b + h), LB * (2 * b + h + 1)), half(x, 1 - h, 0, LB))
+            pairs(b, "n16", "sh", engs)
+            p = tile()
+            PM = R(p, 0, 2 * LB)
+            Ph = lambda h: R(p, LB * h, LB * h + LB)
+            z = tile() if "A" in engs else p
+            sums = [(R(z, 0, LB), R("mR", 128 * k + 64, 128 * k + 192), sh(k)) for k in range(8)] \
+                + [(R(z, LB, 2 * LB), R("mR", 128 * k, 128 * k + 128), sh(8 + k)) for k in range(8)]
+            rest = [(PM, I, st2("n16", b))] + ([(PM, I, R("c2047"))] if last else []) \
+                + [(Ph(h), Bm("mH", 2 + h), ln("vf", b)) for h in range(2)] + [(Ph(h), Bm("mH", 4 + h), ln("nogo", b)) for h in range(2)]
+            if "A" in engs:
+                mm(grp([(R(z, 0, 2 * LB), BIG, R("c128"))] + sums))
+                act(st2("r2", b), R(z, 0, 2 * LB), F.Identity, 0.0, -1.0 / BIGV)
+                act(st2("r3", b), R(z, 0, 2 * LB), F.Identity, UP, -1.0 / BIGV)
+                mm(grp([(PM, PB, st2("r2", b)), (PM, BIG, st2("r3", b))] + rest))
             else:
-                mm(grp([(PM, BIG, R("c128", 0, 2 * n)), (PM, PB, R("c128", 0, 2 * n))] + sums + rest))
-            po = "pf" if last else "po%d" % t
-            tt(R(po, a, b), Pp, R("pk", a, b), A.max)
-            tt(R(po, L + a, L + b), Mp, R("pk", L + a, L + b), A.max)
+                mm(grp(rest + sums))
             if last:
-                act(R("pf2", a, b), R("pf", a, b), F.Identity, CEN)
-                act(R("pf2", L + a, L + b), R("pf", L + a, L + b), F.Identity, CEN)
+                for h in range(2):
+                    tt(R("pf", L * h + a, L * h + a + LB), Ph(h), st2("pk", b, h), A.max)
+            else:
+                tt(st2("po%d" % t, b), PM, st2("pk", b), A.max)
+                send([(st2("po%d" % t, b), st2("%s%d" % (to, t + 1), b), 1 + b) for to in ("um", "pm")], "ap%d_%d" % (t + 1, b))
 
-        def psend(b):
-            send([(R("po%d" % t, q + LB * b, q + LB * (b + 1)), R("%s%d" % (to, t + 1), q + LB * b, q + LB * (b + 1)), 1 + b)
-                  for to in ("um", "pm") for q in (0, L)],
-                 "ap%d_%d" % (t + 1, b))
+        def store(a, b):
+            for h in range(2):
+                dma("S", ("yp", a, b, 64 * h), half("pf", h, L * h + a, L * h + b), 512 * (b - a))
+                dma("S" if a else "A", ("yq", a, b, 64 * h), half("pf", 1 - h, L * h + a, L * h + b), 1024 * (b - a))
 
-        nc = len(CH)
         def stage(tag, fn, *args):
-            TAG[0] = tag + ("L" if last else "")
+            TAG[0], PAR[0] = tag, t
             fn(*args)
 
-        stage("front", front)
+        def finish(c, after=None):
+            at = len(ops)
+            stage("q%d" % c, pick, ORDER[c], "h", "a2u")
+            for o in ops[at:]:
+                o["after"] = after
+            stage("r%d" % c, recode, ORDER[c], E7[c])
+            if last and c:
+                store(LB * ORDER[c], L if c == 1 else LB)
+
+        for i, (a, b) in enumerate(MS):
+            stage("f%d" % i, front, a, b)
         stage("val", values)
-        for c in range(nc):
-            stage("p%d" % c, pick, c, "g", "au")
-            stage("s%d" % c, sample, c)
-            stage("d%d" % c, dist, c)
-            stage("m%d" % c, mid, c)
-            stage("q%d" % c, pick, c, "h", "a2u")
+        for c, b in enumerate(ORDER):
+            stage("k%d" % c, link, b)
+            stage("p%d" % c, pick, b, "g", "au")
+            gate = ops[-1]
+            for d in DEFER:
+                if before and DEFER[d] == c:
+                    before(d, gate)
+            stage("s%d" % c, sample, b, E3[c])
+            stage("d%d" % c, dist, b, E4[c])
+            stage("e%d" % c, least, b)
+            for bs in RUNS:
+                if bs[0] == b:
+                    stage("m%d" % c, mid, bs)
+                    stage("l%d" % c, late, bs)
+                    if not last:
+                        stage("w%d" % c, write, bs, "mem%d" % (t + 1), "om", "bm")
+        for bs in RUNS:
+            stage("w%d" % ORDER.index(bs[0]), write, bs, "comb", "oc", "bc")
+        TAG[0] = "tail"
+        if t == 0:
+            for a, b in LM:
+                keep(R("mem2", a, b), R("mem1", a, b))
         if not last:
-            for b in range(3):
-                xsend(b)
+            count()
         else:
             dma("S", ("yx",), R("xf"), 122880)
-        stage("late", late)
-        stage("write", write)
-        if last:
+            dma("S", ("ys",), R("sf", pstep=16), 8000)
             dma("S", ("ylm", 0, 768), R("comb", 0, 768), 400000)
             dma("S", ("ylm", 768, S), R("comb", 768, S), 800000)
-        for c in range(nc):
-            stage("r%d" % c, recode, c)
-        if not last:
-            for b in range(3):
-                psend(b)
-        else:
-            for h in range(2):
-                dma("S", ("yp", 0, L, 64 * h), half("pf2", h, L * h, L * h + L), 122880)
-                dma("A", ("yq", 0, L, 64 * h), half("pf2", 1 - h, L * h, L * h + L), 240000)
+        for c in range(len(ORDER)):
+            if last or c not in DEFER:
+                finish(c)
+        return finish
 
+    left = None
     for t in range(RO):
-        visit(t)
+        left = visit(t, left)
+    for o in ops:
+        if o["tag"] != "init" and o["cost"] < SHORT and o["eng"] == "A":
+            o["alt"] = []
     return ops
 
 
@@ -573,6 +654,10 @@ def clash(x, y):
 def depend(ops):
     hist = {}
     for o in ops:
+        wr = o["w"][0] if o["w"] else ("", 0, 0, 0, 0)
+        name = "ps" if wr[0][:2] == "ps" else wr[0].split("~")[0].rstrip("0123")
+        o["nth"] = (o["kind"], name, wr[1] % L if name == "xn" else wr[1], wr[4], int(o["cost"]))
+        who = o["id"] if o["alt"] else o["eng"]
         dep = set()
         if o["after"] is not None:
             dep.add(o["after"]["id"])
@@ -580,169 +665,221 @@ def depend(ops):
             for x in set(lst):
                 psum = x[0][:2] == "ps"
                 for (y, yw, oid, eng) in hist.get(x[0], ()):
-                    if oid != o["id"] and oid not in dep and ((psum and eng != o["eng"]) or ((isw or yw) and clash(x, y))):
+                    if oid != o["id"] and oid not in dep and ((psum and eng != who) or ((isw or yw) and clash(x, y))):
                         dep.add(oid)
         o["dep0"] = dep
         o["new"] = [n for n in set(x[0] for x in o["w"]) if n[:2] == "ps" and n not in hist]
         for isw, lst in ((False, o["r"]), (True, o["w"])):
             for x in set(lst):
-                hist.setdefault(x[0], []).append((x, isw, o["id"], o["eng"]))
-    return {n: set(e[2] for e in h) for n, h in hist.items() if n[:2] == "ps"}
-
-
-def schedule(ops, users, prio, slack):
-    if "succ" not in ops[0]:
-        for o in ops:
-            o["succ"] = []
-            o["tiles"] = sorted(set(x[0] for x in o["r"] + o["w"] if x[0][:2] == "ps"))
-        for o in ops:
-            for d in o["dep0"]:
-                ops[d]["succ"].append(o)
-        for o in reversed(ops):
-            o["tail"] = o["cost"] + o["lat"] + max([s["tail"] + HOP for s in o["succ"]] + [0.0])
-    if prio is None:
-        prio = {o["id"]: o["tail"] + BIAS.get(o["tag"], 0.0) for o in ops}
-    ready = {e: [] for e in "VAPGSX"}
+                hist.setdefault(x[0], []).append((x, isw, o["id"], who))
     for o in ops:
-        o["dep"], o["rt"], o["left"] = o["dep0"], 0.0, len(o["dep0"])
-        if not o["left"]:
-            ready[o["eng"]].append(o)
-    free = {e: 0.0 for e in "VAPGSX"}
-    tenant, banks, order = [None] * 8, {}, []
-    alive = {n: len(us) for n, us in users.items()}
-    ends = {n: 0.0 for n in users}
-    open_ = [(0.0, b) for b in range(8)]
-    while len(order) < len(ops):
-        t0, eng = None, None
-        for e, lst in ready.items():
-            if lst:
-                if e == "P":
-                    ts_ = [(o["rt"] if not o["new"] else max(o["rt"], open_[0][0])) for o in lst if open_ or not o["new"]]
-                    if not ts_:
-                        continue
-                    t = max(free[e], min(ts_))
-                else:
-                    t = max(free[e], min([o["rt"] for o in lst]))
-                if t0 is None or t < t0:
-                    t0, eng = t, e
-        if eng is None:
-            return None
-        lim = t0 + slack
-        cand = [o for o in ready[eng] if o["rt"] <= lim and (not o["new"] or (open_ and open_[0][0] <= lim))]
-        o = min(cand, key=lambda c: c["id"]) if eng in "SG" else max(cand, key=lambda c: prio[c["id"]])
-        st = max(free[eng], o["rt"])
-        if o["new"]:
-            st = max(st, open_[0][0])
-            pick = [x for x in open_ if x[0] <= st][-1]
-            open_.remove(pick)
-            if tenant[pick[1]]:
-                o["dep"] = o["dep0"] | users[tenant[pick[1]]]
-            tenant[pick[1]] = o["new"][0]
-            banks[o["new"][0]] = pick[1]
-        ready[eng].remove(o)
-        o["t0"] = st
-        free[eng] = st + o["cost"]
-        o["t1"] = t1 = st + o["cost"] + o["lat"]
-        order.append(o)
-        t1 += HOP
-        for n in o["tiles"]:
-            alive[n] -= 1
-            ends[n] = max(ends[n], t1)
-            if not alive[n]:
-                open_.append((ends[n], banks[n]))
-                open_.sort()
-        for s in o["succ"]:
-            if s["rt"] < t1:
-                s["rt"] = t1
-            s["left"] -= 1
-            if not s["left"]:
-                ready[s["eng"]].append(s)
-    return order, banks
-
-
-def latest(ops, order):
-    succ = {o["id"]: [] for o in ops}
-    for o in ops:
+        o["all"] = set(o["dep0"])
         for d in o["dep0"]:
-            succ[d].append(o["id"])
-    back, busy = {}, {e: [] for e in "VAPGSX"}
-    for o in sorted(order, key=lambda o: (-o["t1"], -o["id"])):
-        at = max([back[s] + HOP for s in succ[o["id"]]] + [0.0]) + o["lat"]
-        lst, i = busy[o["eng"]], 0
-        while i < len(lst) and lst[i][0] < at + o["cost"]:
-            at = max(at, lst[i][1])
-            i += 1
-        while i and lst[i - 1][0] >= at + o["cost"]:
-            i -= 1
-        lst.insert(i, (at, at + o["cost"]))
-        back[o["id"]] = at + o["cost"]
-    return back
+            o["all"] |= ops[d]["all"]
+        implied = set()
+        for d in o["dep0"]:
+            implied |= ops[d]["all"]
+        o["dep0"] = o["dep0"] - implied
+        if o["kind"] == "land":
+            o["all"] = set()
+    return {n: set(e[2] for e in h) for n, h in hist.items() if n[:2] == "ps"}
 
 
 def improve(ops, users, rounds, seed):
     rnd = np.random.RandomState(seed)
-    tags = sorted(set(o["tag"] for o in ops))
+    n = len(ops)
+    forms = [[(ENG.index(f["eng"]), f["cost"]) for f in [o] + o["alt"]] for o in ops]
+    slow = [SLOW.get(o["kind"], SLOW[""]) for o in ops]
+    lat = [o["lat"] for o in ops]
+    dep0 = [sorted(o["dep0"]) for o in ops]
+    succ = [[] for _ in ops]
+    for i in range(n):
+        for d in dep0[i]:
+            succ[d].append(i)
+    names = sorted(users)
+    tiles = [sorted(set(names.index(x[0]) for x in o["r"] + o["w"] if x[0][:2] == "ps")) for o in ops]
+    new = [names.index(o["new"][0]) if o["new"] else -1 for o in ops]
+    use = [sorted(users[x]) for x in names]
+    tensor = [o["id"] for o in ops if o["eng"] == "P"]
+    loads = [o["id"] for o in ops if o["eng"] == "S" and o["tag"] == "init"]
 
-    def look(res):
-        before, on = {}, {}
-        for x in res[0]:
-            before[x["id"]] = on.get(x["eng"])
-            on[x["eng"]] = x
-        o, pairs = max(ops, key=lambda o: o["t1"]), []
-        end = o["t1"]
-        while o is not None:
-            c = [ops[d] for d in o["dep"] if abs(ops[d]["t1"] + HOP - o["t0"]) < 1]
-            if not c and before[o["id"]] is not None and o["rt"] < o["t0"] - 1 and o["eng"] in "VAP":
-                pairs.append((o["id"], before[o["id"]]["id"]))
-            o = c[0] if c else before[o["id"]]
-        free, fin = {e: 0.0 for e in "VAPGSX"}, {}
-        for x in res[0]:
-            st = max([free[x["eng"]]] + [fin[d] for d in x["dep"]])
-            free[x["eng"]] = st = st + slow[x["id"]]
-            fin[x["id"]] = st + x["lat"] + 80.0
-        return (end + MIX * max(fin.values())) / (1.0 + MIX), pairs, res[0]
+    def place(prio, eng, cost, post, back):
+        rank = [-p for p in prio]
+        for i in (range(n - 1, -1, -1) if back else range(n)):
+            r = rank[i] + 0.001
+            for s in post[i]:
+                if rank[s] < r:
+                    rank[s] = r
+        rt, t0 = [0.0] * n, [0.0] * n
+        los, his = [[] for _ in ENG], [[] for _ in ENG]
+        for o in np.argsort(rank, kind="stable").tolist():
+            c, lo, hi = cost[o], los[eng[o]], his[eng[o]]
+            st = rt[o] + (lat[o] if back else 0.0)
+            if c:
+                i = m = len(lo)
+                while i and hi[i - 1] > st:
+                    i -= 1
+                while i < m and lo[i] < st + c:
+                    st = hi[i]
+                    i += 1
+                en = st + c
+                if i and st - hi[i - 1] < 50.0:
+                    if i < m and lo[i] - en < 50.0:
+                        hi[i - 1] = hi[i]
+                        del lo[i], hi[i]
+                    else:
+                        hi[i - 1] = en
+                elif i < m and lo[i] - en < 50.0:
+                    lo[i] = st
+                else:
+                    lo.insert(i, st)
+                    hi.insert(i, en)
+            t0[o] = st
+            en = st + c + HOP + (0.0 if back else lat[o])
+            for s in post[o]:
+                if rt[s] < en:
+                    rt[s] = en
+        return t0
 
-    slow = [o["cost"] * (1.0 if o["eng"] not in "VAP" else 1.55 if o["kind"] in ("gcp", "gts", "gtt", "agat", "sct") else 1.25) for o in ops]
+    def schedule(prio, side, bar=1e18):
+        eng = [forms[i][side[i]][0] for i in range(n)]
+        cost = [forms[i][side[i]][1] for i in range(n)]
+        key = place(prio, eng, cost, succ, False)
+        nxt = 1e18
+        for i in sorted(tensor, key=lambda i: -key[i]):
+            if new[i] >= 0:
+                key[i] = max(key[i], min([nxt] + [key[s] - HOP for s in succ[i]]) - cost[i])
+            nxt = key[i]
+        todo, order, held = np.argsort(key, kind="stable").tolist()[::-1], [], []
+        free, fr2, fin, fi2, t0s, before, on = [0.0] * 6, [0.0] * 6, [0.0] * n, [0.0] * n, [0.0] * n, [-1] * n, [-1] * 6
+        alive, ends, end2 = [len(u) for u in use], [0.0] * len(names), [0.0] * len(names)
+        open_, tenant, bank, extra, rts = list(range(8)), [-1] * 8, [0] * len(names), {}, [0.0] * n
+        while todo:
+            x = todo.pop()
+            if (new[x] >= 0 and not open_) or (held and not all([fin[d] for d in dep0[x]])):
+                held.append(x)
+                continue
+            order.append(x)
+            e = eng[x]
+            st = s2 = 0.0
+            for d in dep0[x]:
+                if fin[d] > st:
+                    st = fin[d]
+                if fi2[d] > s2:
+                    s2 = fi2[d]
+            if new[x] >= 0:
+                b = open_.pop(0)
+                y = tenant[b]
+                if y >= 0:
+                    extra[x] = y
+                    if ends[y] > st:
+                        st = ends[y]
+                    if end2[y] > s2:
+                        s2 = end2[y]
+                tenant[b] = new[x]
+                bank[new[x]] = b
+            rts[x] = st
+            if free[e] > st:
+                st = free[e]
+            if fr2[e] > s2:
+                s2 = fr2[e]
+            t0s[x] = st
+            before[x], on[e] = on[e], x
+            free[e] = st = st + cost[x]
+            fr2[e] = s2 = s2 + slow[x] * cost[x]
+            fin[x] = st = st + lat[x] + HOP
+            fi2[x] = s2 = s2 + lat[x] + 80.0
+            for y in tiles[x]:
+                if ends[y] < st:
+                    ends[y] = st
+                if end2[y] < s2:
+                    end2[y] = s2
+                alive[y] -= 1
+                if not alive[y]:
+                    open_.append(bank[y])
+                    todo += reversed(held)
+                    held = []
+        val = (max(fin) + MIX * max(fi2)) / (1.0 + MIX)
+        if held or val > bar:
+            return None
+        o, pairs, path = fin.index(max(fin)), [], []
+        while o >= 0:
+            path.append(o)
+            c = [d for d in dep0[o] + (use[extra[o]] if o in extra else []) if abs(fin[d] - t0s[o]) < 1]
+            if not c and before[o] >= 0 and rts[o] < t0s[o] - 1 and eng[o] < 4:
+                pairs.append((o, before[o]))
+            o = c[0] if c else before[o]
+        return val, pairs, path, order, t0s, [f - HOP for f in fin], bank, extra, eng, cost, max(fi2)
 
-    same = {}
+    def latest(res):
+        t0 = place(res[5], res[8], res[9], dep0, True)
+        prio = [t0[i] + res[9][i] for i in range(n)]
+        for i in loads:
+            prio[i] = 1e7 - i
+        return prio
+
+    same, stages = {}, {}
     for o in ops:
-        wr = o["w"][0] if o["w"] else ("", 0)
-        name = "ps" if wr[0][:2] == "ps" else wr[0].split("~")[0].rstrip("0123")
-        same.setdefault((o["tag"].rstrip("L"), o["kind"], name, wr[1] % L if name == "xn" else wr[1], int(o["cost"])), []).append(o["id"])
+        same.setdefault((o["tag"], o["nth"]), []).append(o["id"])
+        stages.setdefault(o["tag"], []).append(o["id"])
+        stages.setdefault(o["tag"] + "/%d" % o["vis"], []).append(o["id"])
     twins = {i: lst for lst in same.values() for i in lst}
-    for t in tags:
-        BIAS[t] = STAGGER * int(t[1]) if t[1].isdigit() and t[0] != "r" else 0.0
-    schedule(ops, users, None, SLACK)
-    prio = {o["id"]: o["tail"] + BIAS.get(o["tag"], 0.0) for o in ops}
-    now = look(schedule(ops, users, prio, SLACK))
-    best = (now[0], prio)
+    tags = sorted(stages)
+    flex = [i for i in range(n) if len(forms[i]) > 1]
+    prio, side = [0.0] * n, [0] * n
+    for i in reversed(range(n)):
+        prio[i] = forms[i][0][1] + lat[i] + max([prio[s] + HOP for s in succ[i]] + [0.0])
+    for o in ops:
+        t = o["tag"]
+        prio[o["id"]] += STAGGER * int(t[1]) if t[1].isdigit() and t[0] not in "qr" else 0.0
+        if t == "init" and o["alt"] and o["eng"] == "A" and o["alt"][0]["cost"] < 0.6 * o["cost"]:
+            side[o["id"]] = 1
+    for i in loads:
+        prio[i] = 1e7 - i
+    now = schedule(prio, side)
+    best = (now, side)
     for r in range(rounds):
-        new, move = dict(prio), rnd.rand()
-        if move < 0.6 and now[1]:
+        p2, s2, move = prio, side, rnd.rand()
+        if move < 0.5 and now[1]:
+            p2 = list(prio)
             for _ in range(int(rnd.randint(1, 4))):
                 a, b = now[1][int(rnd.randint(len(now[1])))]
-                d = abs(new[b] - new[a]) + float(rnd.choice([50.0, 500.0, 2000.0]))
+                d = abs(p2[b] - p2[a]) + (50.0, 500.0, 2000.0)[int(rnd.randint(3))]
                 x, d = (a, d) if rnd.rand() < 0.5 else (b, -d)
-                for y in (twins[x] if rnd.rand() < 0.6 else [x]):
-                    new[y] += d
+                for y in (twins[x] if rnd.rand() < 0.5 else [x]):
+                    p2[y] += d
+        elif move < 0.72 and flex:
+            s2 = list(side)
+            on = [i for i in now[2] if len(forms[i]) > 1]
+            for _ in range(int(rnd.randint(1, 3))):
+                lst = on if on and rnd.rand() < 0.6 else flex
+                x = lst[int(rnd.randint(len(lst)))]
+                to = (s2[x] + 1 + int(rnd.randint(len(forms[x]) - 1))) % len(forms[x])
+                for y in (twins[x] if rnd.rand() < 0.5 else [x]):
+                    s2[y] = to % len(forms[y])
         elif move < 0.97:
-            t, d = tags[int(rnd.randint(len(tags)))], float(rnd.choice([-1.0, 1.0]) * rnd.choice([300.0, 1000.0, 3000.0]))
-            eng = str(rnd.choice(["VAP", "V", "A", "P"]))
-            for o in ops:
-                if o["eng"] in eng and (o["tag"] == t or (d > 0 and o["tag"][:-1] == t)):
-                    new[o["id"]] += d
+            p2 = list(prio)
+            d = (-1.0, 1.0)[int(rnd.randint(2))] * (300.0, 1000.0, 3000.0)[int(rnd.randint(3))]
+            e = int(rnd.randint(4))
+            for i in stages[tags[int(rnd.randint(len(tags)))]]:
+                if e == 3 or now[8][i] == e:
+                    p2[i] += d
         else:
-            schedule(ops, users, prio, SLACK)
-            new = latest(ops, now[2])
-        res = schedule(ops, users, new, SLACK)
-        if res is None:
+            p2 = latest(now)
+        got = schedule(p2, s2, now[0] + HEAT * (1.0 - r / rounds) * rnd.rand())
+        if got is None:
             continue
-        got = look(res)
-        if got[0] <= now[0] + 400.0 * (1.0 - r / rounds) * rnd.rand():
-            prio, now = new, got
-        if got[0] < best[0]:
-            best = (got[0], new)
-    return schedule(ops, users, best[1], SLACK)
+        prio, side, now = p2, s2, got
+        if got[0] < best[0][0]:
+            best = (got, s2)
+    res, side = best
+    for o in ops:
+        i = o["id"]
+        if side[i]:
+            o.update(o["alt"][side[i] - 1])
+        o["t0"], o["t1"] = res[4][i], res[5][i]
+        o["dep"] = set(dep0[i]) | set(use[res[7][i]] if i in res[7] else [])
+    return [ops[i] for i in res[3]], {x: res[6][k] for k, x in enumerate(names)}, res[10]
 
 
 PLAN = []
@@ -755,7 +892,7 @@ def rank_program(g, core, T, topo):
     if not PLAN:
         ops = plan()
         PLAN.append((ops,) + improve(ops, depend(ops), ROUNDS, SEED))
-    ops, order, banks = PLAN[0]
+    ops, order, banks, _ = PLAN[0]
     n = len(T.cores)
     Q = {"V": g.vector, "A": g.scalar, "P": g.tensor, "G": g, "S": g.sync}
 
@@ -775,6 +912,13 @@ def rank_program(g, core, T, topo):
 
     def ind(win, off):
         return ap(win).indirect(ap(off))
+
+    def call(q, k, a):
+        if k == "red":
+            return q.tensor_reduce(ap(a[0]), ap(a[1]), AX.X, A.min)
+        if a[5] is None:
+            return q.tensor_scalar(ap(a[0]), ap(a[1]), ap(a[2]), ap(a[3]), a[4])
+        return q.tensor_scalar(ap(a[0]), ap(a[1]), ap(a[2]), ap(a[3]), a[4], a[5])
 
     def engines(dst, parts):
         es = topo.engines(core, dst)
@@ -812,17 +956,21 @@ def rank_program(g, core, T, topo):
                 if kn.get(s2, 0) < v2:
                     kn[s2] = v2
         sem, inc = "e" + e, 1
-        if k == "copy":
+        if k == "many":
+            for s in a[:-1]:
+                call(q, s["kind"], s["args"]).then_inc(T.sem[sem], 1)
+                total[sem] = total.get(sem, 0) + 1
+            k, a = a[-1]["kind"], a[-1]["args"]
+        if k in ("ts", "red"):
+            i = call(q, k, a)
+        elif k == "copy":
             i = q.tensor_copy(ap(a[0]), ap(a[1]))
-        elif k == "ts":
-            i = q.tensor_scalar(ap(a[0]), ap(a[1]), ap(a[2]), ap(a[3]), a[4]) if a[5] is None else \
-                q.tensor_scalar(ap(a[0]), ap(a[1]), ap(a[2]), ap(a[3]), a[4], a[5])
         elif k == "tt":
             i = q.tensor_tensor(ap(a[0]), ap(a[1]), ap(a[2]), a[3])
+        elif k == "scan":
+            i = q.tensor_tensor_scan(ap(a[0]), ap(a[1]), ap(a[2]), a[3], a[4], a[5])
         elif k == "mset":
             i = q.memset(ap(a[0]), a[1])
-        elif k == "red":
-            i = q.tensor_reduce(ap(a[0]), ap(a[1]), AX.X, A.min)
         elif k == "gcp":
             i = q.tensor_copy(ap(a[0]), ind(a[1], a[2]))
         elif k == "gts":
@@ -835,6 +983,8 @@ def rank_program(g, core, T, topo):
             i = q.activation(ap(a[0]), ap(a[1]), a[2], bias=ap(a[3]), scale=ap(a[4]), accum_out=ap(a[5]))
         elif k == "agat":
             i = q.activation(ap(a[0]), ind(a[1], a[2]), F.Identity)
+        elif k == "agact":
+            i = q.activation(ap(a[0]), ind(a[1], a[2]), a[3], bias=a[4], scale=a[5])
         elif k == "mm":
             for m in a:
                 i = q.matmul(ap(m[0]), ap(m[1]), ap(m[2]), m[3], m[4])
@@ -844,7 +994,7 @@ def rank_program(g, core, T, topo):
             else:
                 i = q.iota(ap(a[0]), a[2], a[3], a[4], allow_small_or_imprecise_dtypes=True)
         elif k == "sel":
-            i = q.affine_select(ap(a[0]), ap(a[1]), a[2], a[3], 0.0, a[4], a[5])
+            i = q.affine_select(ap(a[0]), ap(a[1]), a[2], a[3], a[6], a[4], a[5])
         elif k == "dma":
             i = q.dma_start(ap(a[0]), ap(a[1]))
             sem, inc = a[2], 16

import math
import numpy as np
from concourse.bass import DstId, RemoteDMATransfer
from concourse.mybir import AluOpType as A, AxisListType as AX, ActivationFunctionType as F

V, S, L, NH, LB, HB, RO = 4096, 1536, 240, 15, 80, 5, 3
ORDER = (2, 1, 0)
MS = [(80, 240), (0, 80)]
E3 = ("AAA", "AAA", "AAA")
E7 = ("AAA", "AAA", "AAA")
E4 = ("AA", "AA", "AA")
EC = {"um": "A", "n2": "A", "dup": "G", "s2b": "V", "s2w": "A", "pm0": "A", "sn": "AAAAAAAA"}
SEED, ROUNDS, HEAT, STAGGER, SHORT = 4, 24000, 400.0, -2000.0, 350.0
MIX = 1.0
SLOW = {"": 1.16, "dma": 1.0, "send": 1.0, "land": 1.0, "gcp": 1.49, "gts": 1.49, "gtt": 1.49, "agat": 1.49, "sct": 1.7}
DEFER = {}
RUNS = ((2,), (1,), (0,))
HOLE = "A"
NW = 160
PIECE = 40
XB = 4112
WIN = XB + RO * L
TW = S + 1 + L
CEN = 2047.0
BIGV = 262144.0
P23 = 8388608.0
UP = 0.48
SIGC, SIGB = 128.0, -math.log(31.0)

SCRATCH = {}
BUF = {}
POOL = {}
DUP = ("pen", "q2", "mask", "n16", "vf", "nogo", "pk", "h", "kmin", "s2u", "bc", "bm", "au", "oc", "om", "ou")


def _sb(name, cols, dt, parts=128):
    names = [name + "~0", name + "~1"] if name in DUP else [name]
    pool = "small_" + dt if cols <= 256 and parts == 128 else name
    for nm in names:
        BUF[nm] = ("sbuf", [parts, cols], dt)
        at = SCRATCH[pool][1][1] if pool in SCRATCH else 0
        SCRATCH[pool] = ("sbuf", [parts, at + -(-cols // 16) * 16], dt)
        POOL[nm] = (pool, at)


for _n, _c, _d in [
    ("fw", WIN, "bfloat16"), ("snb", WIN, "float32"), ("sni", 257, "int32"), ("sn16", 256, "float16"), ("lmi", S, "int32"), ("memi", S, "int32"),
    ("comb", TW, "float32"), ("mem0", S, "float32"), ("mem1", TW, "float32"), ("mem2", TW, "float32"), ("pqi", 2 * L, "int32"),
    ("ones", 160, "bfloat16"), ("rm4", 16, "float32"), ("c128", 160, "bfloat16"), ("c2048", LB, "bfloat16"), ("cK", LB, "bfloat16"),
    ("c1281", 160, "float16"), ("c2047", 160, "float16"),
    ("mI", 128, "bfloat16"), ("mN", 128, "bfloat16"), ("mBIG", 128, "bfloat16"), ("mPB", 128, "bfloat16"),
    ("mO1", 128, "bfloat16"), ("mO", 128, "bfloat16"), ("mZ", 144, "bfloat16"), ("mZ2", 144, "bfloat16"), ("mY", 208, "bfloat16"),
    ("mYP", 208, "bfloat16"), ("mY8", 208, "bfloat16"), ("mYN", 208, "bfloat16"), ("mD0", 256, "bfloat16"), ("mD", 2048, "bfloat16"), ("mR", 17 * 64, "bfloat16"),
    ("mJ", 128, "bfloat16"), ("mH", 768, "bfloat16"), ("mB", 2048, "bfloat16"), ("mT1", 128, "bfloat16"), ("mT", 128, "bfloat16"),
    ("hm", 16, "float32"), ("sc", 16, "float32"), ("par", 16, "float32"),
    ("um0", 2 * L, "float16"), ("um1", 2 * L, "float16"), ("um2", 2 * L, "float16"),
    ("io1", 16, "int32"), ("ei", 16, "int32"), ("oi", 16, "int32"), ("ef", 16, "float32"), ("rm", 16, "float32"),
    ("iw", L, "int32"), ("iw2", L, "int32"), ("iw3", NW, "int32"), ("tb", L, "float32"), ("e0", NW, "bfloat16"), ("e15", NW, "bfloat16"), ("ds", NW, "bfloat16"),
    ("cx", RO * NW, "bfloat16"), ("co", NW, "bfloat16"), ("nn", L, "float16"), ("ocr", L, "float32"), ("omr", L, "float32"),
    ("mI32", 128, "float32"), ("mP", 128, "bfloat16"), ("bq", 16, "float32"), ("bp", 16, "float32"), ("cu", 16, "float32"),
    ("ku", 24, "uint16"), ("gu", 24, "uint16"), ("su", 24, "uint16"), ("xu", 24, "uint16"), ("s2u", 24, "uint16"), ("ou", 24, "uint16"),
    ("t01", 16, "bfloat16"), ("junk", L, "bfloat16"), ("pk1", 2 * L, "float32"),
    ("kc", LB, "bfloat16"), ("thx", 16, "float32"), ("thr", 16, "float32"),
    ("q16", L, "float16"), ("q2", L, "bfloat16"), ("pen", L, "bfloat16"), ("mask", 16 * L, "bfloat16"), ("au", L, "uint16"), ("a2u", L, "uint16"),
    ("pu", L, "float16"), ("rr", 2 * L, "bfloat16"), ("n16", 2 * L, "float16"), ("nu", L, "uint16"),
    ("vf", L, "bfloat16"), ("kmin", 16, "int32"), ("ki2", 16, "int32"),
    ("seln", L, "float16"), ("xo", L, "float32"), ("s2b", L, "float16"), ("s2x", L, "float16"), ("ox", L, "float32"),
    ("fs", L, "bfloat16"), ("xy", L, "float16"), ("xn", 2 * L, "bfloat16"),
    ("s2w", 16, "float32"), ("cs", L, "bfloat16"), ("c1", 16, "float32"), ("df", 16, "float32"), ("d2", 16, "float32"), ("go", 16, "float32"),
    ("sn1", 16, "float16"), ("sn2", 16, "float16"), ("sn3", 16, "float16"),
    ("eq", NH * NW, "bfloat16"), ("nogo", L, "bfloat16"), ("cnt", 4, "float32"), ("a1", 4, "float16"), ("a4", 4, "float32"),
    ("oc", L, "float32"), ("om", L, "float32"), ("bc", L, "float32"), ("bm", L, "float32"),
    ("r2", 2 * L, "bfloat16"), ("r3", 2 * L, "bfloat16"), ("pk", 2 * L, "float32"),
    ("pm0", 2 * L, "float16"), ("pm1", 2 * L, "float16"), ("pm2", 2 * L, "float16"),
    ("po0", 2 * L, "float16"), ("po1", 2 * L, "float16"), ("pf", 2 * L, "float32"),
    ("s0", 16, "float16"), ("s1", 16, "float16"), ("s2", 16, "float16"),
    ("v0", L, "float16"), ("v1", L, "float16"), ("v2", L, "float16"),
    ("xf", L, "float32"), ("sf", L, "float32"),
    ("g", 16 * L, "float16"), ("h", 16 * L, "float16"), ("sg", 16 * L, "bfloat16"), ("f", 16 * L, "bfloat16"),
    ("ab", 16 * L, "bfloat16"), ("sh", 16 * L, "bfloat16"),
]:
    _sb(_n, _c, _d)
_sb("rwi", L, "int32", 24)
_sb("rw", L, "float16", 24)
_sb("z24", 2 * 144 + 128, "bfloat16", 24)
for _i in range(8):
    SCRATCH["bank%d" % _i] = ("psum", [128, 512], "float32")

NDMA = 24
SEMAPHORES = (["eV", "eA", "eP", "eG", "sent", "rw", "pq"] + ["d%d" % _i for _i in range(NDMA)]
              + ["%s%d_%d" % (_a, _t, _b) for _a in ("ax", "as", "ap") for _t in (1, 2) for _b in range(3)] + ["av1", "av2"])
SIZE = {"float32": 4, "int32": 4, "bfloat16": 2, "float16": 2, "uint16": 2}
CYC, PEC, HOP, GAT, SCT = 1.04, 0.525, 150.0, 1.6, 3.8
PAR, TAG = [0], ["init"]
ENG = "VAPGSX"


def R(name, lo=0, hi=None, step=1, p0=0, p1=None, pstep=1):
    if name in DUP:
        name = "%s~%d" % (name, PAR[0] % 2)
    shp = [128, 512] if name[:2] == "ps" else BUF[name][1]
    return (name, lo, shp[1] if hi is None else hi, step, p0, shp[0] if p1 is None else p1, pstep)


def cnt(r):
    return (r[2] - r[1] + r[3] - 1) // r[3]


def two(*rs):
    return all(r[0][:2] != "ps" and SIZE[BUF[r[0]][2]] == 2 for r in rs)


def plan():
    ops = []
    PAR[0], TAG[0] = 0, "init"

    def add(eng, kind, args, reads, writes, cost, lat=0.0, after=None):
        ops.append({"eng": eng, "kind": kind, "args": args, "r": reads, "w": writes, "cost": cost, "lat": lat, "after": after, "id": len(ops),
                    "tag": TAG[0], "vis": PAR[0], "alt": []})
        return ops[-1]

    def join(n):
        sub = ops[-n:]
        del ops[-n:]
        add(sub[0]["eng"], "many", sub, [r for s in sub for r in s["r"]], [r for s in sub for r in s["w"]], sum(s["cost"] for s in sub))

    def aps(*xs):
        return [x for x in xs if isinstance(x, tuple)]

    def vc(n):
        return max(64.0, n) * CYC

    def copy(out, in_):
        add("V", "copy", (out, in_), [in_], [out], vc(cnt(out) * (0.5 if two(out, in_) else 1)))

    def ts(out, in0, s1, op0, s2=None, op1=None):
        add("V", "ts", (out, in0, s1, s2, op0, op1), aps(in0, s1, s2), [out], vc(cnt(out) * (0.5 if two(out, in0) else 1)))

    def tt(out, in0, in1, op):
        ps = in0[0][:2] == "ps" or in1[0][:2] == "ps"
        add("V", "tt", (out, in0, in1, op), [in0, in1], [out], vc(cnt(out) * (1 if ps else 2)))

    def scan(out, d0, d1, init, op0, op1):
        add("V", "scan", (out, d0, d1, init, op0, op1), [d0, d1], [out], vc(cnt(out) * (0.5 if two(out, d0, d1) else 1)))

    def gat(kind, out, win, off, *rest):
        add("V", kind, (out, win, off) + rest, aps(win, off, *rest), [out], 50 + GAT * CYC * cnt(out))

    def mset(out, val):
        add("V", "mset", (out, val), [], [out], vc(cnt(out) * (0.5 if two(out) else 1)))

    def other():
        o = ops.pop()
        ops[-1]["alt"].append({k: o[k] for k in ("eng", "kind", "args", "cost")})

    def act(out, in_, f=F.Identity, bias=0.0, scale=1.0, acc=None):
        add("A", "act", (out, in_, f, bias, scale, acc), aps(in_, bias, scale), aps(out, acc), vc(cnt(out)) + 30)
        if f == F.Identity and acc is None:
            ts(out, in_, scale, A.mult, bias, A.add)
            other()
        elif f == F.Relu and scale == 1.0:
            ts(out, in_, bias, A.add, 0.0, A.max)
            other()

    def agat(out, win, off):
        add("A", "agat", (out, win, off), [win, off], [out], 65 + GAT * CYC * cnt(out))
        gat("gcp", out, win, off)
        other()

    def offs(out, in_, bias=0.0, scale=1.0):
        ts(out, in_, scale, A.mult, bias, A.add)
        add("A", "act", (out, in_, F.Identity, bias, scale, None), [], [], vc(cnt(out)) + 30)
        other()

    def pool(kind, out, in_, *args):
        add("G", kind, (out, in_) + args, aps(in_), [out], 170 + 2 * CYC * cnt(out))

    def keep(out, in_):
        pool("sel", out, in_, [[0, cnt(out)]], A.is_equal, 0, 0, 0.0)

    def move(eng, out, in_, bias=None):
        if eng == "G":
            keep(out, in_)
            act(out, in_)
            ops[-2]["alt"] += ops[-1]["alt"]
            other()
        else:
            act(out, in_, F.Identity, 0.0 if bias is None else bias)

    def mm(lst):
        add("P", "mm", lst, [m[1] for m in lst] + [m[2] for m in lst], [m[0] for m in lst],
            sum(max(64, cnt(m[2])) * (1 if two(m[2]) else 4) for m in lst) * PEC)

    def grp(lst, first=True, last=True):
        return [(o, l, r, first and i == 0, last and i == len(lst) - 1) for i, (o, l, r) in enumerate(lst)]

    nd, nt = [0], [0]

    def tile():
        nt[0] += 1
        return "ps%d" % nt[0]

    sofar = [0]

    def dma(q, out, in_, nbytes, sem=None, load=False):
        if sem is None:
            sem = "d%d" % nd[0]
            nd[0] += 1
        if load:
            sofar[0] += nbytes
            nbytes = sofar[0]
        rd = [in_] if in_[0] in BUF else []
        wr = [out] if out[0] in BUF else []
        return add(q, "dma", (out, in_, sem), rd, wr, 100.0, 1800.0 + nbytes / 200.0)

    def send(items, sem):
        s = add("G", "send", (items, sem), [i[0] for i in items], [], 700.0)
        add("X", "land", (len(items), sem), [], [i[1] for i in items], 0.0, 2500.0, s)

    Zr = lambda u, m="mZ": R(m, 15 - u, 143 - u)
    Bm = lambda m, u: R(m, 128 * u, 128 * u + 128)
    I, NI, BIG, PB, O = R("mI"), R("mN"), R("mBIG"), R("mPB"), R("mO")
    run = lambda b: (b, b + 1) if isinstance(b, int) else (b[0], b[-1] + 1)
    w = lambda n, b=(0, 1, 2): R(n, HB * run(b)[0], HB * run(b)[1])
    wu = lambda n, b: R(n, 6 * run(b)[0], 6 * run(b)[0] + HB * (run(b)[1] - run(b)[0]))
    ln = lambda n, b, step=1, at=0: R(n, LB * run(b)[0] + at, LB * run(b)[1], step)
    end = lambda n, b: ln(n, b, 16, 15)
    st2 = lambda n, b, h=None: R(n, 2 * LB * run(b)[0], 2 * LB * run(b)[1]) if h is None else R(n, LB * (2 * b + h), LB * (2 * b + h + 1))
    half = lambda m, h, lo, hi, step=1: R(m, lo, hi, step, 64 * h, 64 * h + 64)
    own = lambda m, h, step=1: half(m, h, 64 * h, 64 * h + 64, step)
    col = lambda m, c: R(m, c, c + 1)

    dma("S", R("fw", XB, XB + L), ("lx",), 61440, load=True)
    for i, n in enumerate(("ls", "lv", "th")):
        dma("A", R("rwi", p0=8 * i, p1=8 * i + 8), (n,), 90000, "rw")
    LM = [(0, 512), (512, 1024), (1024, S)]
    dma("S", R("sni", 0, 256), ("sn",), 131072, load=True)
    for a, b in LM:
        dma("S", R("lmi", a, b), ("lm", a, b), 512 * (b - a), load=True)
    for h in range(2):
        dma("S", half("pqi", h, L * h, L * h + L), ("lp", 0, L, 64 * h), 61440, "pq", load=True)
        dma("S", half("pqi", 1 - h, L * h, L * h + L), ("lq", 0, L, 64 * h), 61440, "pq", load=True)
    for o in ops[-4:]:
        o["lat"] = ops[-1]["lat"]
    dma("S", R("fw", 0, V), ("feat",), 1048576, load=True)

    mset(R("ones"), 1.0)
    pool("iota", R("io1"), None, [[-1, 16]], 128, 1)
    pool("sel", R("mO1"), R("ones", 0, 128), [[-16, 8], [0, 16]], A.is_ge, 0, 1, 0.0)
    pool("sel", O, R("mO1"), [[16, 8], [0, 16]], A.is_ge, 15, -1, 0.0)
    pool("sel", I, R("ones", 0, 128), [[-1, 128]], A.is_equal, 0, 1, 0.0)
    for i in range(2):
        pool("sel", R("z24", 144 * i, 144 * i + 143), R("ones", 0, 143, p1=24), [[-1, 143]], A.is_equal, 15 - 256 * i, 16, 0.0)
    pool("sel", R("z24", 288, 416), R("ones", 0, 128, p1=24), [[-1, 8], [0, 16]], A.is_equal, -8, 1, 0.0)
    pool("iota", R("kc"), None, [[1, 16], [0, HB]], 0, 0)
    pool("iota", R("iw"), None, [[-16, NH], [-8193, 16]], 8192 * 128 + 255, 8192)
    pool("iota", R("snb", V, WIN), None, [[0, WIN - V]], 0, 0)
    pool("iota", R("t01", 0, 2), None, [[-1, 2]], 1, 0)
    pool("sel", R("mT1"), O, [[1, 128]], A.is_gt, 0, -1, 0.0)
    pool("sel", R("mT"), R("mT1"), [[1, 128]], A.not_equal, 0, -1, -1.0)
    mset(R("mZ"), 0.0)
    copy(R("mZ", 15, 143, 16), R("mO", 0, 128, 16))
    mset(R("fw", V, XB), 1024.0)
    mset(R("c1281"), -1281.0)
    ts(R("ei"), R("io1"), 15, A.bitwise_and)
    ts(R("oi"), R("io1"), 1, A.bitwise_and)
    ts(R("rm"), R("ei"), 0.0, A.is_equal)
    ts(R("rm4"), R("ei"), 0.0, A.is_equal, 4096.0, A.mult)
    for u in range(16):
        act(Bm("mB", u), O, F.Identity, 0.0, col("rm4", u))
    act(R("bq", 0, RO), R("ei", 0, RO), F.Identity, 20488.5)
    act(R("bp", 0, RO), R("ei", 0, RO), F.Identity, -4096.0, P23)
    ts(col("cu", 0), col("ei", 0), 15.0, A.not_equal, 2048.0, A.mult)
    act(col("cu", 1), col("cu", 0), F.Identity, CEN, -1.0)
    mset(R("cs"), P23)
    mset(R("cs", 15, L, 16), 0.0)
    ts(R("iw2"), R("iw"), 15 * 8192 + 255, A.bitwise_and)
    act(R("tb"), R("iw2"), F.Identity, 256.0, -1.0)
    nw = LB * max(len(b) for b in RUNS)
    ts(R("iw3", 0, nw), R("iw2", 0, nw), 13, A.logical_shift_right)
    ts(R("e0", 0, nw), R("iw3", 0, nw), 0.0, A.is_equal, 4096.0, A.mult)
    ts(R("e15", 0, nw), R("iw3", 0, nw), 15.0, A.is_equal, -2048.0, A.mult)
    tt(R("ds", 0, nw), R("e0", 0, nw), R("e15", 0, nw), A.add)
    XC = [XB - 1 - CEN + L * t for t in range(RO)]
    for t in range(RO):
        act(R("cx", NW * t, NW * t + nw), R("e0", 0, nw), F.Identity, 4096.0, -(XC[t] + 4096.0) / 4096)
    act(R("co", 0, nw), R("e0", 0, nw), F.Identity, 12288.0, (4096.0 - S - 12288.0) / 4096)
    if HOLE != "V":
        act(R("mI32"), I)
        act(R("mP"), I, F.Identity, 0.0, -2 * P23)
    act(NI, I, F.Identity, 0.0, -1.0)
    for n, c in (("c128", 128.0), ("c2048", 2048.0), ("cK", 255 * P23), ("c2047", CEN)):
        mset(R(n), c)
    act(BIG, I, F.Identity, 0.0, -BIGV)
    act(PB, I, F.Identity, 0.0, BIGV)
    mset(R("mZ2"), 0.0)
    mset(R("mY"), 0.0)
    mset(R("sc"), 1.0)
    for h in range(2):
        copy(half("mZ2", h, 79 - 64 * h, 143 - 64 * h, 16), own("mO", h, 16))
        copy(half("mY", h, 78 + h, 142 + h, 16), own("mO", h, 16))
        tt(half("sc", h, 8 * h, 8 * h + 8), half("rm", h, 0, 16, 2), half("rm", h, 1, 16, 2), A.add)
    ts(col("par", 0), col("oi", 0), 0.0, A.is_equal)
    copy(col("par", 1), col("oi", 0))
    for h in range(2):
        for kk in range(2):
            act(half("mD0", h, 128 * h + 64 * kk, 128 * h + 64 * kk + 64), own("mO", h), F.Identity, 0.0, half("par", h, kk, kk + 1))
            act(half("mD0", 1 - h, 128 * h + 64 * kk, 128 * h + 64 * kk + 64), own("mN", 1 - h), F.Identity)
        for kp in range(8):
            act(Bm("mD", 8 * h + kp), R("mD0", 128 * h, 128 * h + 128), F.Identity, 0.0, col("sc", 8 * h + kp))
    if "AAA" in E3:
        act(R("mYP"), R("mY"), F.Identity, 0.0, BIGV)
    if "VVV" in E3:
        act(R("mY8"), R("mY"), F.Identity, 0.0, 8192.0)
    act(R("mYN"), R("mY"), F.Identity, 0.0, -BIGV)
    for h in range(2):
        act(half("mR", h, 0, 64), own("mBIG", h), F.Identity)
    for h in range(2):
        act(R("mJ", 64 * h, 64 * h + 64), R("mR", 0, 64), F.Identity, 0.0, 8192.0 / BIGV)
    mset(R("hm", 0, 2), 0.0)
    for h in range(2):
        mset(half("hm", h, h, h + 1), 1.0)
    for h in range(2):
        act(Bm("mH", h), I, F.Identity, 0.0, col("hm", h))
        act(Bm("mH", 2 + h), BIG, F.Identity, 0.0, col("hm", h))
        act(Bm("mH", 4 + h), R("mJ"), F.Identity, 0.0, col("hm", h))
    for kp in range(8):
        keep(R("mR", 128 * kp + 64, 128 * kp + 128), R("mYN", 78 - 2 * kp, 142 - 2 * kp))
        keep(R("mR", 128 * kp + 128, 128 * kp + 192), R("mR", 0, 64))

    act(R("rw"), R("rwi"), F.Identity, -CEN)
    p = tile()
    mm(grp([(R(p, 0, NH), R("z24", 15 - u, 143 - u), R("rw", u, L, 16)) for u in range(16)]))
    act(w("s0"), R(p, 0, NH), F.Identity, col("cu", 1))
    p = tile()
    mm(grp([(R(p, 0, NH), R("z24", 159 - u, 287 - u), R("rw", u, L, 16)) for u in range(16)]))
    act(w("thr"), R(p, 0, NH), F.Identity, 16 * CEN, 16.0)
    act(w("thx"), R(p, 0, NH), F.Identity, 16 * CEN + 512 * 1536.0, 16.0)
    p = tile()
    mm(grp([(R(p, 0, L), R("z24", 288, 416), R("rw"))]))
    act(R("v0"), R(p, 0, L))
    copy(R("sn16"), R("sni", 0, 256))
    for i in range(0, 16, 2):
        p = tile()
        mm([(R(p, 256 * j, 256 * j + 256), Bm("mB", i + j), R("sn16"), True, True) for j in range(2)])
        act(R("snb", 256 * i, 256 * i + 512), R(p), F.Identity, 0.0, 1.0 / 4096)
    for t in (1, 2):
        send([(ln("v0", b), ln("v%d" % t, b), t * (1 + b)) for b in range(3)], "av%d" % t)
    for a, b in LM:
        ts(R("memi", a, b), R("lmi", a, b), V - 1, A.bitwise_and)
        act(R("mem0", a, b), R("memi", a, b), F.Identity, -CEN)
    for b in ORDER:
        for h in range(2):
            move(EC["pm0"], st2("pm0", b, h), R("pqi", L * h + LB * b, L * h + LB * b + LB), -CEN)
        move("G", st2("um0", b), st2("pm0", b))
    for a, b in LM:
        keep(R("comb", a, b), R("lmi", a, b))
        keep(R("mem1", a, b), R("mem0", a, b))

    KS = [(0, 6), (6, 11), (11, 16)]

    def links(out, tab, off):
        gat("gts", out, tab, off, -2047.5, 1.0 / 4096, A.add, A.mult)
        add("A", "agact", (out, tab, off, F.Identity, -2047.5 / 4096, 1.0 / 4096), [], [], 65 + GAT * CYC * cnt(out))
        other()

    def pairs(b, u, dst, engs):
        for (j0, j1), eng in zip(KS, engs):
            bk = tile()
            mm([(R(bk, (j - j0) * LB, (j - j0 + 1) * LB), Bm("mD", j), st2(u, b, j // 8), True, True) for j in range(j0, j1)])
            o, i_ = R(dst, LB * (16 * b + j0), LB * (16 * b + j1)), R(bk, 0, (j1 - j0) * LB)
            if eng == "A":
                act(o, i_, F.Sigmoid, SIGB, SIGC)
                ts(o, i_, 0.0, A.is_equal, 1.0 / 32, A.mult)
                other()
            else:
                ts(o, i_, 0.0, A.is_equal)

    def visit(t, before):
        PAR[0] = t
        last = t == RO - 1
        X = lambda a, b: R("fw", XB + L * t + a, XB + L * t + b)
        pm, um, sw, vw, snew = "pm%d" % t, "um%d" % t, "s%d" % t, "v%d" % t, "sn%d" % (t + 1)
        tab = R("lmi") if t == 0 else R("comb", 0, S)
        mem = R("mem%d" % t, 0, S)

        def front(a, b):
            n = b - a
            p = R(tile(), 0, n)
            mm(grp([(p, O, X(a, b))]))
            act(R("q16", a, b), p, F.Identity, col("bq", t), -1.0)
            p = R(tile(), 0, n)
            mm(grp([(p, O, R("c1281", 0, n)), (p, O, X(a, b)), (p, I, R("q16", a, b))]))
            act(R("pen", a, b), p, F.Identity, col("bp", t), -P23)
            for k in range(16):
                ts(R("mask", 16 * a + k, 16 * b, 16), R("pen", a, b), k * P23 if k else -4096.0, A.is_equal)
                if k % 4 == 3:
                    join(4)
            act(R("q2", a, b), R("pen", a, b), F.Identity, -127.8 * 2 * P23, -1.0)

        def link(b):
            offs(wu("su", b), w(sw, b), col("cu", 0))
            links(ln("au", b), tab, wu("su", b))

        def pick(b, buf, off):
            for a in range(LB * b, LB * b + LB, PIECE):
                c = min(a + PIECE, LB * b + LB)
                gat("gtt", R(buf, 16 * a, 16 * c), mem, R(off, a, c), R("mask", 16 * a, 16 * c), A.mult)

        def sample(b, engs):
            a = LB * b
            sg = lambda k: R("sg", 16 * a + k * LB, 16 * a + (k + 1) * LB)
            p = R(tile(), 0, LB)
            mm(grp([(p, I, ln("pen", b)), (p, I, ln("q2", b)), (p, I, R("cK"))] + [(p, Bm("mH", h), st2(pm, b, h)) for h in range(2)]))
            ts(ln("pu", b), p, -2048.0, A.max)
            p = tile()
            mm(grp([(R(p, 0, LB), Zr(k), R("g", 16 * a + k, 16 * (a + LB), 16)) for k in range(16)]))
            for h in range(2):
                move(EC["um"], half(um, h, LB * (2 * b + h), LB * (2 * b + h + 1)), half(p, h, 0, LB))
            pairs(b, um, "sg", engs)
            Mp = R(tile(), 0, LB)
            rest = [(Mp, BIG, R("c2048")), (Mp, BIG, ln("pu", b))] + [(Mp, Bm("mH", h), st2(um, b, h)) for h in range(2)]
            Y = lambda m, j: R(m, 78 - 64 * (j // 8) - 2 * (j % 8), 206 - 64 * (j // 8) - 2 * (j % 8))
            if "A" in engs:
                Sp = R(tile(), 0, LB)
                mm(grp([(Sp, PB, R("c128", 0, LB))] + [(Sp, Y("mYP", j), sg(j)) for j in range(16)]))
                act(st2("rr", b, 0), Sp, F.Identity, 0.0, 1.0 / BIGV / 32)
                act(st2("rr", b, 1), Sp, F.Identity, UP / 32, 1.0 / BIGV / 32)
                mm(grp(rest + [(Mp, BIG, st2("rr", b, 0)), (Mp, PB, st2("rr", b, 1))]))
            else:
                mm(grp(rest + [(Mp, Y("mY8", j), sg(j)) for j in range(16)]))
                ts(Mp, Mp, 8192.0, A.min)
            tt(ln("nn", b), Mp, ln("pu", b), A.max)
            for h in range(2):
                move("G", st2("n16", b, h), ln("nn", b))
            ts(ln("nu", b), ln("nn", b), V - CEN, A.min, CEN, A.add)
            act(ln("vf", b), Mp, F.Relu, -4096.0)

        def dist(b, engs):
            a = LB * b
            n = LB // len(engs)
            for i, e in enumerate(engs):
                a1 = a + i * n
                agat(R("f", 16 * a1, 16 * (a1 + n)), R("fw", 0, XB), R("nu", a1, a1 + n))
            for k0, k1 in KS:
                bk = tile()
                lst = []
                for k in range(k0, k1):
                    o = R(bk, (k - k0) * LB, (k - k0 + 1) * LB)
                    lst += grp([(o, NI, X(a, a + LB)), (o, I, R("f", 16 * a + k, 16 * (a + LB), 16))])
                mm(lst)
                act(R("ab", 16 * a + k0 * LB, 16 * a + k1 * LB), R(bk, 0, (k1 - k0) * LB), F.Abs, 0.0, 16.0)

        def least(b):
            a = LB * b
            p = tile()
            mm(grp([(R(p, 0, LB), I, R("kc"))] + [(R(p, 0, LB), Zr(u), R("ab", 16 * a + u, 16 * (a + LB), 16)) for u in range(16)]))
            for h in range(HB):
                o, i_ = col("kmin", HB * b + h), R(p, h, LB, HB)
                add("V", "red", (o, i_), [i_], [o], vc(16))
            join(HB)

        def mid(b):
            a, n = LB * b[0], LB * len(b)
            ts(w("ki2", b), w("kmin", b), 15, A.bitwise_and)
            offs(wu("ku", b), w("ki2", b))
            tt(w("c1", b), w("kmin", b), w("thr", b), A.is_lt)
            gat("gtt", ln("seln", b), R("rm"), wu("ku", b), ln("nn", b), A.mult)
            p = R(tile(), 0, n)
            mm(grp([(p, I, R("cx", NW * t, NW * t + n)), (p, O, ln("seln", b))]))
            scan(ln("xo", b), ln("tb", b), p, -8192.0, A.max, A.min)
            offs(wu("xu", b), end("xo", b), XC[t] + CEN)
            agat(ln("s2b", b), R("snb"), wu("xu", b))
            scan(ln("s2x", b), R("ds", 0, n), ln("s2b", b), 0.0, A.add, A.min)
            offs(wu("s2u", b), end("s2x", b), col("cu", 0))
            act(w("s2w", b), end("s2x", b), F.Identity, col("cu", 0))
            agat(ln("fs", b), R("fw", 0, XB + L * (t + 1)), wu("xu", b))
            p = R(tile(), 0, n)
            mm(grp([(p, I, X(a, a + n)), (p, I, ln("fs", b))]))
            act(ln("xy", b), p, F.Identity, 1535.75, 0.5)
            act(ln("xf", b) if last else R("xn", L * t + a, L * t + a + n), ln("xy", b), F.Identity, -1536.0)
            if not last:
                at = XB + L * (t + 1)
                send([(R("xn", L * t + LB * c, L * t + LB * c + LB), R("fw", at + LB * c, at + LB * c + LB), 1 + c) for c in b], "ax%d_%d" % (t + 1, b[0]))
            for o, tb in (("oc", tab), ("om", mem))[:1 if last else 2]:
                if HOLE == "V":
                    gat("gtt", ln(o, b), tb, wu("s2u", b), ln("pen", b), A.min)
                else:
                    agat(ln(o + "r", b), tb, wu("s2u", b))
                    p = R(tile(), 0, n)
                    mm(grp([(p, R("mI32"), ln(o + "r", b)), (p, R("mP"), R("mask", 16 * a, 16 * (a + n), 16))]))
                    act(ln(o, b), p)
            if HOLE == "V":
                links(ln("a2u", b), tab, wu("s2u", b))
            else:
                offs(ln("a2u", b), ln("ocr", b), -2047.5 / 4096, 1.0 / 4096)

        def late(b):
            a, n, nh = LB * b[0], LB * len(b), HB * len(b)
            tt(w("df", b), end("s2x", b), w(sw, b), A.subtract)
            tt(w("d2", b), w("df", b), w("c1", b), A.mult)
            ts(w("go", b), w("d2", b), 0.0, A.not_equal, 4096.0, A.mult)
            tt(w(snew, b), w("d2", b), w(sw, b), A.add)
            if not last:
                send([(w(snew, c), w("s%d" % (t + 1), c), 1 + c) for c in b], "as%d_%d" % (t + 1, b[0]))
            offs(wu("gu", b), w("go", b), 0.0, 1.0 / 4096)
            agat(ln("nogo", b), R("t01", 0, 2), wu("gu", b))
            eq = lambda h, lo, hi: R("eq", NW * (HB * b[0] + h) + lo, NW * (HB * b[0] + h) + hi)
            for h in range(nh):
                ts(eq(h, 16 * h, n), R("s2b", a + 16 * h, a + n), col("s2w", HB * b[0] + h), A.is_equal, col("go", HB * b[0] + h), A.mult)
                if h % HB == HB - 1:
                    join(HB)
            p = tile()
            mm(grp([(R(p, 0, n), I, R("co", 0, n)), (R(p, 0, n), I, ln("s2b", b))], last=False))
            mm(grp([(R(p, 16 * h + 16, n), O, eq(h, 16 * h + 16, n)) for h in range(nh - 1)]
                   + [(R(p, 16 * h, 16 * h + 16), R("mT"), eq(h, 16 * h, 16 * h + 16)) for h in range(nh)], first=False))
            scan(ln("ox", b), ln("tb", b), R(p, 0, n), -8192.0, A.max, A.min)
            offs(wu("ou", b), end("ox", b), float(S))
            p = tile()
            mm(grp([(R(p, 0, 2 * n), NI, st2(pm, b))] + [(R(p, LB * (2 * (c - b[0]) + h), LB * (2 * (c - b[0]) + h + 1)), Bm("mH", 4 + h), ln("nogo", c))
                                                         for c in b for h in range(2)]))
            if last:
                act(st2("pk1", b), R(p, 0, 2 * n), F.Relu, 2048.0 - 8192.0, -1.0)
                act(st2("pk", b), st2("pk1", b), F.Identity, -1.0)
                p = tile()
                mm(grp([(R(p, 0, n), I, ln("cs", b))] + [(R(p, u, n, 16), Bm("mB", u), w(snew, b)) for u in range(16)]))
                act(ln("sf", b), R(p, 0, n), F.Identity, 0.0, 1.0 / 4096)
            else:
                act(st2("pk", b), R(p, 0, 2 * n), F.Identity, -8192.0, -1.0)

        def count():
            act(R("junk"), R("nogo"), F.Identity, 16.0, -16.0, col("cnt", 0))
            act(col("a1", 0), col("cnt", 0), F.Identity, 1536.0 - 15.5 / 32, 1.0 / 512)
            act(col("a4", 0), col("a1", 0), F.Identity, col("cnt", 0), -512.0)
            act(w("thr"), w("thx"), F.Identity, col("a4", 0))

        def values():
            if not last:
                Vp = R(tile(), 0, L)
                mm(grp([(Vp, NI, R("pen")), (Vp, I, R(vw))]))
                act(R("bm"), Vp, F.Identity, -4096.0)
            p = tile()
            Vp = R(p, 0, L)
            mm(grp([(Vp, I, R("cs"))] + [(R(p, u, L, 16), Bm("mB", u), w(sw)) for u in range(16)] + [(Vp, NI, R("pen")), (Vp, I, R(vw))]))
            act(R("bc"), Vp, F.Identity, CEN - 4096.0)

        def write(b, tb, o, bb):
            add("V", "sct", (R(tb), wu("ou", b), ln(o, b), ln(bb, b), A.max), [wu("ou", b), ln(o, b), ln(bb, b)], [R(tb)], 50 + SCT * CYC * LB * len(b))

        def recode(b, engs):
            a = LB * b
            sh = lambda k: R("sh", 16 * a + k * LB, 16 * a + (k + 1) * LB)
            x = tile()
            mm(grp([(R(x, 0, LB), Zr(k, "mZ2"), R("h", 16 * a + k, 16 * (a + LB), 16)) for k in range(16)]))
            for h in range(2):
                move(EC["n2"], half("n16", 1 - h, LB * (2 * b + h), LB * (2 * b + h + 1)), half(x, 1 - h, 0, LB))
            pairs(b, "n16", "sh", engs)
            p = tile()
            PM = R(p, 0, 2 * LB)
            Ph = lambda h: R(p, LB * h, LB * h + LB)
            z = tile() if "A" in engs else p
            sums = [(R(z, 0, LB), R("mR", 128 * k + 64, 128 * k + 192), sh(k)) for k in range(8)] \
                + [(R(z, LB, 2 * LB), R("mR", 128 * k, 128 * k + 128), sh(8 + k)) for k in range(8)]
            rest = [(PM, I, st2("n16", b))] + ([(PM, I, R("c2047"))] if last else []) \
                + [(Ph(h), Bm("mH", 2 + h), ln("vf", b)) for h in range(2)] + [(Ph(h), Bm("mH", 4 + h), ln("nogo", b)) for h in range(2)]
            if "A" in engs:
                mm(grp([(R(z, 0, 2 * LB), BIG, R("c128"))] + sums))
                act(st2("r2", b), R(z, 0, 2 * LB), F.Identity, 0.0, -1.0 / BIGV)
                act(st2("r3", b), R(z, 0, 2 * LB), F.Identity, UP, -1.0 / BIGV)
                mm(grp([(PM, PB, st2("r2", b)), (PM, BIG, st2("r3", b))] + rest))
            else:
                mm(grp(rest + sums))
            if last:
                for h in range(2):
                    tt(R("pf", L * h + a, L * h + a + LB), Ph(h), st2("pk", b, h), A.max)
            else:
                tt(st2("po%d" % t, b), PM, st2("pk", b), A.max)
                send([(st2("po%d" % t, b), st2("%s%d" % (to, t + 1), b), 1 + b) for to in ("um", "pm")], "ap%d_%d" % (t + 1, b))

        def store(a, b):
            for h in range(2):
                dma("S", ("yp", a, b, 64 * h), half("pf", h, L * h + a, L * h + b), 512 * (b - a))
                dma("S" if a else "A", ("yq", a, b, 64 * h), half("pf", 1 - h, L * h + a, L * h + b), 1024 * (b - a))

        def stage(tag, fn, *args):
            TAG[0], PAR[0] = tag, t
            fn(*args)

        def finish(c, after=None):
            at = len(ops)
            stage("q%d" % c, pick, ORDER[c], "h", "a2u")
            for o in ops[at:]:
                o["after"] = after
            stage("r%d" % c, recode, ORDER[c], E7[c])
            if last and c:
                store(LB * ORDER[c], L if c == 1 else LB)

        for i, (a, b) in enumerate(MS):
            stage("f%d" % i, front, a, b)
        stage("val", values)
        for c, b in enumerate(ORDER):
            stage("k%d" % c, link, b)
            stage("p%d" % c, pick, b, "g", "au")
            gate = ops[-1]
            for d in DEFER:
                if before and DEFER[d] == c:
                    before(d, gate)
            stage("s%d" % c, sample, b, E3[c])
            stage("d%d" % c, dist, b, E4[c])
            stage("e%d" % c, least, b)
            for bs in RUNS:
                if bs[0] == b:
                    stage("m%d" % c, mid, bs)
                    stage("l%d" % c, late, bs)
                    if not last:
                        stage("w%d" % c, write, bs, "mem%d" % (t + 1), "om", "bm")
        for bs in RUNS:
            stage("w%d" % ORDER.index(bs[0]), write, bs, "comb", "oc", "bc")
        TAG[0] = "tail"
        if t == 0:
            for a, b in LM:
                keep(R("mem2", a, b), R("mem1", a, b))
        if not last:
            count()
        else:
            dma("S", ("yx",), R("xf"), 122880)
            dma("S", ("ys",), R("sf", pstep=16), 8000)
            dma("S", ("ylm", 0, 768), R("comb", 0, 768), 400000)
            dma("S", ("ylm", 768, S), R("comb", 768, S), 800000)
        for c in range(len(ORDER)):
            if last or c not in DEFER:
                finish(c)
        return finish

    left = None
    for t in range(RO):
        left = visit(t, left)
    for o in ops:
        if o["tag"] != "init" and o["cost"] < SHORT and o["eng"] == "A":
            o["alt"] = []
    return ops


def clash(x, y):
    if x[2] <= y[1] or y[2] <= x[1]:
        return False
    if x[3] == y[3] and x[3] > 1 and (x[1] - y[1]) % x[3]:
        return False
    if x[5] <= y[4] or y[5] <= x[4]:
        return False
    return not (x[6] == y[6] and x[6] > 1 and (x[4] - y[4]) % x[6])


def depend(ops):
    hist = {}
    for o in ops:
        wr = o["w"][0] if o["w"] else ("", 0, 0, 0, 0)
        name = "ps" if wr[0][:2] == "ps" else wr[0].split("~")[0].rstrip("0123")
        o["nth"] = (o["kind"], name, wr[1] % L if name == "xn" else wr[1], wr[4], int(o["cost"]))
        who = o["id"] if o["alt"] else o["eng"]
        dep = set()
        if o["after"] is not None:
            dep.add(o["after"]["id"])
        for isw, lst in ((False, o["r"]), (True, o["w"])):
            for x in set(lst):
                psum = x[0][:2] == "ps"
                for (y, yw, oid, eng) in hist.get(x[0], ()):
                    if oid != o["id"] and oid not in dep and ((psum and eng != who) or ((isw or yw) and clash(x, y))):
                        dep.add(oid)
        o["dep0"] = dep
        o["new"] = [n for n in set(x[0] for x in o["w"]) if n[:2] == "ps" and n not in hist]
        for isw, lst in ((False, o["r"]), (True, o["w"])):
            for x in set(lst):
                hist.setdefault(x[0], []).append((x, isw, o["id"], who))
    for o in ops:
        o["all"] = set(o["dep0"])
        for d in o["dep0"]:
            o["all"] |= ops[d]["all"]
        implied = set()
        for d in o["dep0"]:
            implied |= ops[d]["all"]
        o["dep0"] = o["dep0"] - implied
        if o["kind"] == "land":
            o["all"] = set()
    return {n: set(e[2] for e in h) for n, h in hist.items() if n[:2] == "ps"}


def improve(ops, users, rounds, seed):
    rnd = np.random.RandomState(seed)
    n = len(ops)
    forms = [[(ENG.index(f["eng"]), f["cost"]) for f in [o] + o["alt"]] for o in ops]
    slow = [SLOW.get(o["kind"], SLOW[""]) for o in ops]
    lat = [o["lat"] for o in ops]
    dep0 = [sorted(o["dep0"]) for o in ops]
    succ = [[] for _ in ops]
    for i in range(n):
        for d in dep0[i]:
            succ[d].append(i)
    names = sorted(users)
    tiles = [sorted(set(names.index(x[0]) for x in o["r"] + o["w"] if x[0][:2] == "ps")) for o in ops]
    new = [names.index(o["new"][0]) if o["new"] else -1 for o in ops]
    use = [sorted(users[x]) for x in names]
    tensor = [o["id"] for o in ops if o["eng"] == "P"]
    loads = [o["id"] for o in ops if o["eng"] == "S" and o["tag"] == "init"]

    def place(prio, eng, cost, post, back):
        rank = [-p for p in prio]
        for i in (range(n - 1, -1, -1) if back else range(n)):
            r = rank[i] + 0.001
            for s in post[i]:
                if rank[s] < r:
                    rank[s] = r
        rt, t0 = [0.0] * n, [0.0] * n
        los, his = [[] for _ in ENG], [[] for _ in ENG]
        for o in np.argsort(rank, kind="stable").tolist():
            c, lo, hi = cost[o], los[eng[o]], his[eng[o]]
            st = rt[o] + (lat[o] if back else 0.0)
            if c:
                i = m = len(lo)
                while i and hi[i - 1] > st:
                    i -= 1
                while i < m and lo[i] < st + c:
                    st = hi[i]
                    i += 1
                en = st + c
                if i and st - hi[i - 1] < 50.0:
                    if i < m and lo[i] - en < 50.0:
                        hi[i - 1] = hi[i]
                        del lo[i], hi[i]
                    else:
                        hi[i - 1] = en
                elif i < m and lo[i] - en < 50.0:
                    lo[i] = st
                else:
                    lo.insert(i, st)
                    hi.insert(i, en)
            t0[o] = st
            en = st + c + HOP + (0.0 if back else lat[o])
            for s in post[o]:
                if rt[s] < en:
                    rt[s] = en
        return t0

    def schedule(prio, side, bar=1e18):
        eng = [forms[i][side[i]][0] for i in range(n)]
        cost = [forms[i][side[i]][1] for i in range(n)]
        key = place(prio, eng, cost, succ, False)
        nxt = 1e18
        for i in sorted(tensor, key=lambda i: -key[i]):
            if new[i] >= 0:
                key[i] = max(key[i], min([nxt] + [key[s] - HOP for s in succ[i]]) - cost[i])
            nxt = key[i]
        todo, order, held = np.argsort(key, kind="stable").tolist()[::-1], [], []
        free, fr2, fin, fi2, t0s, before, on = [0.0] * 6, [0.0] * 6, [0.0] * n, [0.0] * n, [0.0] * n, [-1] * n, [-1] * 6
        alive, ends, end2 = [len(u) for u in use], [0.0] * len(names), [0.0] * len(names)
        open_, tenant, bank, extra, rts = list(range(8)), [-1] * 8, [0] * len(names), {}, [0.0] * n
        while todo:
            x = todo.pop()
            if (new[x] >= 0 and not open_) or (held and not all([fin[d] for d in dep0[x]])):
                held.append(x)
                continue
            order.append(x)
            e = eng[x]
            st = s2 = 0.0
            for d in dep0[x]:
                if fin[d] > st:
                    st = fin[d]
                if fi2[d] > s2:
                    s2 = fi2[d]
            if new[x] >= 0:
                b = open_.pop(0)
                y = tenant[b]
                if y >= 0:
                    extra[x] = y
                    if ends[y] > st:
                        st = ends[y]
                    if end2[y] > s2:
                        s2 = end2[y]
                tenant[b] = new[x]
                bank[new[x]] = b
            rts[x] = st
            if free[e] > st:
                st = free[e]
            if fr2[e] > s2:
                s2 = fr2[e]
            t0s[x] = st
            before[x], on[e] = on[e], x
            free[e] = st = st + cost[x]
            fr2[e] = s2 = s2 + slow[x] * cost[x]
            fin[x] = st = st + lat[x] + HOP
            fi2[x] = s2 = s2 + lat[x] + 80.0
            for y in tiles[x]:
                if ends[y] < st:
                    ends[y] = st
                if end2[y] < s2:
                    end2[y] = s2
                alive[y] -= 1
                if not alive[y]:
                    open_.append(bank[y])
                    todo += reversed(held)
                    held = []
        val = (max(fin) + MIX * max(fi2)) / (1.0 + MIX)
        if held or val > bar:
            return None
        o, pairs, path = fin.index(max(fin)), [], []
        while o >= 0:
            path.append(o)
            c = [d for d in dep0[o] + (use[extra[o]] if o in extra else []) if abs(fin[d] - t0s[o]) < 1]
            if not c and before[o] >= 0 and rts[o] < t0s[o] - 1 and eng[o] < 4:
                pairs.append((o, before[o]))
            o = c[0] if c else before[o]
        return val, pairs, path, order, t0s, [f - HOP for f in fin], bank, extra, eng, cost, max(fi2)

    def latest(res):
        t0 = place(res[5], res[8], res[9], dep0, True)
        prio = [t0[i] + res[9][i] for i in range(n)]
        for i in loads:
            prio[i] = 1e7 - i
        return prio

    same, stages = {}, {}
    for o in ops:
        same.setdefault((o["tag"], o["nth"]), []).append(o["id"])
        stages.setdefault(o["tag"], []).append(o["id"])
        stages.setdefault(o["tag"] + "/%d" % o["vis"], []).append(o["id"])
    twins = {i: lst for lst in same.values() for i in lst}
    tags = sorted(stages)
    flex = [i for i in range(n) if len(forms[i]) > 1]
    prio, side = [0.0] * n, [0] * n
    for i in reversed(range(n)):
        prio[i] = forms[i][0][1] + lat[i] + max([prio[s] + HOP for s in succ[i]] + [0.0])
    for o in ops:
        t = o["tag"]
        prio[o["id"]] += STAGGER * int(t[1]) if t[1].isdigit() and t[0] not in "qr" else 0.0
        if t == "init" and o["alt"] and o["eng"] == "A" and o["alt"][0]["cost"] < 0.6 * o["cost"]:
            side[o["id"]] = 1
    for i in loads:
        prio[i] = 1e7 - i
    now = schedule(prio, side)
    best = (now, side)
    for r in range(rounds):
        p2, s2, move = prio, side, rnd.rand()
        if move < 0.5 and now[1]:
            p2 = list(prio)
            for _ in range(int(rnd.randint(1, 4))):
                a, b = now[1][int(rnd.randint(len(now[1])))]
                d = abs(p2[b] - p2[a]) + (50.0, 500.0, 2000.0)[int(rnd.randint(3))]
                x, d = (a, d) if rnd.rand() < 0.5 else (b, -d)
                for y in (twins[x] if rnd.rand() < 0.5 else [x]):
                    p2[y] += d
        elif move < 0.72 and flex:
            s2 = list(side)
            on = [i for i in now[2] if len(forms[i]) > 1]
            for _ in range(int(rnd.randint(1, 3))):
                lst = on if on and rnd.rand() < 0.6 else flex
                x = lst[int(rnd.randint(len(lst)))]
                to = (s2[x] + 1 + int(rnd.randint(len(forms[x]) - 1))) % len(forms[x])
                for y in (twins[x] if rnd.rand() < 0.5 else [x]):
                    s2[y] = to % len(forms[y])
        elif move < 0.97:
            p2 = list(prio)
            d = (-1.0, 1.0)[int(rnd.randint(2))] * (300.0, 1000.0, 3000.0)[int(rnd.randint(3))]
            e = int(rnd.randint(4))
            for i in stages[tags[int(rnd.randint(len(tags)))]]:
                if e == 3 or now[8][i] == e:
                    p2[i] += d
        else:
            p2 = latest(now)
        got = schedule(p2, s2, now[0] + HEAT * (1.0 - r / rounds) * rnd.rand())
        if got is None:
            continue
        prio, side, now = p2, s2, got
        if got[0] < best[0][0]:
            best = (got, s2)
    res, side = best
    for o in ops:
        i = o["id"]
        if side[i]:
            o.update(o["alt"][side[i] - 1])
        o["t0"], o["t1"] = res[4][i], res[5][i]
        o["dep"] = set(dep0[i]) | set(use[res[7][i]] if i in res[7] else [])
    return [ops[i] for i in res[3]], {x: res[6][k] for k, x in enumerate(names)}, res[10]


PLAN = []


def rank_program(g, core, T, topo):
    rank = T.rank_of(core)
    if rank is None:
        return
    if not PLAN:
        ops = plan()
        PLAN.append((ops,) + improve(ops, depend(ops), ROUNDS, SEED))
    ops, order, banks, _ = PLAN[0]
    n = len(T.cores)
    Q = {"V": g.vector, "A": g.scalar, "P": g.tensor, "G": g, "S": g.sync}

    def ap(r):
        if not isinstance(r, tuple):
            return r
        if r[0] in banks:
            name, at = "bank%d" % banks[r[0]], 0
        elif r[0] in BUF:
            name, at = POOL[r[0]]
        elif len(r) == 4:
            return T[r[0]][r[3]:r[3] + 64, r[1]:r[2]]
        else:
            return T[r[0]][:] if len(r) == 1 else T[r[0]][:, r[1]:r[2]]
        last = r[1] + (cnt(r) - 1) * r[3] + 1
        return T[name][r[4]:r[5]:r[6], at + r[1]:at + last:r[3]]

    def ind(win, off):
        return ap(win).indirect(ap(off))

    def call(q, k, a):
        if k == "red":
            return q.tensor_reduce(ap(a[0]), ap(a[1]), AX.X, A.min)
        if a[5] is None:
            return q.tensor_scalar(ap(a[0]), ap(a[1]), ap(a[2]), ap(a[3]), a[4])
        return q.tensor_scalar(ap(a[0]), ap(a[1]), ap(a[2]), ap(a[3]), a[4], a[5])

    def engines(dst, parts):
        es = topo.engines(core, dst)
        k = 1
        while 2 * k * parts <= len(es):
            k *= 2
        return [sum(1 << e for e in es[i * k:(i + 1) * k]) for i in range(parts)], k

    total, shared = {}, {}
    for o in ops:
        if o["kind"] == "dma":
            shared[o["args"][2]] = shared.get(o["args"][2], 0) + 16
    known = {e: {} for e in Q}
    done = {}
    for o in order:
        e, k, a = o["eng"], o["kind"], o["args"]
        if k == "land":
            per = engines(T.cores[(rank + 1) % n], a[0])[1]
            total[a[1]] = per * a[0]
            done[o["id"]] = (a[1], per * a[0], {})
            continue
        q, kn = Q[e], known[e]
        need = {}
        for d in o["dep"]:
            s, v, _ = done[d]
            if kn.get(s, 0) < v:
                need[d] = (s, v)
        for d in sorted(need, key=lambda d: -ops[d]["t1"]):
            s, v, clock = done[d]
            if kn.get(s, 0) < v:
                v = max(vv for (ss, vv) in need.values() if ss == s)
                q.wait_ge(T.sem[s], v)
                kn[s] = v
            for s2, v2 in clock.items():
                if kn.get(s2, 0) < v2:
                    kn[s2] = v2
        sem, inc = "e" + e, 1
        if k == "many":
            for s in a[:-1]:
                call(q, s["kind"], s["args"]).then_inc(T.sem[sem], 1)
                total[sem] = total.get(sem, 0) + 1
            k, a = a[-1]["kind"], a[-1]["args"]
        if k in ("ts", "red"):
            i = call(q, k, a)
        elif k == "copy":
            i = q.tensor_copy(ap(a[0]), ap(a[1]))
        elif k == "tt":
            i = q.tensor_tensor(ap(a[0]), ap(a[1]), ap(a[2]), a[3])
        elif k == "scan":
            i = q.tensor_tensor_scan(ap(a[0]), ap(a[1]), ap(a[2]), a[3], a[4], a[5])
        elif k == "mset":
            i = q.memset(ap(a[0]), a[1])
        elif k == "gcp":
            i = q.tensor_copy(ap(a[0]), ind(a[1], a[2]))
        elif k == "gts":
            i = q.tensor_scalar(ap(a[0]), ind(a[1], a[2]), a[3], a[4], a[5], a[6])
        elif k == "gtt":
            i = q.tensor_tensor(ap(a[0]), ind(a[1], a[2]), ap(a[3]), a[4])
        elif k == "sct":
            i = q.tensor_tensor(ind(a[0], a[1]), ap(a[2]), ap(a[3]), a[4])
        elif k == "act":
            i = q.activation(ap(a[0]), ap(a[1]), a[2], bias=ap(a[3]), scale=ap(a[4]), accum_out=ap(a[5]))
        elif k == "agat":
            i = q.activation(ap(a[0]), ind(a[1], a[2]), F.Identity)
        elif k == "agact":
            i = q.activation(ap(a[0]), ind(a[1], a[2]), a[3], bias=a[4], scale=a[5])
        elif k == "mm":
            for m in a:
                i = q.matmul(ap(m[0]), ap(m[1]), ap(m[2]), m[3], m[4])
        elif k == "iota":
            if BUF[a[0][0]][2] == "int32":
                i = q.iota(ap(a[0]), a[2], a[3], a[4])
            else:
                i = q.iota(ap(a[0]), a[2], a[3], a[4], allow_small_or_imprecise_dtypes=True)
        elif k == "sel":
            i = q.affine_select(ap(a[0]), ap(a[1]), a[2], a[3], a[6], a[4], a[5])
        elif k == "dma":
            i = q.dma_start(ap(a[0]), ap(a[1]))
            sem, inc = a[2], 16
        elif k == "send":
            trs = []
            for j, (src, dst, ahead) in enumerate(a[0]):
                to = T.cores[(rank + ahead) % n]
                masks, per = engines(to, len(a[0]))
                rid, pid, _ = topo.addr(to)
                trs.append(RemoteDMATransfer(dst_ids=[DstId(rid=rid, pnc=pid)], dma_engine_mask=masks[j], remote_sem=T.sem[a[1]],
                                             src=ap(src), dst=ap(dst)))
                total["sent"] = total.get("sent", 0) + per
            q.remote_dma_fused(trs, local_sem=T.sem.sent)
            continue
        i.then_inc(T.sem[sem], inc)
        total[sem] = total.get(sem, 0) + inc
        done[o["id"]] = (sem, shared[sem] if k == "dma" else total[sem], dict(kn))
    for s, v in total.items():
        g.wait_ge(T.sem[s], v)
